import numpy as np, ml_dtypes
CORES = [8,136,40,168]
N = 4
BF = ml_dtypes.bfloat16
def gentries(a):
    return np.ascontiguousarray(a.reshape(8, 16, -1).transpose(0, 2, 1)).reshape(8, -1)
def gtable(e):
    e = np.asarray(e); return np.ascontiguousarray(e.reshape(8, -1, 16).transpose(0, 2, 1)).reshape(128, -1).astype(np.int32)
W, K, NM, SM, RO = 6144, 2048, 4095, 31, 7
def walks(rng):
    pace = rng.choice(np.array([0.02, 0.1, 0.4, 1.0]), (N, 8, 16, 1))
    x = rng.integers(-3, 4, (N, 8, 16, W)) * (rng.random((N, 8, 16, W), dtype=np.float32) < pace)
    x[..., 0] = rng.integers(-SM, SM + 1, (N, 8, 16))
    return np.abs((np.add.accumulate(x, axis=-1) + SM) % (4 * SM) - 2 * SM) - SM
def spans(rng):
    u = np.exp2(6 + rng.random((8, K)) * (np.log2(NM + 1) - 6)).astype(np.int64)
    return np.clip(np.where(rng.random((8, K)) < 0.5, u, rng.integers(64, NM + 1, (8, K))), 64, NM)
def starts(rng, n, power=1):
    return np.minimum((rng.random((N, 8, K)) ** power * (W - n)).astype(np.int64), W - 1 - n)
def pack(s, lo, n):
    return {"walk": np.ascontiguousarray(s.reshape(N, 128, W)).astype(np.float32).astype(BF), "lo": np.stack([gtable(a) for a in lo]), "span": np.stack([gtable(n)] * N)}
def setup_inputs(rng):
    s = walks(rng); n = spans(rng)
    return pack(s, starts(rng, n), n)
def setup_inputs_ends(rng):
    s = walks(rng); n = rng.choice(np.array([64, 65, 127, 128, NM - 1, NM]), (8, K)); lo = starts(rng, n)
    k = rng.integers(0, 3, (N, 8, K)); lo = np.where(k == 0, 0, np.where(k == 1, W - 1 - n, lo))
    s[:, 0] = SM; s[:, 0, :, 0] = -SM; s[:, 0, :, NM] = -SM; s[:, 0, ::2] = -s[:, 0, ::2]
    n[0, ::2] = NM; lo[:, 0, ::2] = 0; n[0, 1::2] = 64; lo[:, 0, 1::2] = np.minimum(lo[:, 0, 1::2], W - 65)
    s[:, 1] = SM * (2 * rng.integers(0, 2, (N, 16, W)) - 1)
    n[3] = NM; lo[:, 3] = rng.integers(0, W - NM, (N, 1))
    s[:, 2] = SM - rng.integers(0, 2, (N, 16, W))
    s[:, 2, :, :32] *= -1; s[:, 2, :, NM - 31:NM + 1] *= -1
    s[:, 2] *= 2 * rng.integers(0, 2, (N, 16, 1)) - 1
    n[2] = NM - rng.integers(0, 32, K); lo[:, 2] = np.minimum((rng.random((N, K)) * (NM - n[2] + 1)).astype(np.int64), NM - n[2])
    h = NM >> 2; q = int(rng.integers(0, N)); j = int(rng.integers(0, 16)); i = rng.integers(0, 16, N)
    s[:, 4] = SM
    s[q, 4, j] = SM - 1; s[q, 4, j, h - 15:h + 5] = SM - 2; s[q, 4, j, 3 * h - 45:3 * h + 6] = SM
    s[:, 4, :, :4] = -SM; s[:, 4, :, 4 * h - 60:NM + 1] = -SM
    for a in range(N): s[a, 4, int(i[a]), 4 * h - 60:NM + 1] = 1 - SM
    s[:, 4] *= 2 * rng.integers(0, 2, (N, 16, 1)) - 1
    n[4] = 4 * (h - rng.integers(0, 16, K)) + rng.choice(np.array([0, 1, 3]), K); n[4, :3] = 4 * h + np.array([1, 0, 3])
    lo[:, 4] = np.minimum(rng.integers(0, 4, (N, K)), NM - n[4])
    c = rng.integers(-SM, SM + 1, (N, 2, 16)); e = rng.integers(1, SM + 1, (N, 2, 16)); e = np.where(c > 0, c - e, c + e)
    last = rng.integers(NM, W, N); begin = rng.integers(0, W - NM, N); more = spans(rng)
    for a in range(N):
        s[a, 5] = c[a, 0][:, None]; s[a, 5, :, int(last[a])] = e[a, 0]
        s[a, 6] = c[a, 1][:, None]; s[a, 6, :, int(begin[a])] = e[a, 1]
    n[5] = np.where(rng.random(K) < 0.5, NM - rng.integers(0, 63, K), more[5]); n[5, 0] = NM - 30; lo[:, 5] = last[:, None] - n[5]
    n[6] = np.where(rng.random(K) < 0.5, 1024 + 2 * rng.integers(0, 100, K), more[6]); n[6, 0] = 1024; lo[:, 6] = begin[:, None]
    return pack(s, lo, n)
def setup_inputs_ties(rng):
    amp = rng.integers(1, SM + 1, (N, 8, 16, 1)) * (2 * rng.integers(0, 2, (N, 8, 16, 1)) - 1)
    pat = np.repeat(rng.integers(0, 2, (N, 8, 1, W // 64)), 64, axis=-1); n = spans(rng); lo = starts(rng, n)
    pat[:, 1::2] = pat[:1, 1::2].copy(); lo[:, 1::2] = lo[:1, 1::2].copy(); pat[:, 6] = 1
    return pack(amp * pat, lo, n)
def setup_inputs_short(rng):
    s = walks(rng); n = rng.integers(64, 97, (8, K)); lo = starts(rng, n)
    u = np.arange(W) % 64; saw = np.where(u == 0, -SM, SM - (u * SM >> 5)); v = (64 - u) % 64; was = np.where(v == 0, -SM, SM - (v * SM >> 5))
    sg = 2 * rng.integers(0, 2, (N, 16, 1)) - 1
    s[:, 0] = sg * saw; s[:, 4] = sg * was; s[:, 2, ::2] = saw; s[:, 6, 1::2] = was
    n[::2] = 64; lo[:, ::2] = 64 * rng.integers(0, W // 64 - 1, (N, 4, K))
    tail = np.maximum(-SM, SM - 64 + np.arange(66)); tail[0] = -SM; tail[65] = -SM
    s[:, 1, :, W - 66:] = sg * tail; n[1, ::4] = 65; lo[:, 1, ::4] = W - 66
    return pack(s, lo, n)
def setup_inputs_uneven(rng):
    s = walks(rng); n = spans(rng); lo = starts(rng, n); big = rng.integers(0, N, 8); big[0] = 0; big[1] = N - 1
    keep = np.arange(N)[:, None] == big[None, :]
    s = np.where(keep[:, :, None, None], s, np.sign(s))
    one = s[big[5], 5, 3].copy(); s[:, 5] = 0; s[big[5], 5, 3] = one
    k = rng.integers(0, 5, K); n[7] = n[7][k]; lo[:, 7] = lo[:, 7][:, k]
    return pack(s, lo, n)
def setup_inputs_spread(rng):
    z = np.exp2(-rng.integers(0, 6, (N, 8, 1, W)).astype(np.float64)) * (rng.random((N, 8, 1, W)) > 0.0625)
    s = np.rint(SM * z * (2 * rng.random((N, 8, 16, W)) - 1)).astype(np.int64); n = spans(rng)
    return pack(s, starts(rng, n, 4), n)
def check_inputs(d):
    bad = []; s = d["walk"].astype(np.float32); lo = d["lo"].astype(np.int64); n = d["span"].astype(np.int64)
    if not np.all((np.abs(s) <= SM) & (s == np.rint(s))): bad.append("whole numbers of walk")
    if np.min(n) < 64 or np.max(n) > NM: bad.append("range of span")
    if not np.all(n == n[:1]): bad.append("span alike on all ranks")
    if np.min(lo) < 0 or np.max(lo + n) > W - 1: bad.append("range of lo")
    return bad
def reference(walk, lo, span):
    s = walk.astype(np.float32).astype(np.int64).reshape(N, 8, 16, W)
    at = np.stack([gentries(a) for a in lo]).astype(np.int64)
    n = gentries(span[0]).astype(np.int64)
    def pick(q, t):
        return np.take_along_axis(s[q], (at[q] + t)[:, None, :], 2)
    first = [pick(q, 0 * n) for q in range(N)]; rise = [pick(q, n) - first[q] for q in range(N)]
    def gain(t):
        g = np.zeros((8, K), np.int64)
        for q in range(N):
            g = g + np.add.reduce(np.abs(n[:, None, :] * (pick(q, t) - first[q]) - t[:, None, :] * rise[q]), axis=1)
        return g
    l = np.zeros((8, K), np.int64); r = n.copy(); m = n >> 1; gm = gain(m)
    for rnd in range(RO):
        a = r - m; b = m - l; right = a > b
        w = np.where(right, m + (a >> 1), m - (b >> 1))
        gw = gain(w); up = gw > gm
        end = np.where(up, m, w); low = right == up
        l = np.where(low, end, l); r = np.where(low, r, end)
        m = np.where(up, w, m); gm = np.where(up, gw, gm)
    return {"ym": np.stack([gtable(m)] * N).astype(np.float32), "yg": np.stack([gtable(gm)] * N).astype(np.float32)}

@@ -1,0 +1,550 @@
+from concourse.bass import DstId, RemoteDMATransfer
+from concourse.mybir import AluOpType, ActivationFunctionType
+
+ALU = AluOpType
+ACT = ActivationFunctionType
+N, W, ROUNDS = 4, 6144, 7
+HALF = W // 2
+PIECE = HALF // 4
+MID = 2048.0
+F32, BF, F16, I32, U16 = "float32", "bfloat16", "float16", "int32", "uint16"
+
+SCRATCH = {name: ("sbuf", [128] + shape, kind) for names, shape, kind in (
+    ("tabA tabB", [W], BF), ("stage land", [6 * PIECE], BF), ("lost lold", [96], I32),
+    ("loA loB n32 J nTi", [128], I32), ("V XI tmpi", [384], I32), ("V16", [384], F16), ("Jt", [512], I32),
+    ("offA", [512], U16), ("offB", [256], U16), ("offw", [128], U16), ("nb16 w16 Rep", [128], F16),
+    ("n2i", [256], I32), ("n2f fl", [256], F32), ("lohi lolo Ibf Ineg", [128], BF), ("If", [128], F32),
+    ("Pi", [8], I32), ("Pf onesA onesB", [8], F32), ("M16", [16], F32), ("BD", [256], BF), ("Sel", [4096], BF),
+    ("nA mA wA nB Db", [2048], F32), ("riseB g0B geB gw", [2048], BF), ("gA", [8192], BF), ("Ab", [1024], F32),
+    ("ps0 ps1", [4, 32], F32), ("pl g2", [192], F32), ("Q0 Q1", [7, 32], F32), ("t3", [3, 32], F32),
+    ("gp hh", [3, 32], I32), ("c2", [8, 32], F32), ("sm", [160], F32), ("Z", [72], F32),
+    ("fs", [512], F32)) for name in names.split()}
+PSUM = ("pd0", "pd1", "pw0", "pw1", "pw2", "pw3", "pg", "px")
+SCRATCH.update({name: ("psum", [128, 512], F32) for name in PSUM})
+SEMAPHORES = (["cv", "ca", "cp", "cg", "sent", "hin", "lo_in", "part0", "part1", "fin0", "fin1", "relay", "lorel", "lost"]
+              + ["in%d" % i for i in range(6)] + ["d%d" % i for i in range(24)])
+CSEM = {"v": "cv", "a": "ca", "p": "cp", "g": "cg"}
+
+SEL_V = 2
+EVAC_A = "aavvavavaaaa"
+EVAC_B = "aaaa"
+PICK_A = "vavaaaaa"
+PICK_B = "aaav"
+RISE_B = "vvaa"
+RELAYOUT = (0, 2, 4, 1, 3, 5)
+OPENING = ("s00 s10 g01 s01 g02 g03 g11 g12 g00 g10 c a00 s11 a01 g13 u00 i n01 n00 u01 n10 p0 a10 a11 q0 n11 u10 u11 "
+           "l e00 p1 e01 e10 f e11 F r0 r1 z q1")
+ORDER = ("..b.Ea.d.vA.,.DVs..5S", "Be..,.,.,,Ea.dA,v..,D,Vs,.,,,,,,6.S1,")
+EARLY = "123456"
+
+
+def bits(engines):
+    m = 0
+    for e in engines:
+        m |= 1 << e
+    return m
+
+
+def helpers_of(core, topo):
+    return [c for c in topo.cores_of(core) if topo.die(c) != topo.die(core)]
+
+
+def emit(g, T, ops):
+    queue = {"v": g.vector, "a": g.scalar, "p": g.tensor, "g": g, "s": g.sync}
+    know = {q: {} for q in queue}
+    seq = {q: 0 for q in queue}
+    writer, readers, needed, plan = {}, {}, set(), []
+    for op in ops:
+        q = op["q"]
+        deps = list(op["after"])
+        for r in op["r"]:
+            if r in writer:
+                deps.append(writer[r])
+            if r in PSUM:
+                deps += [t for t in readers.get(r, []) if t[3] != q]
+        for r in op["w"]:
+            if r in writer:
+                deps.append(writer[r])
+            deps += readers.get(r, [])
+        best = {}
+        for t in deps:
+            if t[3] == "p" and q == "p":
+                continue
+            if t[1] > know[q].get(t[0], 0) and t[1] > best.get(t[0], (0, 0))[1]:
+                best[t[0]] = t
+        waits = []
+        for t in sorted(best.values(), key=lambda t: -len(t[2])):
+            if t[1] > know[q].get(t[0], 0):
+                waits.append((t[0], t[1]))
+                for k, v in list(t[2].items()) + [(t[0], t[1])]:
+                    know[q][k] = max(know[q].get(k, 0), v)
+                if t[0] in CSEM:
+                    needed.add((t[0], t[1]))
+        if op["dma"]:
+            tok = (op["dma"][0], op["dma"][1], dict(know[q]), "dma")
+        elif op["fn"] is None or op["remote"]:
+            tok = None
+        else:
+            seq[q] += 1
+            tok = (q, seq[q], dict(know[q]), q)
+        if tok:
+            for r in op["r"]:
+                readers.setdefault(r, []).append(tok)
+            for r in op["w"]:
+                writer[r] = tok
+                readers[r] = []
+        plan.append((op, waits, tok))
+    count = {}
+    for q in CSEM:
+        c = 0
+        for s in range(1, seq[q] + 1):
+            if (q, s) in needed:
+                c += 1
+                count[(q, s)] = c
+    for op, waits, tok in plan:
+        e = queue[op["q"]]
+        for k, v in waits:
+            if k in CSEM:
+                e.wait_ge(T.sem[CSEM[k]], count[(k, v)])
+            else:
+                e.wait_ge(T.sem[k], v)
+        if op["fn"] is None:
+            continue
+        ins = op["fn"](e)
+        if op["dma"]:
+            ins.then_inc(T.sem[op["dma"][0]], 16)
+        elif tok and (tok[0], tok[1]) in needed:
+            ins.then_inc(T.sem[CSEM[tok[0]]], 1)
+
+
+def hand_on(g, core, T, topo):
+    for src in T.cores:
+        hs = helpers_of(src, topo)[:N - 1]
+        if core in hs:
+            d = hs.index(core) + 1
+            dst = T.cores[(T.rank_of(src) + d) % N]
+            near = [e for e in topo.engines(src, core) if e not in topo.engines(src, dst)]
+            out = topo.engines(core, dst)
+            s = 2 * (d - 1) + 1
+            rid, pid = topo.addr(dst, core)
+            g.wait_ge(T.sem.hin, len(near))
+            g.remote_dma(T.land[:, s * PIECE:(s + 1) * PIECE], T.stage[:, s * PIECE:(s + 1) * PIECE],
+                         T.sem["in%d" % s], T.sem.sent, pid, rid, bits(out))
+            g.wait_ge(T.sem.sent, len(out))
+
+
+def rank_program(g, core, T, topo):
+    rank = T.rank_of(core)
+    if rank is None:
+        hand_on(g, core, T, topo)
+        return
+
+    ops, ndma, sent, bank, cur = [], [0], [0], [0], [0]
+
+    def op(q, fn, r=(), w=(), after=(), dma=None, remote=False):
+        ops.append({"q": q, "fn": fn, "r": list(r), "w": list(w), "dma": dma, "remote": remote,
+                    "after": [(k, v, {}, "x") for k, v in after]})
+
+    def dma(q, out, in_, r=(), w=(), after=(), sem=None):
+        if sem is None:
+            sem = ("d%d" % ndma[0], 16)
+            ndma[0] += 1
+        op(q, lambda e: e.dma_start(out, in_), r, w, after, dma=sem)
+        return sem
+
+    def tt(out, a, b, alu, r, w, after=()):
+        op("v", lambda e: e.tensor_tensor(out, a, b, alu), r, w, after)
+
+    def ts(out, a, s1, o1, r, w, s2=None, o2=None):
+        if o2 is None:
+            op("v", lambda e: e.tensor_scalar(out, a, s1, None, o1), r, w)
+        else:
+            op("v", lambda e: e.tensor_scalar(out, a, s1, s2, o1, o2), r, w)
+
+    def cp(out, a, r, w, q="v"):
+        if q == "v":
+            op("v", lambda e: e.tensor_copy(out, a), r, w)
+        else:
+            act(out, a, ACT.Copy, r, w)
+
+    def act(out, a, func, r, w, **kw):
+        op("a", lambda e: e.activation(out, a, func, **kw), r, w)
+
+    def mm(out, lhsT, rhs, start, stop, r, w, after=()):
+        op("p", lambda e: e.matmul(out, lhsT, rhs, start, stop), r, w, after)
+
+    def run(steps):
+        for f in steps:
+            f()
+
+    def peer(d):
+        return T.cores[(rank + d) % N]
+
+    def dstid(c):
+        rid, pid = topo.addr(c, core)
+        return DstId(rid=rid, pnc=pid)
+
+    def fused(transfers, r):
+        sent[0] += sum(len(t[1]) for t in transfers)
+        lst = [RemoteDMATransfer(dst_ids=[dstid(c)], dma_engine_mask=bits(en), remote_sem=T.sem[sem], src=src, dst=dst)
+               for c, en, sem, src, dst in transfers]
+        op("g", lambda e: e.remote_dma_fused(lst, local_sem=T.sem.sent), r, (), remote=True)
+
+    def next_bank():
+        bank[0] += 1
+        return "pw%d" % (bank[0] % 4)
+
+    far = topo.engines(core, peer(1))
+    share = 1
+    while 2 * share * (N - 1) <= len(far):
+        share *= 2
+    small = [far[i * share:(i + 1) * share] for i in range(N - 1)]
+    three = share * (N - 1)
+    hs = helpers_of(core, topo)
+    near = [e for e in topo.engines(core, hs[0]) if e not in far]
+    r0 = 32 * rank
+
+    dma("s", T.loA[:, :], T.lo[:, :], w=["loA"])
+    dma("a", T.V[:, 0:128], T.span[:, :], w=["V0"])
+    dma("a", T.n32[0:32, :], T.span[r0:r0 + 32, :], w=["n32"])
+    for k in range(2):
+        dma("s", T.n2i[0:16, 128 * k:128 * k + 128], T.span[r0:r0 + 32, 64 * k:64 * k + 64], w=["n2i%d" % k])
+    for d in range(1, N):
+        q0 = 32 * ((rank + d) % N)
+        dma("s", T.lost[:, 32 * (d - 1):32 * d], T.lo[q0:q0 + 32, :], w=["lost"] if d == N - 1 else [], sem=("lost", 16 * d))
+    dma("s", T.loB[r0:r0 + 32, :], T.lo[r0:r0 + 32, :], w=["loBown"])
+    dma("s", T.tabA[:, :], T.walk[:, :], w=["tabA"])
+    for s in range(6):
+        q0, a = 32 * ((rank + 1 + s // 2) % N), s % 2
+        dma("s", T.stage[:, s * PIECE:(s + 1) * PIECE], T.walk[q0:q0 + 32, a * HALF:(a + 1) * HALF], w=["stage%d" % s])
+
+    op("g", lambda e: e.iota(T.J[:, :], [[1, 128]], 0, 0), w=["J"])
+    op("g", lambda e: e.iota(T.Pi[:, 0:1], [[1, 1]], 0, 1), w=["Pi0"])
+    ts(T.Jt[:, 0:128], T.J[:, :], 4, ALU.arith_shift_right, ["J"], ["Jt0"])
+    ts(T.Jt[:, 128:256], T.J[:, :], 4, ALU.arith_shift_right, ["J"], ["Jt1"], 1, ALU.bitwise_and)
+    ts(T.Pi[:, 1:2], T.Pi[:, 0:1], 15, ALU.bitwise_and, ["Pi0"], ["Pi1"])
+    ts(T.Pi[:, 2:3], T.Pi[:, 0:1], 4, ALU.arith_shift_right, ["Pi0"], ["Pi2"])
+    ts(T.Pi[:, 3:4], T.Pi[:, 0:1], 4, ALU.arith_shift_right, ["Pi0"], ["Pi3"], 1, ALU.bitwise_and)
+    cp(T.Pf[:, 0:4], T.Pi[:, 0:4], ["Pi0", "Pi1", "Pi2", "Pi3"], ["Pf"])
+    ts(T.Jt[:, 256:384], T.J[:, :], 31, ALU.bitwise_and, ["J"], ["Jt2"])
+    ts(T.M16[:, :], T.J[:, 0:16], T.Pf[:, 1:2], ALU.is_equal, ["J", "Pf"], ["M16"])
+    ts(T.BD[:, 0:256], T.Jt[:, 0:256], T.Pf[:, 2:3], ALU.is_equal, ["Jt0", "Jt1", "Pf"], ["BD"])
+    ts(T.Jt[:, 384:512], T.J[:, :], 15, ALU.bitwise_and, ["J"], ["Jt3"])
+    ts(T.BD[32:64, 128:256], T.J[32:64, :], 0.0, ALU.mult, ["J"], ["BD"], 1.0, ALU.add)
+    for r in range(16):
+        if r % 8 < SEL_V:
+            ts(T.Sel[:, 256 * r:256 * r + 256], T.BD[:, :], T.M16[:, r:r + 1], ALU.mult, ["BD", "M16"], ["Sel%d" % r])
+        else:
+            act(T.Sel[:, 256 * r:256 * r + 256], T.BD[:, :], ACT.Identity, ["BD", "M16"], ["Sel%d" % r], scale=T.M16[:, r:r + 1])
+
+    ts(T.V[:, 128:256], T.V[:, 0:128], 1, ALU.arith_shift_right, ["V0"], ["V1"])
+    ts(T.tmpi[:, 0:128], T.V[:, 0:128], 1, ALU.bitwise_and, ["V0"], ["tm0"])
+    ts(T.tmpi[:, 128:256], T.V[:, 0:128], 2, ALU.arith_shift_right, ["V0"], ["tm1"])
+    tt(T.tmpi[:, 256:384], T.tmpi[:, 0:128], T.V[:, 128:256], ALU.mult, ["tm0", "V1"], ["tm2"])
+    tt(T.tmpi[:, 128:256], T.V[:, 128:256], T.tmpi[:, 128:256], ALU.subtract, ["V1", "tm1"], ["tm1"])
+    cp(T.offA[:, 0:128], T.loA[:, :], ["loA"], ["offA0"])
+    tt(T.V[:, 256:384], T.tmpi[:, 128:256], T.tmpi[:, 256:384], ALU.add, ["tm1", "tm2"], ["V2"])
+    ts(T.Ibf[:, :], T.J[:, :], T.Pf[:, 0:1], ALU.is_equal, ["J", "Pf"], ["Ibf"])
+    ts(T.V16[:, :], T.V[:, :], -MID, ALU.add, ["V0", "V1", "V2"], ["V16"])
+    for i in range(3):
+        tt(T.XI[:, 128 * i:128 * i + 128], T.loA[:, :], T.V[:, 128 * i:128 * i + 128], ALU.add, ["loA", "V%d" % i], ["XI%d" % i])
+    ts(T.Ineg[:, :], T.J[:, :], T.Pf[:, 0:1], ALU.is_equal, ["J", "Pf"], ["Ineg"], -1.0, ALU.mult)
+    cp(T.offA[:, 128:512], T.XI[:, :], ["XI0", "XI1", "XI2"], ["offA1"])
+
+    fused([(peer(d), small[d - 1], "lo_in", T.lost[:, 32 * (d - 1):32 * d], T.lold[:, 32 * (d - 1):32 * d])
+           for d in range(1, N)], ["lost"])
+    for d in range(1, N):
+        s = 2 * (d - 1)
+        a0, a1 = slice(s * PIECE, (s + 1) * PIECE), slice((s + 1) * PIECE, (s + 2) * PIECE)
+        fused([(peer(d), far, "in%d" % s, T.stage[:, a0], T.land[:, a0]),
+               (hs[d - 1], near, "hin", T.stage[:, a1], T.stage[:, a1])], ["stage%d" % s, "stage%d" % (s + 1)])
+    for d in range(1, N):
+        q0 = 32 * ((rank - d) % N)
+        dma("s", T.loB[q0:q0 + 32, :], T.lold[:, 32 * (d - 1):32 * d], after=[("lo_in", three)],
+            w=["loB"] if d == N - 1 else [], sem=("lorel", 16 * d))
+    for i, s in enumerate(RELAYOUT):
+        q0, a = 32 * ((rank - 1 - s // 2) % N), s % 2
+        if i == 1:
+            dma("s", T.tabB[r0:r0 + 32, :], T.walk[r0:r0 + 32, :], w=["tabBown"])
+        dma("s", T.tabB[q0:q0 + 32, a * HALF:(a + 1) * HALF], T.land[:, s * PIECE:(s + 1) * PIECE],
+            after=[("in%d" % s, len(far))], w=["tabB"] if i == 5 else [], sem=("relay", 16 * (i + 1)))
+
+    def spread(s, lhs, rhs, rr, b):
+        for r in range(8 * s, 8 * s + 8):
+            mm(T[b][:, 64 * (r - 8 * s):64 * (r - 8 * s) + 64], lhs(r), rhs, True, True, rr + ["Sel%d" % r], [b])
+
+    def selA(r):
+        return T.Sel[:, 256 * r:256 * r + 128]
+
+    def selB(r):
+        return T.Sel[0:48, 256 * r + 128:256 * r + 256]
+
+    def spreadA(k, s):
+        for i, name in enumerate(("nA", "mA", "wA")):
+            b, c0 = next_bank(), 1024 * k + 512 * s
+            spread(s, selA, T.V16[:, 128 * i + 64 * k:128 * i + 64 * k + 64], ["V16"], b)
+            if EVAC_A[3 * (2 * k + s) + i] == "a":
+                act(T[name][:, c0:c0 + 512], T[b][:, :], ACT.Identity, [b], [name + "%d%d" % (k, s)], bias=MID)
+            else:
+                ts(T[name][:, c0:c0 + 512], T[b][:, :], MID, ALU.add, [b], [name + "%d%d" % (k, s)])
+
+    def spread_nB(k, s):
+        b, c0 = next_bank(), 1024 * k + 512 * s
+        spread(s, selB, T.nb16[0:48, 64 * k:64 * k + 64], ["nb16", "nbc"], b)
+        cp(T.nB[:, c0:c0 + 512], T[b][:, :], [b], ["nB%d%d" % (k, s)], EVAC_B[2 * k + s])
+
+    def more_constants():
+        ts(T.If[:, :], T.J[:, :], T.Pf[:, 0:1], ALU.is_equal, ["J", "Pf"], ["If"])
+        cp(T.n2f[0:16, :], T.n2i[0:16, :], ["n2i0", "n2i1"], ["n2f"])
+        ts(T.onesA[:, :], T.J[:, 0:8], T.Pf[:, 2:3], ALU.is_equal, ["J", "Pf"], ["onesA"])
+        ts(T.onesB[:, :], T.J[:, 0:8], T.Pf[:, 3:4], ALU.is_equal, ["J", "Pf"], ["onesB"])
+        ts(T.Rep[0:32, :], T.Jt[0:32, 256:384], T.Pf[0:32, 0:1], ALU.is_equal, ["Jt2", "Pf"], ["Rep0"])
+        ts(T.Rep[32:64, :], T.Jt[32:64, 384:512], T.Pf[32:64, 1:2], ALU.is_equal, ["Jt3", "Pf"], ["Rep1"])
+        ts(T.nb16[32:64, :], T.J[32:64, :], 0.0, ALU.mult, ["J"], ["nbc"], MID, ALU.add)
+        ts(T.w16[32:64, :], T.J[32:64, :], 0.0, ALU.mult, ["J"], ["wc"], MID, ALU.add)
+        ts(T.nb16[0:32, :], T.n32[0:32, :], -MID, ALU.add, ["n32"], ["nb16"])
+        op("v", lambda e: e.memset(T.Z[:, :], 0.0), w=["Z0", "Z1"])
+        op("v", lambda e: e.memset(T.Q0[:, 0, :], 0.0), w=["Q0l"])
+
+    def diff(b, s, x, rx, y, ry):
+        for r in range(8 * s, 8 * s + 8):
+            o = T[b][:, 64 * (r - 8 * s):64 * (r - 8 * s) + 64]
+            mm(o, T.Ibf[:, :], x[0][:, x[1] + r:x[1] + 1024:16], True, False, rx + ["Ibf"], [b])
+            mm(o, T.Ineg[:, :], y[0][:, y[1] + r:y[1] + 1024:16], False, True, ry + ["Ineg"], [b])
+
+    def sums(slot, s, col, ones, width, rones):
+        for u in range(4 * s, 4 * s + 4):
+            c0 = 512 * slot + 128 * (u - 4 * s)
+            mm(T.pg[:, col + u:col + 8 * width:8], T.Db[:, c0:c0 + 128], ones[:, 0:width], True, True,
+               ["D%d" % slot, rones], ["pg"])
+
+    def absD(slot):
+        act(T.Db[:, 512 * slot:512 * slot + 512], T.Db[:, 512 * slot:512 * slot + 512], ACT.Abs, ["D%d" % slot], ["D%d" % slot])
+
+    def gm(k):
+        return T.sm[:, 16 * k:16 * k + 16]
+
+    def after_probe():
+        Q, qn = T["Q%d" % cur[0]], "Q%d" % cur[0]
+        gp, hh, c2, w_ = T.gp, T.hh, T.c2, T.Z[:, 1:65:2]
+        return [
+            lambda: tt(Q[:, 2, :], Q[:, 3, :], w_, ALU.min, [qn + "m", "Z0", "Z1"], [qn + "p"]),
+            lambda: tt(Q[:, 4, :], Q[:, 3, :], w_, ALU.max, [qn + "m", "Z0", "Z1"], [qn + "q"]),
+            lambda: tt(T.sm[:, 96:128], w_, Q[:, 3, :], ALU.is_gt, [qn + "m", "Z0", "Z1"], ["rt"]),
+            lambda: tt(gp[:, :, :], Q[:, 2:7:2, :], Q[:, 0:5:2, :], ALU.subtract, [qn + c for c in "lpqr"], ["gp"]),
+            lambda: ts(hh[:, :, :], gp[:, :, :], 1, ALU.arith_shift_right, ["gp"], ["hh"]),
+            lambda: tt(c2[:, 0:2, :], gp[:, 1:3, :], gp[:, 0:2, :], ALU.is_gt, ["gp"], ["ca"]),
+            lambda: tt(c2[:, 2:4, :], Q[:, 2:5:2, :], hh[:, 1:3, :], ALU.add, [qn + "p", qn + "q", "hh"], ["cb"]),
+            lambda: tt(c2[:, 4:6, :], Q[:, 2:5:2, :], hh[:, 0:2, :], ALU.subtract, [qn + "p", qn + "q", "hh"], ["cc"]),
+            lambda: tt(c2[:, 0:2, :], c2[:, 0:2, :], c2[:, 2:4, :], ALU.mult, ["ca", "cb"], ["ca"]),
+            lambda: tt(c2[:, 6:8, :], c2[:, 0:2, :], c2[:, 4:6, :], ALU.max, ["ca", "cc"], ["w2"]),
+        ]
+
+    def new_bracket():
+        Q, qn = T["Q%d" % cur[0]], "Q%d" % cur[0]
+        cur[0] ^= 1
+        P, pn = T["Q%d" % cur[0]], "Q%d" % cur[0]
+        st = [lambda i=i: tt(T.t3[:, i, :], T.sm[:, 64:96], Q[:, 2 + 2 * i, :], ALU.mult, ["low0", "low1", qn + "pqr"[i]], ["t%d" % i])
+              for i in range(3)]
+        st += [lambda: tt(P[:, 0:7:3, :], T.t3[:, :, :], Q[:, 0:5:2, :], ALU.max,
+                          ["t0", "t1", "t2", qn + "l", qn + "p", qn + "q"], [pn + "l", pn + "m", pn + "r"])]
+        return st + after_probe()
+
+    def choose(k, gw_, rg, last):
+        Q, qn, c2, a = T["Q%d" % cur[0]], "Q%d" % cur[0], T.c2, slice(16 * k, 16 * k + 16)
+        up, low, rt, tw = (T.sm[:, c + 16 * k:c + 16 + 16 * k] for c in (32, 64, 96, 128))
+        f0 = 128 * k + r0
+        chain = [lambda: tt(up, gw_, gm(k), ALU.is_gt, rg + ["gm%d" % k], ["up%d" % k]),
+                 lambda: tt(low, up, rt, ALU.is_equal, ["up%d" % k, "rt"], ["low%d" % k])]
+        if last:
+            chain[1:1] = [lambda: tt(T.fl[:, f0 + 1:f0 + 32:2], gw_, gm(k), ALU.max, rg + ["gm%d" % k], ["flg%d" % k])]
+            return chain + [lambda: tt(tw, low, Q[:, 4, a], ALU.mult, ["low%d" % k, qn + "q"], ["tw%d" % k]),
+                            lambda: tt(T.fl[:, f0:f0 + 32:2], tw, Q[:, 2, a], ALU.max, ["tw%d" % k, qn + "p"], ["flm%d" % k]),
+                            lambda: finish(k)], []
+        chain += [lambda: tt(tw, low, c2[:, 7, a], ALU.mult, ["low%d" % k, "w2"], ["tw%d" % k]),
+                  lambda: (tt(T.Z[:, 32 * k + 1:32 * k + 33:2], tw, c2[:, 6, a], ALU.max, ["tw%d" % k, "w2"], ["Z%d" % k]), turn(k)),
+                  lambda: (centre(k), columns(T.w16, ["w16%d" % k, "wc"], 64 * k, 64)),
+                  lambda: (offsets(k), pick(k, 0)), lambda: wrep(k, 0), lambda: wrep(k, 1), lambda: pick(k, 1)]
+        rest = [lambda: tt(gm(k), gw_, gm(k), ALU.max, rg + ["gm%d" % k], ["gm%d" % k])]
+        return chain, rest + (new_bracket() if k == 1 else [])
+
+    def turn(k):
+        z = 32 * k
+        mm(T.px[0:32, 0:64], T.Z[:, z + 1:z + 33], T.If[:, 0:64], True, False, ["Z%d" % k, "If"], ["px"])
+        mm(T.px[0:32, 0:64], T.Z[:, z:z + 32], T.If[:, 64:128], False, True, ["Z%d" % k, "If"], ["px"])
+
+    def centre(k):
+        ts(T.w16[0:32, 64 * k:64 * k + 64], T.px[0:32, 0:64], -MID, ALU.add, ["px"], ["w16%d" % k])
+
+    def columns(src, rs, c0, n):
+        o = T.px[:, 128:128 + n]
+        mm(o, T.Ibf[:, :], T.lohi[:, c0:c0 + n], True, False, ["Ibf", "lohi"], ["px"])
+        mm(o, T.Ibf[:, :], T.lolo[:, c0:c0 + n], False, False, ["Ibf", "lolo"], ["px"])
+        mm(o, T.Rep[0:48, :], src[0:48, c0:c0 + n], False, True, rs + ["Rep0", "Rep1"], ["px"])
+
+    def offsets(k):
+        cp(T.offw[:, 64 * k:64 * k + 64], T.px[:, 128:192], ["px"], ["offw%d" % k])
+
+    def wrep(k, s):
+        spread(s, selB, T.w16[0:48, 64 * k:64 * k + 64], ["w16%d" % k, "wc"], "pw%d" % (2 * k + s))
+
+    def pick(k, part):
+        c0 = 64 * k + 32 * part
+        cp(T.gw[:, 16 * c0:16 * c0 + 512], T.tabB[:, 0:W].indirect(T.offw[:, c0:c0 + 32]),
+           ["tabB", "tabBown", "offw%d" % k], ["gw%d%d" % (k, part)], "a")
+
+    def dS(k, s):
+        diff("pd%d" % s, s, (T.gw, 1024 * k), ["gw%d0" % k, "gw%d1" % k], (T.g0B, 1024 * k), ["g0B%d" % k])
+
+    def opB(k, s):
+        b, c0 = "pw%d" % (2 * k + s), 1024 * k + 512 * s
+        tt(T[b][:, :], T[b][:, :], T.riseB[:, c0:c0 + 512], ALU.mult, [b, "rB%d%d" % (k, s)], [b])
+
+    def opA(k, s):
+        c0 = 1024 * k + 512 * s
+        tt(T.Ab[:, 512 * s:512 * s + 512], T["pd%d" % s][:, :], T.nB[:, c0:c0 + 512], ALU.mult,
+           ["pd%d" % s, "nB%d%d" % (k, s)], ["A%d" % s])
+
+    def opD(k, s):
+        b, slot = "pw%d" % (2 * k + s), 2 * k + s
+        tt(T.Db[:, 512 * slot:512 * slot + 512], T.Ab[:, 512 * s:512 * s + 512], T[b][:, :], ALU.subtract, ["A%d" % s, b], ["D%d" % slot])
+
+    def sumB(k, s):
+        sums(2 * k + s, s, 256 + 16 * k, T.onesB, 2, "onesB")
+
+    def start_state():
+        n = T.nTi
+        for k in range(2):
+            mm(T.px[:, 256 + 16 * k:272 + 16 * k], T.n2f[0:16, 128 * k:128 * k + 128], T.If[0:16, 0:16], True, True, ["n2f", "If"], ["px"])
+        cp(n[:, 0:32], T.px[:, 256:288], ["px"], ["n0"])
+        ts(n[:, 32:64], n[:, 0:32], 1, ALU.arith_shift_right, ["n0"], ["n1"])
+        ts(n[:, 64:96], n[:, 0:32], 2, ALU.arith_shift_right, ["n0"], ["n2"])
+        ts(n[:, 96:128], n[:, 0:32], 1, ALU.bitwise_and, ["n0"], ["n3"])
+        tt(n[:, 64:96], n[:, 32:64], n[:, 64:96], ALU.subtract, ["n1", "n2"], ["n2"])
+        tt(n[:, 96:128], n[:, 32:64], n[:, 96:128], ALU.mult, ["n1", "n3"], ["n3"])
+        cp(T.Q0[:, 6, :], n[:, 0:32], ["n0"], ["Q0r"])
+        cp(T.Q0[:, 3, :], n[:, 32:64], ["n1"], ["Q0m"])
+        tt(T.Z[:, 1:65:2], n[:, 64:96], n[:, 96:128], ALU.add, ["n2", "n3"], ["Z0", "Z1"])
+        run(after_probe())
+
+    def pickA(k, i):
+        cp(T.gA[:, 2048 * i + 1024 * k:2048 * i + 1024 * k + 1024],
+           T.tabA[:, 0:W].indirect(T.offA[:, 128 * i + 64 * k:128 * i + 64 * k + 64]),
+           ["tabA", "offA0" if i == 0 else "offA1"], ["gA%d%d" % (i, k)], PICK_A[4 * k + i])
+
+    def evalA(k, s):
+        b, c0 = next_bank(), 1024 * k + 512 * s
+        diff(b, s, (T.gA, 2048 + 1024 * k), ["gA1%d" % k], (T.gA, 1024 * k), ["gA0%d" % k])
+        for ev in range(2):
+            diff("pd%d" % ev, s, (T.gA, 2048 * (2 + ev) + 1024 * k), ["gA%d%d" % (2 + ev, k)], (T.gA, 1024 * k), ["gA0%d" % k])
+        for ev in range(2):
+            name, pd = ("mA", "wA")[ev], "pd%d" % ev
+            tt(T.Ab[:, 512 * ev:512 * ev + 512], T[b][:, :], T[name][:, c0:c0 + 512], ALU.mult, [b, name + "%d%d" % (k, s)], ["A%d" % ev])
+            tt(T[pd][:, :], T[pd][:, :], T.nA[:, c0:c0 + 512], ALU.mult, [pd, "nA%d%d" % (k, s)], [pd])
+        for ev in range(2):
+            pd, slot = "pd%d" % ev, 2 * s + ev
+            tt(T.Db[:, 512 * slot:512 * slot + 512], T[pd][:, :], T.Ab[:, 512 * ev:512 * ev + 512], ALU.subtract, [pd, "A%d" % ev], ["D%d" % slot])
+            absD(slot)
+
+    def sumA(k, s):
+        for ev in range(2):
+            sums(2 * s + ev, s, 128 * k + 64 * ev, T.onesA, 8, "onesA")
+
+    def send_parts(k):
+        ps = T["ps%d" % k]
+        for ev in range(2):
+            cp(ps[:, :, 16 * ev:16 * ev + 16], T.pg[:, 128 * k + 64 * ev:128 * k + 64 * ev + 64], ["pg"], ["ps%d%d" % (k, ev)])
+        fused([(peer(d), small[d - 1], "part%d" % k, ps[:, (rank + d) % N, :], T.pl[:, 96 * k + 32 * (d - 1):96 * k + 32 * d])
+               for d in range(1, N)], ["ps%d0" % k, "ps%d1" % k])
+
+    def add_parts(k):
+        ps, a = T["ps%d" % k], 96 * k
+        tt(T.g2[:, a:a + 32], ps[:, rank, :], T.pl[:, a:a + 32], ALU.add, ["ps%d0" % k, "ps%d1" % k], ["g2a%d" % k],
+           after=[("part%d" % k, three)])
+        tt(T.g2[:, a + 32:a + 64], T.pl[:, a + 32:a + 64], T.pl[:, a + 64:a + 96], ALU.add, [], ["g2b%d" % k])
+        tt(gm(k), T.g2[:, a:a + 16], T.g2[:, a + 32:a + 48], ALU.add, ["g2a%d" % k, "g2b%d" % k], ["gm%d" % k])
+        tt(T.g2[:, a + 64:a + 80], T.g2[:, a + 16:a + 32], T.g2[:, a + 48:a + 64], ALU.add, ["g2a%d" % k, "g2b%d" % k], ["g2c%d" % k])
+
+    def lo_setup():
+        cp(T.lohi[:, :], T.loB[:, :], ["loB", "loBown"], ["lohi"])
+        cp(T.offB[:, 0:128], T.loB[:, :], ["loB", "loBown"], ["offB0"])
+        tt(T.lolo[:, :], T.loB[:, :], T.lohi[:, :], ALU.subtract, ["loB", "loBown", "lohi"], ["lolo"])
+        columns(T.nb16, ["nb16", "nbc"], 0, 128)
+        cp(T.offB[:, 128:256], T.px[:, 128:256], ["px"], ["offB1"])
+
+    def endB(k, i):
+        name = ("g0B", "geB")[i]
+        cp(T[name][:, 1024 * k:1024 * k + 1024], T.tabB[:, 0:W].indirect(T.offB[:, 128 * i + 64 * k:128 * i + 64 * k + 64]),
+           ["tabB", "tabBown", "offB%d" % i], [name + "%d" % k], PICK_B[2 * k + i])
+
+    def riseB(k):
+        for s in range(2):
+            b, c0 = "pd%d" % s, 1024 * k + 512 * s
+            diff(b, s, (T.geB, 1024 * k), ["geB%d" % k], (T.g0B, 1024 * k), ["g0B%d" % k])
+            cp(T.riseB[:, c0:c0 + 512], T[b][:, :], [b], ["rB%d%d" % (k, s)], RISE_B[2 * k + s])
+
+    def finish(k):
+        f0 = 128 * k + r0
+        sent[0] += len(far)
+        one = RemoteDMATransfer(dst_ids=[dstid(peer(d)) for d in range(1, N)], dma_engine_mask=bits(far), remote_sem=T.sem["fin%d" % k],
+                                srcs=[T.fl[:, f0:f0 + 32]], dsts=[T.fl[:, f0:f0 + 32]] * (N - 1))
+        op("g", lambda e: e.remote_dma_fused([one], local_sem=T.sem.sent), ["flm%d" % k, "flg%d" % k], (), remote=True)
+
+    def store(k):
+        b = "pw%d" % (2 * k)
+        for o in range(2):
+            mm(T[b][0:64, 128 * o:128 * o + 128], T.fl[:, 128 * k + o:128 * k + 128:2], T.If[:, :], True, True,
+               ["flm%d" % k, "flg%d" % k, "If"], [b], after=[("fin%d" % k, len(far) * (N - 1))])
+        cp(T.fs[0:64, 256 * k:256 * k + 256], T[b][0:64, 0:256], [b], ["fs%d" % k])
+        return [dma("sa"[o], (T.ym, T.yg)[o][:, 64 * k:64 * k + 64], T.fs[0:64, 256 * k + 128 * o:256 * k + 128 * o + 128], r=["fs%d" % k])
+                for o in range(2)]
+
+    def early(k, ch):
+        (dS, opA, opB)[EARLY.index(ch) // 2](k, EARLY.index(ch) % 2)
+
+    first = []
+    todo = {"c": more_constants, "l": lo_setup, "i": start_state, "F": lambda: run(first[1]),
+            "f": lambda: (first.extend(choose(0, T.g2[:, 64:80], ["g2c0"], False)), run(first[0])),
+            "z": lambda: [early(0, ch) for ch in ORDER[0] if ch in EARLY]}
+    for k in range(2):
+        todo["p%d" % k] = lambda k=k: send_parts(k)
+        todo["q%d" % k] = lambda k=k: add_parts(k)
+        todo["r%d" % k] = lambda k=k: riseB(k)
+        for s in range(2):
+            todo["e%d%d" % (k, s)] = lambda k=k, s=s: endB(k, s)
+            todo["s%d%d" % (k, s)] = lambda k=k, s=s: spreadA(k, s)
+            todo["n%d%d" % (k, s)] = lambda k=k, s=s: spread_nB(k, s)
+            todo["a%d%d" % (k, s)] = lambda k=k, s=s: evalA(k, s)
+            todo["u%d%d" % (k, s)] = lambda k=k, s=s: sumA(k, s)
+        for i in range(4):
+            todo["g%d%d" % (k, i)] = lambda k=k, i=i: pickA(k, i)
+    for name in OPENING.split():
+        todo[name]()
+
+    steps = 2 * (ROUNDS - 1)
+    for t in range(1, steps + 1):
+        y, x = t % 2, 1 - t % 2
+        gw_, rg = (T.g2[:, 160:176], ["g2c1"]) if t == 1 else (T.pg[:, 256 + 16 * y:272 + 16 * y], ["pg"])
+        chain, rest = choose(y, gw_, rg, t == steps)
+        if t == steps - 1:
+            rest = rest[:8]
+        big = {"b": lambda: opB(x, 0), "B": lambda: opB(x, 1), "a": lambda: opA(x, 0), "A": lambda: opA(x, 1),
+               "d": lambda: opD(x, 0), "D": lambda: opD(x, 1), "v": lambda: absD(2 * x), "V": lambda: absD(2 * x + 1),
+               "s": lambda: sumB(x, 0), "S": lambda: sumB(x, 1), "e": lambda: dS(x, 0), "E": lambda: dS(x, 1)}
+        for ch in ORDER[y]:
+            if ch in EARLY:
+                if t < steps:
+                    early(y, ch)
+            elif ch == ".":
+                run(chain[:1])
+                chain = chain[1:]
+            elif ch == ",":
+                run(rest[:1])
+                rest = rest[1:]
+            else:
+                big[ch]()
+    y = 1 - steps % 2
+    run(choose(y, T.pg[:, 256 + 16 * y:272 + 16 * y], ["pg"], True)[0])
+    stored = store(1 - y) + store(y)
+    op("g", None, after=stored + [("sent", sent[0])])
+    emit(g, T, ops)

@@ -7,35 +7,45 @@ N, W, ROUNDS = 4, 6144, 7
 HALF = W // 2
 PIECE = HALF // 4
 MID = 2048.0
+KY = 2046.0
+WHOLE = 12582912.0
+UNDER = 0.4998
 F32, BF, F16, I32, U16 = "float32", "bfloat16", "float16", "int32", "uint16"
 
 SCRATCH = {name: ("sbuf", [128] + shape, kind) for names, shape, kind in (
     ("tabA tabB", [W], BF), ("stage land", [6 * PIECE], BF), ("lost lold", [96], I32),
-    ("loA loB n32 J nTi", [128], I32), ("V XI tmpi", [384], I32), ("V16", [384], F16), ("Jt", [512], I32),
-    ("offA", [512], U16), ("offB", [256], U16), ("offw", [128], U16), ("nb16 w16 Rep", [128], F16),
-    ("n2i", [256], I32), ("n2f fl", [256], F32), ("lohi lolo Ibf Ineg", [128], BF), ("If", [128], F32),
-    ("Pi", [8], I32), ("Pf onesA onesB", [8], F32), ("M16", [16], F32), ("BD", [256], BF), ("Sel", [4096], BF),
-    ("nA mA wA nB Db", [2048], F32), ("riseB g0B geB gw", [2048], BF), ("gA", [8192], BF), ("Ab", [1024], F32),
-    ("ps0 ps1", [4, 32], F32), ("pl g2", [192], F32), ("Q0 Q1", [7, 32], F32), ("t3", [3, 32], F32),
-    ("gp hh", [3, 32], I32), ("c2", [8, 32], F32), ("sm", [160], F32), ("Z", [72], F32),
-    ("fs", [512], F32)) for name in names.split()}
+    ("loA n4 J", [128], I32), ("V XI tmpi", [384], I32), ("LB", [256], I32), ("V16", [512], F16), ("Jt", [384], I32),
+    ("offA", [512], U16), ("offB", [256], U16), ("offw", [128], U16), ("nb16 w16 K0 K1 K2", [128], F16),
+    ("lohi lolo Ibf Ineg", [128], BF), ("If Inf lo2", [128], F32), ("fl", [256], F32),
+    ("Pi", [8], I32), ("Pf onesB", [8], F32), ("M16 onesA", [16], F32), ("BD", [256], BF), ("Sel", [4096], BF),
+    ("nA wA nB Db", [2048], F32), ("riseB g0B geB gw", [2048], BF), ("gA", [8192], BF), ("Ab", [1024], F32),
+    ("X", [2, 14, 24], I32), ("S2", [8, 24], F32), ("S1", [4, 24], F32), ("CO PR", [4, 16], F32),
+    ("Q0 Q1", [7, 128], F32), ("D0", [2, 128], F32), ("RW", [3, 128], F32), ("CH", [2, 96], F32), ("FC", [2, 64], F32),
+    ("t3", [3, 32], F32), ("gm", [2, 32], F32), ("tm", [32], F32), ("Z", [200], F16), ("fs", [512], F32)) for name in names.split()}
 PSUM = ("pd0", "pd1", "pw0", "pw1", "pw2", "pw3", "pg", "px")
 SCRATCH.update({name: ("psum", [128, 512], F32) for name in PSUM})
-SEMAPHORES = (["cv", "ca", "cp", "cg", "sent", "hin", "lo_in", "part0", "part1", "fin0", "fin1", "relay", "lorel", "lost"]
-              + ["in%d" % i for i in range(6)] + ["d%d" % i for i in range(24)])
+SCRATCH["pg"] = ("psum", [128, 32, 16], F32)
+SEMAPHORES = (["cv", "ca", "cp", "cg", "sent", "hin", "lo_in", "part0", "part1", "fin0", "fin1"]
+              + ["in%d" % i for i in range(6)] + ["d%d" % i for i in range(40)])
 CSEM = {"v": "cv", "a": "ca", "p": "cp", "g": "cg"}
 
-SEL_V = 2
-EVAC_A = "aavvavavaaaa"
+SEL_ON = "vvavvavavvavvava"
+EVAC_A = "aaaaaaaa"
 EVAC_B = "aaaa"
-PICK_A = "vavaaaaa"
-PICK_B = "aaav"
-RISE_B = "vvaa"
+PICK_A = "avavavav"
+PICK_B = "vaaa"
+RISE_B = "aaaa"
 RELAYOUT = (0, 2, 4, 1, 3, 5)
-OPENING = ("s00 s10 g01 s01 g02 g03 g11 g12 g00 g10 c a00 s11 a01 g13 u00 i n01 n00 u01 n10 p0 a10 a11 q0 n11 u10 u11 "
-           "l e00 p1 e01 e10 f e11 F r0 r1 z q1")
-ORDER = ("..b.Ea.d.vA.,.DVs..5S", "Be..,.,.,,Ea.dA,v..,D,Vs,.,,,,,,6.S1,")
-EARLY = "123456"
+ON_PE = ()
+SPLIT_SCAN = True
+
+CYC, PE_CYC, FIX, WAKE, PICK = 0.83, 0.42, {"v": 50, "a": 65, "g": 130}, 90, 1.5
+AHEAD = 100
+LOAD = 2000
+LOAD_BIG = 5000
+CROSS = 3000
+CROSS_LO = 13000
+CROSS_BIG = 16000
 
 
 def bits(engines):
@@ -49,6 +59,59 @@ def helpers_of(core, topo):
     return [c for c in topo.cores_of(core) if topo.die(c) != topo.die(core)]
 
 
+def arrange(ops):
+    writer, readers, deps = {}, {}, []
+    for i, op in enumerate(ops):
+        d = set()
+        for r in op["r"]:
+            if r in writer:
+                d.add(writer[r])
+            if r in PSUM:
+                d.update(j for j in readers.get(r, []) if ops[j]["q"] != op["q"])
+        for r in op["w"]:
+            if r in writer:
+                d.add(writer[r])
+            d.update(readers.get(r, []))
+        d.discard(i)
+        deps.append(d)
+        for r in op["r"]:
+            readers.setdefault(r, []).append(i)
+        for r in op["w"]:
+            writer[r] = i
+            readers[r] = []
+    users = [[] for op in ops]
+    for i, d in enumerate(deps):
+        for j in d:
+            users[j].append(i)
+
+    def gap(j, i):
+        if ops[j]["q"] == ops[i]["q"] and (ops[i]["q"] == "p" or "#" + ops[i]["q"] in ops[i]["w"]):
+            return ops[j]["busy"]
+        return ops[j]["done"] + WAKE
+
+    left = [len(d) for d in deps]
+    ready = [0.0] * len(ops)
+    pool = {q: [] for q in "vapgs"}
+    free = {q: 0.0 for q in pool}
+    for i, op in enumerate(ops):
+        if not left[i]:
+            pool[op["q"]].append(i)
+    order = []
+    while len(order) < len(ops):
+        t, q = min((max(free[q], min(ready[i] for i in pool[q])), q) for q in pool if pool[q])
+        i = min(i for i in pool[q] if ready[i] <= t + ops[i]["ahead"])
+        pool[q].remove(i)
+        start = max(t, ready[i])
+        free[q] = start + ops[i]["busy"]
+        order.append(i)
+        for u in users[i]:
+            ready[u] = max(ready[u], start + gap(i, u))
+            left[u] -= 1
+            if not left[u]:
+                pool[ops[u]["q"]].append(u)
+    return [ops[i] for i in order]
+
+
 def emit(g, T, ops):
     queue = {"v": g.vector, "a": g.scalar, "p": g.tensor, "g": g, "s": g.sync}
     know = {q: {} for q in queue}
@@ -56,6 +119,7 @@ def emit(g, T, ops):
     writer, readers, needed, plan = {}, {}, set(), []
     for op in ops:
         q = op["q"]
+        op = dict(op, r=[r for r in op["r"] if r[0] not in "@#"], w=[r for r in op["w"] if r[0] not in "@#"])
         deps = list(op["after"])
         for r in op["r"]:
             if r in writer:
@@ -81,7 +145,7 @@ def emit(g, T, ops):
                 if t[0] in CSEM:
                     needed.add((t[0], t[1]))
         if op["dma"]:
-            tok = (op["dma"][0], op["dma"][1], dict(know[q]), "dma")
+            tok = (op["dma"], 16, dict(know[q]), "dma")
         elif op["fn"] is None or op["remote"]:
             tok = None
         else:
@@ -112,7 +176,7 @@ def emit(g, T, ops):
             continue
         ins = op["fn"](e)
         if op["dma"]:
-            ins.then_inc(T.sem[op["dma"][0]], 16)
+            ins.then_inc(T.sem[op["dma"]], 16)
         elif tok and (tok[0], tok[1]) in needed:
             ins.then_inc(T.sem[CSEM[tok[0]]], 1)
 
@@ -139,43 +203,46 @@ def rank_program(g, core, T, topo):
         hand_on(g, core, T, topo)
         return
 
-    ops, ndma, sent, bank, cur = [], [0], [0], [0], [0]
+    ops, ndma, sent, bank, cur, now, ahead = [], [0], [0], [0], [0], [0], [0]
 
-    def op(q, fn, r=(), w=(), after=(), dma=None, remote=False):
-        ops.append({"q": q, "fn": fn, "r": list(r), "w": list(w), "dma": dma, "remote": remote,
-                    "after": [(k, v, {}, "x") for k, v in after]})
+    def op(q, fn, r, w, cycles=0, after=(), dma=None, remote=False, busy=None, done=None):
+        if busy is None:
+            busy = cycles * PE_CYC if q == "p" else FIX[q] + cycles * CYC
+        ops.append({"q": q, "fn": fn, "r": list(r), "w": list(w) + ["#" + q] * (q in "sg"), "dma": dma, "remote": remote, "busy": busy,
+                    "done": done or busy, "ahead": ahead[0], "after": [(k, v, {}, "x") for k, v in after]})
 
-    def dma(q, out, in_, r=(), w=(), after=(), sem=None):
-        if sem is None:
-            sem = ("d%d" % ndma[0], 16)
-            ndma[0] += 1
-        op(q, lambda e: e.dma_start(out, in_), r, w, after, dma=sem)
-        return sem
+    def dma(q, out, in_, r=(), w=(), after=(), done=LOAD):
+        sem = "d%d" % ndma[0]
+        ndma[0] += 1
+        op(q, lambda e: e.dma_start(out, in_), r, w, after=after, dma=sem, busy=60, done=done)
+        return sem, 16
 
-    def tt(out, a, b, alu, r, w, after=()):
-        op("v", lambda e: e.tensor_tensor(out, a, b, alu), r, w, after)
+    def tt(out, a, b, alu, r, w, c, after=()):
+        op("v", lambda e: e.tensor_tensor(out, a, b, alu), r, w, c, after)
 
-    def ts(out, a, s1, o1, r, w, s2=None, o2=None):
+    def ts(out, a, s1, o1, r, w, c, s2=None, o2=None):
         if o2 is None:
-            op("v", lambda e: e.tensor_scalar(out, a, s1, None, o1), r, w)
+            op("v", lambda e: e.tensor_scalar(out, a, s1, None, o1), r, w, c)
         else:
-            op("v", lambda e: e.tensor_scalar(out, a, s1, s2, o1, o2), r, w)
+            op("v", lambda e: e.tensor_scalar(out, a, s1, s2, o1, o2), r, w, c)
 
-    def cp(out, a, r, w, q="v"):
+    def cp(out, a, r, w, c, q="v"):
         if q == "v":
-            op("v", lambda e: e.tensor_copy(out, a), r, w)
+            op("v", lambda e: e.tensor_copy(out, a), r, w, c)
         else:
-            act(out, a, ACT.Copy, r, w)
+            act(out, a, ACT.Copy, r, w, c)
 
-    def act(out, a, func, r, w, **kw):
-        op("a", lambda e: e.activation(out, a, func, **kw), r, w)
+    def fill(out, x, w, c):
+        op("v", lambda e: e.memset(out, x), [], w, c)
 
-    def mm(out, lhsT, rhs, start, stop, r, w, after=()):
-        op("p", lambda e: e.matmul(out, lhsT, rhs, start, stop), r, w, after)
+    def scan(out, d0, d1, r, w, c):
+        op("v", lambda e: e.tensor_tensor_scan(out, d0, d1, 0.0, ALU.mult, ALU.add), r, w, c)
 
-    def run(steps):
-        for f in steps:
-            f()
+    def act(out, a, func, r, w, c, **kw):
+        op("a", lambda e: e.activation(out, a, func, **kw), r, w, c)
+
+    def mm(out, lhsT, rhs, start, stop, r, w, c=64, after=()):
+        op("p", lambda e: e.matmul(out, lhsT, rhs, start, stop), r, w, c, after)
 
     def peer(d):
         return T.cores[(rank + d) % N]
@@ -184,15 +251,15 @@ def rank_program(g, core, T, topo):
         rid, pid = topo.addr(c, core)
         return DstId(rid=rid, pnc=pid)
 
-    def fused(transfers, r):
+    def fused(transfers, r, w, done):
         sent[0] += sum(len(t[1]) for t in transfers)
         lst = [RemoteDMATransfer(dst_ids=[dstid(c)], dma_engine_mask=bits(en), remote_sem=T.sem[sem], src=src, dst=dst)
                for c, en, sem, src, dst in transfers]
-        op("g", lambda e: e.remote_dma_fused(lst, local_sem=T.sem.sent), r, (), remote=True)
+        op("g", lambda e: e.remote_dma_fused(lst, local_sem=T.sem.sent), r, w, remote=True, busy=600, done=done)
 
     def next_bank():
         bank[0] += 1
-        return "pw%d" % (bank[0] % 4)
+        return PSUM[bank[0] % 6]
 
     far = topo.engines(core, peer(1))
     share = 1
@@ -203,71 +270,93 @@ def rank_program(g, core, T, topo):
     hs = helpers_of(core, topo)
     near = [e for e in topo.engines(core, hs[0]) if e not in far]
     r0 = 32 * rank
+    TABB = ["tabB%d" % i for i in range(7)]
+    LOB = ["loB%d" % i for i in range(N)]
+    N4 = ["n4%d" % i for i in range(N)]
 
-    dma("s", T.loA[:, :], T.lo[:, :], w=["loA"])
     dma("a", T.V[:, 0:128], T.span[:, :], w=["V0"])
-    dma("a", T.n32[0:32, :], T.span[r0:r0 + 32, :], w=["n32"])
-    for k in range(2):
-        dma("s", T.n2i[0:16, 128 * k:128 * k + 128], T.span[r0:r0 + 32, 64 * k:64 * k + 64], w=["n2i%d" % k])
+    dma("a", T.loA[:, :], T.lo[:, :], w=["loA"])
     for d in range(1, N):
         q0 = 32 * ((rank + d) % N)
-        dma("s", T.lost[:, 32 * (d - 1):32 * d], T.lo[q0:q0 + 32, :], w=["lost"] if d == N - 1 else [], sem=("lost", 16 * d))
-    dma("s", T.loB[r0:r0 + 32, :], T.lo[r0:r0 + 32, :], w=["loBown"])
-    dma("s", T.tabA[:, :], T.walk[:, :], w=["tabA"])
+        dma("s", T.lost[:, 32 * (d - 1):32 * d], T.lo[q0:q0 + 32, :], w=["lost%d" % d])
+    dma("s", T.tabA[:, :], T.walk[:, :], w=["tabA"], done=LOAD_BIG)
     for s in range(6):
         q0, a = 32 * ((rank + 1 + s // 2) % N), s % 2
         dma("s", T.stage[:, s * PIECE:(s + 1) * PIECE], T.walk[q0:q0 + 32, a * HALF:(a + 1) * HALF], w=["stage%d" % s])
+    dma("s", T.LB[r0:r0 + 32, 0:128], T.lo[r0:r0 + 32, :], w=["loB0"])
+    for q in range(N):
+        dma("s", T.n4[32 * q:32 * q + 32, :], T.span[r0:r0 + 32, :], w=["n4%d" % q])
 
-    op("g", lambda e: e.iota(T.J[:, :], [[1, 128]], 0, 0), w=["J"])
-    op("g", lambda e: e.iota(T.Pi[:, 0:1], [[1, 1]], 0, 1), w=["Pi0"])
-    ts(T.Jt[:, 0:128], T.J[:, :], 4, ALU.arith_shift_right, ["J"], ["Jt0"])
-    ts(T.Jt[:, 128:256], T.J[:, :], 4, ALU.arith_shift_right, ["J"], ["Jt1"], 1, ALU.bitwise_and)
-    ts(T.Pi[:, 1:2], T.Pi[:, 0:1], 15, ALU.bitwise_and, ["Pi0"], ["Pi1"])
-    ts(T.Pi[:, 2:3], T.Pi[:, 0:1], 4, ALU.arith_shift_right, ["Pi0"], ["Pi2"])
-    ts(T.Pi[:, 3:4], T.Pi[:, 0:1], 4, ALU.arith_shift_right, ["Pi0"], ["Pi3"], 1, ALU.bitwise_and)
-    cp(T.Pf[:, 0:4], T.Pi[:, 0:4], ["Pi0", "Pi1", "Pi2", "Pi3"], ["Pf"])
-    ts(T.Jt[:, 256:384], T.J[:, :], 31, ALU.bitwise_and, ["J"], ["Jt2"])
-    ts(T.M16[:, :], T.J[:, 0:16], T.Pf[:, 1:2], ALU.is_equal, ["J", "Pf"], ["M16"])
-    ts(T.BD[:, 0:256], T.Jt[:, 0:256], T.Pf[:, 2:3], ALU.is_equal, ["Jt0", "Jt1", "Pf"], ["BD"])
-    ts(T.Jt[:, 384:512], T.J[:, :], 15, ALU.bitwise_and, ["J"], ["Jt3"])
-    ts(T.BD[32:64, 128:256], T.J[32:64, :], 0.0, ALU.mult, ["J"], ["BD"], 1.0, ALU.add)
-    for r in range(16):
-        if r % 8 < SEL_V:
-            ts(T.Sel[:, 256 * r:256 * r + 256], T.BD[:, :], T.M16[:, r:r + 1], ALU.mult, ["BD", "M16"], ["Sel%d" % r])
-        else:
-            act(T.Sel[:, 256 * r:256 * r + 256], T.BD[:, :], ACT.Identity, ["BD", "M16"], ["Sel%d" % r], scale=T.M16[:, r:r + 1])
+    op("g", lambda e: e.iota(T.J[:, :], [[1, 128]], 0, 0), [], ["J"], 256)
+    op("g", lambda e: e.iota(T.Pi[:, 0:1], [[1, 1]], 0, 1), [], ["Pi0"], 2)
+    ts(T.Jt[:, 0:128], T.J[:, :], 4, ALU.arith_shift_right, ["J"], ["Jt0"], 128)
+    ts(T.Jt[:, 128:256], T.J[:, :], 4, ALU.arith_shift_right, ["J"], ["Jt1"], 128, 1, ALU.bitwise_and)
+    ts(T.Jt[:, 256:272], T.J[:, 0:16], 7, ALU.bitwise_and, ["J"], ["Jt2"], 16)
+    ts(T.Pi[:, 1:2], T.Pi[:, 0:1], 15, ALU.bitwise_and, ["Pi0"], ["Pi1"], 1)
+    ts(T.Pi[:, 2:3], T.Pi[:, 0:1], 4, ALU.arith_shift_right, ["Pi0"], ["Pi2"], 1)
+    ts(T.Pi[:, 3:4], T.Pi[:, 0:1], 4, ALU.arith_shift_right, ["Pi0"], ["Pi3"], 1, 1, ALU.bitwise_and)
+    cp(T.Pf[:, 0:4], T.Pi[:, 0:4], ["Pi0", "Pi1", "Pi2", "Pi3"], ["Pf"], 4)
+    ts(T.M16[:, :], T.J[:, 0:16], T.Pf[:, 1:2], ALU.is_equal, ["J", "Pf"], ["M16"], 16)
+    ts(T.BD[:, 0:256], T.Jt[:, 0:256], T.Pf[:, 2:3], ALU.is_equal, ["Jt0", "Jt1", "Pf"], ["BD"], 256)
+    fill(T.BD[32:64, 128:256], 1.0, ["BD"], 64)
 
-    ts(T.V[:, 128:256], T.V[:, 0:128], 1, ALU.arith_shift_right, ["V0"], ["V1"])
-    ts(T.tmpi[:, 0:128], T.V[:, 0:128], 1, ALU.bitwise_and, ["V0"], ["tm0"])
-    ts(T.tmpi[:, 128:256], T.V[:, 0:128], 2, ALU.arith_shift_right, ["V0"], ["tm1"])
-    tt(T.tmpi[:, 256:384], T.tmpi[:, 0:128], T.V[:, 128:256], ALU.mult, ["tm0", "V1"], ["tm2"])
-    tt(T.tmpi[:, 128:256], T.V[:, 128:256], T.tmpi[:, 128:256], ALU.subtract, ["V1", "tm1"], ["tm1"])
-    cp(T.offA[:, 0:128], T.loA[:, :], ["loA"], ["offA0"])
-    tt(T.V[:, 256:384], T.tmpi[:, 128:256], T.tmpi[:, 256:384], ALU.add, ["tm1", "tm2"], ["V2"])
-    ts(T.Ibf[:, :], T.J[:, :], T.Pf[:, 0:1], ALU.is_equal, ["J", "Pf"], ["Ibf"])
-    ts(T.V16[:, :], T.V[:, :], -MID, ALU.add, ["V0", "V1", "V2"], ["V16"])
+    ts(T.V[:, 128:256], T.V[:, 0:128], 1, ALU.arith_shift_right, ["V0"], ["V1"], 128)
+    ts(T.tmpi[:, 0:128], T.V[:, 0:128], 1, ALU.bitwise_and, ["V0"], ["tm0"], 128)
+    ts(T.tmpi[:, 128:256], T.V[:, 0:128], 2, ALU.arith_shift_right, ["V0"], ["tm1"], 128)
+    tt(T.tmpi[:, 256:384], T.tmpi[:, 0:128], T.V[:, 128:256], ALU.mult, ["tm0", "V1"], ["tm2"], 256)
+    tt(T.tmpi[:, 128:256], T.V[:, 128:256], T.tmpi[:, 128:256], ALU.subtract, ["V1", "tm1"], ["tm1"], 256)
+    ts(T.V16[:, 0:128], T.V[:, 0:128], -MID, ALU.add, ["V0"], ["V160"], 128)
+    tt(T.V[:, 256:384], T.tmpi[:, 128:256], T.tmpi[:, 256:384], ALU.add, ["tm1", "tm2"], ["V2"], 256)
+    cp(T.offA[:, 0:128], T.loA[:, :], ["loA"], ["offA0"], 128)
+    ts(T.V16[:, 128:384], T.V[:, 128:384], -MID, ALU.add, ["V1", "V2"], ["V161", "V162"], 256)
     for i in range(3):
-        tt(T.XI[:, 128 * i:128 * i + 128], T.loA[:, :], T.V[:, 128 * i:128 * i + 128], ALU.add, ["loA", "V%d" % i], ["XI%d" % i])
-    ts(T.Ineg[:, :], T.J[:, :], T.Pf[:, 0:1], ALU.is_equal, ["J", "Pf"], ["Ineg"], -1.0, ALU.mult)
-    cp(T.offA[:, 128:512], T.XI[:, :], ["XI0", "XI1", "XI2"], ["offA1"])
+        tt(T.XI[:, 128 * i:128 * i + 128], T.loA[:, :], T.V[:, 128 * i:128 * i + 128], ALU.add, ["loA", "V%d" % i], ["XI%d" % i], 256)
+    cp(T.offA[:, 128:512], T.XI[:, :], ["XI0", "XI1", "XI2"], ["offA1", "offA2", "offA3"], 384)
+
+    for r in range(16):
+        if SEL_ON[r] == "v":
+            ts(T.Sel[:, 256 * r:256 * r + 256], T.BD[:, :], T.M16[:, r:r + 1], ALU.mult, ["BD", "M16"], ["Sel%d" % r], 128)
+        else:
+            act(T.Sel[:, 256 * r:256 * r + 256], T.BD[:, :], ACT.Identity, ["BD", "M16"], ["Sel%d" % r], 256, scale=T.M16[:, r:r + 1])
+    ts(T.If[:, :], T.J[:, :], T.Pf[:, 0:1], ALU.is_equal, ["J", "Pf"], ["If"], 128)
+    for name, x in (("Ibf", 1.0), ("Ineg", -1.0)) + ((("Inf", -1.0),) if ON_PE else ()):
+        act(T[name][:, :], T.If[:, :], ACT.Identity, ["If"], [name], 128, scale=x)
+    for name, x in (("K0", 2 * KY), ("K1", -KY - 1), ("K2", 1 - KY)):
+        ts(T[name][:, :], T.Ibf[:, :], x, ALU.mult, ["Ibf"], [name], 64)
+    ts(T.onesA[:, :], T.Jt[:, 256:272], T.Pf[:, 2:3], ALU.is_equal, ["Jt2", "Pf"], ["onesA"], 16)
+
+    def more_constants():
+        ts(T.onesB[:, :], T.J[:, 0:8], T.Pf[:, 3:4], ALU.is_equal, ["J", "Pf"], ["onesB"], 8)
+        fill(T.nb16[32:64, :], MID, ["nbc"], 64)
+        fill(T.w16[32:64, :], MID, ["wc"], 64)
+        fill(T.Z[:, :], 0.0, ["Z0", "Z1"], 100)
+        fill(T.CH[:, 1, 0:96:3], 0.0, ["CHz"], 32)
+        fill(T.FC[:, 1, 0:64:2], 0.0, ["FCz"], 32)
+        fill(T.RW[:, 0, 3:128:4], WHOLE, ["RWc"], 32)
+        for i, x in ((0, 0.0), (2, UNDER), (3, 1.0)):
+            fill(T.D0[:, :, i:128:4], x, ["D0c%d" % i], 64)
+        for i in range(2):
+            fill(T["Q%d" % i][:, 2:5:2, 3:128:4], WHOLE, ["Q%dc" % i], 64)
+        fill(T.Q0[:, 0, 2:128:4], -MID, ["Q0l"], 32)
+        cp(T.V16[:, 384:512], T.tmpi[:, 0:128], ["tm0"], ["V163"], 128)
+        ts(T.nb16[0:32, :], T.n4[0:32, :], -MID, ALU.add, ["n40"], ["nb16"], 128)
 
     fused([(peer(d), small[d - 1], "lo_in", T.lost[:, 32 * (d - 1):32 * d], T.lold[:, 32 * (d - 1):32 * d])
-           for d in range(1, N)], ["lost"])
+           for d in range(1, N)], ["lost1", "lost2", "lost3"], ["@lo"], CROSS_LO)
     for d in range(1, N):
         s = 2 * (d - 1)
         a0, a1 = slice(s * PIECE, (s + 1) * PIECE), slice((s + 1) * PIECE, (s + 2) * PIECE)
         fused([(peer(d), far, "in%d" % s, T.stage[:, a0], T.land[:, a0]),
-               (hs[d - 1], near, "hin", T.stage[:, a1], T.stage[:, a1])], ["stage%d" % s, "stage%d" % (s + 1)])
+               (hs[d - 1], near, "hin", T.stage[:, a1], T.stage[:, a1])], ["stage%d" % s, "stage%d" % (s + 1)],
+              ["@in%d" % s, "@in%d" % (s + 1)], CROSS_BIG)
     for d in range(1, N):
         q0 = 32 * ((rank - d) % N)
-        dma("s", T.loB[q0:q0 + 32, :], T.lold[:, 32 * (d - 1):32 * d], after=[("lo_in", three)],
-            w=["loB"] if d == N - 1 else [], sem=("lorel", 16 * d))
+        dma("s", T.LB[q0:q0 + 32, 0:128], T.lold[:, 32 * (d - 1):32 * d], ["@lo"], ["loB%d" % d], [("lo_in", three)])
+    dma("s", T.tabB[r0:r0 + 32, :], T.walk[r0:r0 + 32, :], ["@lo"], ["tabB6"])
     for i, s in enumerate(RELAYOUT):
         q0, a = 32 * ((rank - 1 - s // 2) % N), s % 2
-        if i == 1:
-            dma("s", T.tabB[r0:r0 + 32, :], T.walk[r0:r0 + 32, :], w=["tabBown"])
         dma("s", T.tabB[q0:q0 + 32, a * HALF:(a + 1) * HALF], T.land[:, s * PIECE:(s + 1) * PIECE],
-            after=[("in%d" % s, len(far))], w=["tabB"] if i == 5 else [], sem=("relay", 16 * (i + 1)))
+            ["@in%d" % s], ["tabB%d" % s], [("in%d" % s, len(far))])
 
     def spread(s, lhs, rhs, rr, b):
         for r in range(8 * s, 8 * s + 8):
@@ -280,271 +369,225 @@ def rank_program(g, core, T, topo):
         return T.Sel[0:48, 256 * r + 128:256 * r + 256]
 
     def spreadA(k, s):
-        for i, name in enumerate(("nA", "mA", "wA")):
+        for j, (name, i) in enumerate((("nA", 0), ("wA", 2))):
             b, c0 = next_bank(), 1024 * k + 512 * s
-            spread(s, selA, T.V16[:, 128 * i + 64 * k:128 * i + 64 * k + 64], ["V16"], b)
-            if EVAC_A[3 * (2 * k + s) + i] == "a":
-                act(T[name][:, c0:c0 + 512], T[b][:, :], ACT.Identity, [b], [name + "%d%d" % (k, s)], bias=MID)
+            spread(s, selA, T.V16[:, 128 * i + 64 * k:128 * i + 64 * k + 64], ["V16%d" % i], b)
+            if EVAC_A[2 * (2 * k + s) + j] == "a":
+                act(T[name][:, c0:c0 + 512], T[b][:, :], ACT.Identity, [b], [name + "%d%d" % (k, s)], 512, bias=MID)
             else:
-                ts(T[name][:, c0:c0 + 512], T[b][:, :], MID, ALU.add, [b], [name + "%d%d" % (k, s)])
+                ts(T[name][:, c0:c0 + 512], T[b][:, :], MID, ALU.add, [b], [name + "%d%d" % (k, s)], 512)
 
     def spread_nB(k, s):
-        b, c0 = next_bank(), 1024 * k + 512 * s
+        b, c0 = "pd%d" % s, 1024 * k + 512 * s
         spread(s, selB, T.nb16[0:48, 64 * k:64 * k + 64], ["nb16", "nbc"], b)
-        cp(T.nB[:, c0:c0 + 512], T[b][:, :], [b], ["nB%d%d" % (k, s)], EVAC_B[2 * k + s])
+        cp(T.nB[:, c0:c0 + 512], T[b][:, :], [b], ["nB%d%d" % (k, s)], 512, EVAC_B[2 * k + s])
 
-    def more_constants():
-        ts(T.If[:, :], T.J[:, :], T.Pf[:, 0:1], ALU.is_equal, ["J", "Pf"], ["If"])
-        cp(T.n2f[0:16, :], T.n2i[0:16, :], ["n2i0", "n2i1"], ["n2f"])
-        ts(T.onesA[:, :], T.J[:, 0:8], T.Pf[:, 2:3], ALU.is_equal, ["J", "Pf"], ["onesA"])
-        ts(T.onesB[:, :], T.J[:, 0:8], T.Pf[:, 3:4], ALU.is_equal, ["J", "Pf"], ["onesB"])
-        ts(T.Rep[0:32, :], T.Jt[0:32, 256:384], T.Pf[0:32, 0:1], ALU.is_equal, ["Jt2", "Pf"], ["Rep0"])
-        ts(T.Rep[32:64, :], T.Jt[32:64, 384:512], T.Pf[32:64, 1:2], ALU.is_equal, ["Jt3", "Pf"], ["Rep1"])
-        ts(T.nb16[32:64, :], T.J[32:64, :], 0.0, ALU.mult, ["J"], ["nbc"], MID, ALU.add)
-        ts(T.w16[32:64, :], T.J[32:64, :], 0.0, ALU.mult, ["J"], ["wc"], MID, ALU.add)
-        ts(T.nb16[0:32, :], T.n32[0:32, :], -MID, ALU.add, ["n32"], ["nb16"])
-        op("v", lambda e: e.memset(T.Z[:, :], 0.0), w=["Z0", "Z1"])
-        op("v", lambda e: e.memset(T.Q0[:, 0, :], 0.0), w=["Q0l"])
-
-    def diff(b, s, x, rx, y, ry):
+    def combine(b, s, terms):
         for r in range(8 * s, 8 * s + 8):
             o = T[b][:, 64 * (r - 8 * s):64 * (r - 8 * s) + 64]
-            mm(o, T.Ibf[:, :], x[0][:, x[1] + r:x[1] + 1024:16], True, False, rx + ["Ibf"], [b])
-            mm(o, T.Ineg[:, :], y[0][:, y[1] + r:y[1] + 1024:16], False, True, ry + ["Ineg"], [b])
+            for i, (weight, x, c0, rx) in enumerate(terms):
+                mm(o, T[weight][:, :], x[:, c0 + r:c0 + 1024:16], i == 0, i == len(terms) - 1, rx + [weight], [b])
 
-    def sums(slot, s, col, ones, width, rones):
+    def sums(slot, s, out, ones, rones):
         for u in range(4 * s, 4 * s + 4):
             c0 = 512 * slot + 128 * (u - 4 * s)
-            mm(T.pg[:, col + u:col + 8 * width:8], T.Db[:, c0:c0 + 128], ones[:, 0:width], True, True,
-               ["D%d" % slot, rones], ["pg"])
+            mm(out(u), T.Db[:, c0:c0 + 128], ones, True, True, ["D%d" % slot, rones], ["pg"], 256)
 
-    def absD(slot):
-        act(T.Db[:, 512 * slot:512 * slot + 512], T.Db[:, 512 * slot:512 * slot + 512], ACT.Abs, ["D%d" % slot], ["D%d" % slot])
-
-    def gm(k):
-        return T.sm[:, 16 * k:16 * k + 16]
+    W_, LOW = T.Z[:, 4:192:6], T.Z[:, 2:192:6]
 
     def after_probe():
         Q, qn = T["Q%d" % cur[0]], "Q%d" % cur[0]
-        gp, hh, c2, w_ = T.gp, T.hh, T.c2, T.Z[:, 1:65:2]
-        return [
-            lambda: tt(Q[:, 2, :], Q[:, 3, :], w_, ALU.min, [qn + "m", "Z0", "Z1"], [qn + "p"]),
-            lambda: tt(Q[:, 4, :], Q[:, 3, :], w_, ALU.max, [qn + "m", "Z0", "Z1"], [qn + "q"]),
-            lambda: tt(T.sm[:, 96:128], w_, Q[:, 3, :], ALU.is_gt, [qn + "m", "Z0", "Z1"], ["rt"]),
-            lambda: tt(gp[:, :, :], Q[:, 2:7:2, :], Q[:, 0:5:2, :], ALU.subtract, [qn + c for c in "lpqr"], ["gp"]),
-            lambda: ts(hh[:, :, :], gp[:, :, :], 1, ALU.arith_shift_right, ["gp"], ["hh"]),
-            lambda: tt(c2[:, 0:2, :], gp[:, 1:3, :], gp[:, 0:2, :], ALU.is_gt, ["gp"], ["ca"]),
-            lambda: tt(c2[:, 2:4, :], Q[:, 2:5:2, :], hh[:, 1:3, :], ALU.add, [qn + "p", qn + "q", "hh"], ["cb"]),
-            lambda: tt(c2[:, 4:6, :], Q[:, 2:5:2, :], hh[:, 0:2, :], ALU.subtract, [qn + "p", qn + "q", "hh"], ["cc"]),
-            lambda: tt(c2[:, 0:2, :], c2[:, 0:2, :], c2[:, 2:4, :], ALU.mult, ["ca", "cb"], ["ca"]),
-            lambda: tt(c2[:, 6:8, :], c2[:, 0:2, :], c2[:, 4:6, :], ALU.max, ["ca", "cc"], ["w2"]),
-        ]
+        m = Q[:, 3, 2:128:4]
+        tt(Q[:, 2, 2:128:4], m, W_, ALU.min, [qn + "m", "Z0", "Z1"], [qn + "p"], 64)
+        tt(Q[:, 4, 2:128:4], m, W_, ALU.max, [qn + "m", "Z0", "Z1"], [qn + "q"], 64)
+        tt(T.CH[:, 0, 1:96:3], W_, m, ALU.is_le, [qn + "m", "Z0", "Z1"], ["left"], 64)
+        act(T.CH[:, 1, 1:96:3], T.CH[:, 0, 1:96:3], ACT.Identity, ["left"], ["sgn"], 32, scale=-2.0, bias=1.0)
+        tt(Q[:, 2:7:2, 1:128:4], Q[:, 0:5:2, 2:128:4], Q[:, 2:7:2, 2:128:4], ALU.subtract, [qn + c for c in "lpqr"], [qn + "g"], 192)
+        tt(T.D0[:, :, 1:128:4], Q[:, 4:7:2, 2:128:4], Q[:, 0:3:2, 2:128:4], ALU.subtract, [qn + c for c in "lpqr"], ["span"], 128)
+        tt(Q[:, 2:5:2, 0:128:4], Q[:, 4:7:2, 1:128:4], Q[:, 2:5:2, 1:128:4], ALU.is_lt, [qn + "g"], [qn + "s"], 128)
+        need = [qn + c for c in "pqgsc"] + ["span", "D0c0", "D0c2", "D0c3"]
+        if SPLIT_SCAN:
+            for i in range(2):
+                scan(T.RW[:, 1 + i, :], T.D0[:, i, :], Q[:, 2 + 2 * i, :], need, ["RW%d" % i], 128)
+        else:
+            scan(T.RW[:, 1:3, :], T.D0[:, :, :], Q[:, 2:5:2, :], need, ["RW0", "RW1"], 256)
+        tt(T.CH[:, :, 2:96:3], T.RW[:, 1:3, 3:128:4], T.RW[:, 0:2, 3:128:4], ALU.subtract, ["RW0", "RW1", "RWc"], ["W2"], 128)
 
-    def new_bracket():
+    def new_bracket(last):
         Q, qn = T["Q%d" % cur[0]], "Q%d" % cur[0]
         cur[0] ^= 1
         P, pn = T["Q%d" % cur[0]], "Q%d" % cur[0]
-        st = [lambda i=i: tt(T.t3[:, i, :], T.sm[:, 64:96], Q[:, 2 + 2 * i, :], ALU.mult, ["low0", "low1", qn + "pqr"[i]], ["t%d" % i])
-              for i in range(3)]
-        st += [lambda: tt(P[:, 0:7:3, :], T.t3[:, :, :], Q[:, 0:5:2, :], ALU.max,
-                          ["t0", "t1", "t2", qn + "l", qn + "p", qn + "q"], [pn + "l", pn + "m", pn + "r"])]
-        return st + after_probe()
-
-    def choose(k, gw_, rg, last):
-        Q, qn, c2, a = T["Q%d" % cur[0]], "Q%d" % cur[0], T.c2, slice(16 * k, 16 * k + 16)
-        up, low, rt, tw = (T.sm[:, c + 16 * k:c + 16 + 16 * k] for c in (32, 64, 96, 128))
-        f0 = 128 * k + r0
-        chain = [lambda: tt(up, gw_, gm(k), ALU.is_gt, rg + ["gm%d" % k], ["up%d" % k]),
-                 lambda: tt(low, up, rt, ALU.is_equal, ["up%d" % k, "rt"], ["low%d" % k])]
+        for i in ((1,) if last else (0, 1, 2)):
+            tt(T.t3[:, i, :], LOW, Q[:, 2 + 2 * i, 1:128:4], ALU.mult, ["Z0", "Z1", qn + "g"], ["t%d" % i], 64)
         if last:
-            chain[1:1] = [lambda: tt(T.fl[:, f0 + 1:f0 + 32:2], gw_, gm(k), ALU.max, rg + ["gm%d" % k], ["flg%d" % k])]
-            return chain + [lambda: tt(tw, low, Q[:, 4, a], ALU.mult, ["low%d" % k, qn + "q"], ["tw%d" % k]),
-                            lambda: tt(T.fl[:, f0:f0 + 32:2], tw, Q[:, 2, a], ALU.max, ["tw%d" % k, qn + "p"], ["flm%d" % k]),
-                            lambda: finish(k)], []
-        chain += [lambda: tt(tw, low, c2[:, 7, a], ALU.mult, ["low%d" % k, "w2"], ["tw%d" % k]),
-                  lambda: (tt(T.Z[:, 32 * k + 1:32 * k + 33:2], tw, c2[:, 6, a], ALU.max, ["tw%d" % k, "w2"], ["Z%d" % k]), turn(k)),
-                  lambda: (centre(k), columns(T.w16, ["w16%d" % k, "wc"], 64 * k, 64)),
-                  lambda: (offsets(k), pick(k, 0)), lambda: wrep(k, 0), lambda: wrep(k, 1), lambda: pick(k, 1)]
-        rest = [lambda: tt(gm(k), gw_, gm(k), ALU.max, rg + ["gm%d" % k], ["gm%d" % k])]
-        return chain, rest + (new_bracket() if k == 1 else [])
+            tt(T.tm[:, :], Q[:, 2, 2:128:4], T.t3[:, 1, :], ALU.subtract, ["t1", qn + "p"], ["tm"], 64)
+            tt(T.FC[:, 1, 1:64:2], W_, T.tm[:, :], ALU.subtract, ["tm", "Z0", "Z1"], ["step"], 64)
+            act(T.FC[:, 0, 1:64:2], T.tm[:, :], ACT.Identity, ["tm"], ["mU"], 32, bias=MID)
+            return
+        tt(P[:, 0:7:3, 2:128:4], Q[:, 0:5:2, 2:128:4], T.t3[:, :, :], ALU.subtract,
+           ["t0", "t1", "t2", qn + "l", qn + "p", qn + "q"], [pn + "l", pn + "m", pn + "r"], 192)
+        after_probe()
 
-    def turn(k):
-        z = 32 * k
-        mm(T.px[0:32, 0:64], T.Z[:, z + 1:z + 33], T.If[:, 0:64], True, False, ["Z%d" % k, "If"], ["px"])
-        mm(T.px[0:32, 0:64], T.Z[:, z:z + 32], T.If[:, 64:128], False, True, ["Z%d" % k, "If"], ["px"])
+    def choose(k, gw_, rg, c):
+        a = slice(48 * k, 48 * k + 48)
+        ahead[0] = AHEAD
+        tt(T.CH[:, 0, 48 * k:48 * k + 48:3], gw_, T.gm[:, now[0], 16 * k:16 * k + 16], ALU.is_gt, rg + ["gm%d%d" % (now[0], k)], ["up%d" % k], c)
+        scan(T.Z[:, 96 * k:96 * k + 96:2], T.CH[:, 1, a], T.CH[:, 0, a], ["up%d" % k, "left", "sgn", "W2", "CHz"], ["Z%d" % k], 48)
+        c0, z = 64 * k, 96 * k
+        mm(T.px[:, 0:64], T.Ibf[:, :], T.lohi[:, c0:c0 + 64], True, False, ["Ibf", "lohi"], ["px"])
+        mm(T.px[:, 0:64], T.Ibf[:, :], T.lolo[:, c0:c0 + 64], False, False, ["Ibf", "lolo"], ["px"])
+        for q in range(N):
+            mm(T.px[32 * q:32 * q + 32, 0:64], T.Z[:, z + 4:z + 100:3], T.Ibf[:, 0:64], False, False, ["Z%d" % k, "Ibf"], ["px"])
+            mm(T.px[32 * q:32 * q + 32, 0:64], T.Z[:, z + 1:z + 97:3], T.Ibf[:, 64:128], False, True, ["Z%d" % k, "Ibf"], ["px"])
+        cp(T.offw[:, c0:c0 + 64], T.px[:, 0:64], ["px"], ["offw%d" % k], 64)
+        tt(T.w16[0:32, c0:c0 + 64], T.px[0:32, 0:64], T.lo2[0:32, c0:c0 + 64], ALU.subtract, ["px", "lo2"], ["w16%d" % k], 64)
+        for part in range(2):
+            c1 = c0 + 32 * part
+            cp(T.gw[:, 16 * c1:16 * c1 + 512], T.tabB[:, 0:W].indirect(T.offw[:, c1:c1 + 32]),
+               TABB + ["offw%d" % k], ["gw%d%d" % (k, part)], 512 * PICK, "a")
+        for s in range(2):
+            spread(s, selB, T.w16[0:48, c0:c0 + 64], ["w16%d" % k, "wc"], "pw%d" % (2 * k + s))
+        ahead[0] = 0
 
-    def centre(k):
-        ts(T.w16[0:32, 64 * k:64 * k + 64], T.px[0:32, 0:64], -MID, ALU.add, ["px"], ["w16%d" % k])
+    def best(gw_, rg, c):
+        old, new = now[0], 1 - now[0]
+        tt(T.gm[:, new, :], gw_, T.gm[:, old, :], ALU.max, rg + ["gm%d0" % old, "gm%d1" % old], ["gm%d0" % new, "gm%d1" % new], c)
+        now[0] = new
 
-    def columns(src, rs, c0, n):
-        o = T.px[:, 128:128 + n]
-        mm(o, T.Ibf[:, :], T.lohi[:, c0:c0 + n], True, False, ["Ibf", "lohi"], ["px"])
-        mm(o, T.Ibf[:, :], T.lolo[:, c0:c0 + n], False, False, ["Ibf", "lolo"], ["px"])
-        mm(o, T.Rep[0:48, :], src[0:48, c0:c0 + n], False, True, rs + ["Rep0", "Rep1"], ["px"])
-
-    def offsets(k):
-        cp(T.offw[:, 64 * k:64 * k + 64], T.px[:, 128:192], ["px"], ["offw%d" % k])
-
-    def wrep(k, s):
-        spread(s, selB, T.w16[0:48, 64 * k:64 * k + 64], ["w16%d" % k, "wc"], "pw%d" % (2 * k + s))
-
-    def pick(k, part):
-        c0 = 64 * k + 32 * part
-        cp(T.gw[:, 16 * c0:16 * c0 + 512], T.tabB[:, 0:W].indirect(T.offw[:, c0:c0 + 32]),
-           ["tabB", "tabBown", "offw%d" % k], ["gw%d%d" % (k, part)], "a")
-
-    def dS(k, s):
-        diff("pd%d" % s, s, (T.gw, 1024 * k), ["gw%d0" % k, "gw%d1" % k], (T.g0B, 1024 * k), ["g0B%d" % k])
-
-    def opB(k, s):
-        b, c0 = "pw%d" % (2 * k + s), 1024 * k + 512 * s
-        tt(T[b][:, :], T[b][:, :], T.riseB[:, c0:c0 + 512], ALU.mult, [b, "rB%d%d" % (k, s)], [b])
-
-    def opA(k, s):
-        c0 = 1024 * k + 512 * s
-        tt(T.Ab[:, 512 * s:512 * s + 512], T["pd%d" % s][:, :], T.nB[:, c0:c0 + 512], ALU.mult,
-           ["pd%d" % s, "nB%d%d" % (k, s)], ["A%d" % s])
-
-    def opD(k, s):
-        b, slot = "pw%d" % (2 * k + s), 2 * k + s
-        tt(T.Db[:, 512 * slot:512 * slot + 512], T.Ab[:, 512 * s:512 * s + 512], T[b][:, :], ALU.subtract, ["A%d" % s, b], ["D%d" % slot])
-
-    def sumB(k, s):
-        sums(2 * k + s, s, 256 + 16 * k, T.onesB, 2, "onesB")
+    def gain(k):
+        for s in range(2):
+            b, pd, slot, c0 = "pw%d" % (2 * k + s), "pd%d" % s, 2 * k + s, 1024 * k + 512 * s
+            A, D = T.Ab[:, 512 * s:512 * s + 512], T.Db[:, 512 * slot:512 * slot + 512]
+            tt(T[b][:, :], T[b][:, :], T.riseB[:, c0:c0 + 512], ALU.mult, [b, "rB%d%d" % (k, s)], [b], 512)
+            combine(pd, s, [("Ibf", T.gw, 1024 * k, ["gw%d0" % k, "gw%d1" % k]), ("Ineg", T.g0B, 1024 * k, ["g0B%d" % k])])
+            tt(A, T[pd][:, :], T.nB[:, c0:c0 + 512], ALU.mult, [pd, "nB%d%d" % (k, s)], ["A%d" % s], 512)
+            if slot in ON_PE:
+                mm(T[b][:, :], T.Inf[:, :], A, False, True, ["Inf", "A%d" % s], [b], 2048)
+                act(D, T[b][:, :], ACT.Abs, [b], ["D%d" % slot], 512)
+            else:
+                tt(D, A, T[b][:, :], ALU.subtract, ["A%d" % s, b], ["D%d" % slot], 512)
+                act(D, D, ACT.Abs, ["D%d" % slot], ["D%d" % slot], 512)
+            sums(slot, s, lambda u: T.pg[:, 16 + k, u:16:8], T.onesB[:, 0:2], "onesB")
 
     def start_state():
-        n = T.nTi
-        for k in range(2):
-            mm(T.px[:, 256 + 16 * k:272 + 16 * k], T.n2f[0:16, 128 * k:128 * k + 128], T.If[0:16, 0:16], True, True, ["n2f", "If"], ["px"])
-        cp(n[:, 0:32], T.px[:, 256:288], ["px"], ["n0"])
-        ts(n[:, 32:64], n[:, 0:32], 1, ALU.arith_shift_right, ["n0"], ["n1"])
-        ts(n[:, 64:96], n[:, 0:32], 2, ALU.arith_shift_right, ["n0"], ["n2"])
-        ts(n[:, 96:128], n[:, 0:32], 1, ALU.bitwise_and, ["n0"], ["n3"])
-        tt(n[:, 64:96], n[:, 32:64], n[:, 64:96], ALU.subtract, ["n1", "n2"], ["n2"])
-        tt(n[:, 96:128], n[:, 32:64], n[:, 96:128], ALU.mult, ["n1", "n3"], ["n3"])
-        cp(T.Q0[:, 6, :], n[:, 0:32], ["n0"], ["Q0r"])
-        cp(T.Q0[:, 3, :], n[:, 32:64], ["n1"], ["Q0m"])
-        tt(T.Z[:, 1:65:2], n[:, 64:96], n[:, 96:128], ALU.add, ["n2", "n3"], ["Z0", "Z1"])
-        run(after_probe())
+        for j, i in enumerate((1, 0, 2, 3)):
+            for k in range(2):
+                for rr in range(2):
+                    c0 = 128 + 32 * j + 16 * k
+                    mm(T.px[64 * rr:64 * rr + 64, c0:c0 + 16], T.V16[:, 128 * i + 64 * k:128 * i + 64 * k + 64],
+                       T.Ibf[:, r0 + rr:r0 + 32:2], True, True, ["V16%d" % i, "Ibf"], ["px"])
+        cp(T.Q0[:, 3:7:3, 2:128:4], T.px[:, 128:192], ["px"], ["Q0m", "Q0r"], 64)
+        cp(W_, T.px[:, 192:224], ["px"], ["Z0", "Z1"], 32)
+        act(T.CO[:, :, 0:8], T.px[:, 224:256], ACT.Identity, ["px"], ["co"], 32, scale=0.5)
+        act(T.tm[:, :], T.px[:, 224:256], ACT.Identity, ["px"], ["tm"], 32, scale=(1 - KY) / 2, bias=MID)
+        tt(T.CO[:, :, 8:16], T.px[:, 128:160], T.tm[:, :], ALU.add, ["px", "tm"], ["cm"], 32)
+        after_probe()
 
     def pickA(k, i):
         cp(T.gA[:, 2048 * i + 1024 * k:2048 * i + 1024 * k + 1024],
            T.tabA[:, 0:W].indirect(T.offA[:, 128 * i + 64 * k:128 * i + 64 * k + 64]),
-           ["tabA", "offA0" if i == 0 else "offA1"], ["gA%d%d" % (i, k)], PICK_A[4 * k + i])
+           ["tabA", "offA%d" % i], ["gA%d%d" % (i, k)], 1024 * PICK, PICK_A[4 * k + i])
 
     def evalA(k, s):
-        b, c0 = next_bank(), 1024 * k + 512 * s
-        diff(b, s, (T.gA, 2048 + 1024 * k), ["gA1%d" % k], (T.gA, 1024 * k), ["gA0%d" % k])
-        for ev in range(2):
-            diff("pd%d" % ev, s, (T.gA, 2048 * (2 + ev) + 1024 * k), ["gA%d%d" % (2 + ev, k)], (T.gA, 1024 * k), ["gA0%d" % k])
-        for ev in range(2):
-            name, pd = ("mA", "wA")[ev], "pd%d" % ev
-            tt(T.Ab[:, 512 * ev:512 * ev + 512], T[b][:, :], T[name][:, c0:c0 + 512], ALU.mult, [b, name + "%d%d" % (k, s)], ["A%d" % ev])
-            tt(T[pd][:, :], T[pd][:, :], T.nA[:, c0:c0 + 512], ALU.mult, [pd, "nA%d%d" % (k, s)], [pd])
-        for ev in range(2):
-            pd, slot = "pd%d" % ev, 2 * s + ev
-            tt(T.Db[:, 512 * slot:512 * slot + 512], T[pd][:, :], T.Ab[:, 512 * ev:512 * ev + 512], ALU.subtract, [pd, "A%d" % ev], ["D%d" % slot])
-            absD(slot)
-
-    def sumA(k, s):
-        for ev in range(2):
-            sums(2 * s + ev, s, 128 * k + 64 * ev, T.onesA, 8, "onesA")
+        def term(weight, i):
+            return weight, T.gA, 2048 * i + 1024 * k, ["gA%d%d" % (i, k)]
+        bz, br, bx, c0 = next_bank(), next_bank(), next_bank(), 1024 * k + 512 * s
+        A, ones = T.Ab[:, 512 * s:512 * s + 512], T.onesA[:, (2 * rank + 2) % 8:(2 * rank + 2) % 8 + 8]
+        D = [T.Db[:, 512 * (2 * s + ev):512 * (2 * s + ev) + 512] for ev in range(2)]
+        combine(br, s, [term("Ibf", 1), term("Ineg", 0)])
+        tt(A, T[br][:, :], T.wA[:, c0:c0 + 512], ALU.mult, [br, "wA%d%d" % (k, s)], ["A%d" % s], 512)
+        combine(bz, s, [term("K0", 2), term("K1", 0), term("K2", 1)])
+        act(D[1], T[bz][:, :], ACT.Abs, [bz], ["D%d" % (2 * s + 1)], 512)
+        sums(2 * s + 1, s, lambda u: T.pg[:, 8 * k:8 * k + 8, 8 + u], ones, "onesA")
+        combine(bx, s, [term("Ibf", 3), term("Ineg", 0)])
+        tt(T[bx][:, :], T[bx][:, :], T.nA[:, c0:c0 + 512], ALU.mult, [bx, "nA%d%d" % (k, s)], [bx], 512)
+        tt(D[0], T[bx][:, :], A, ALU.subtract, [bx, "A%d" % s], ["D%d" % (2 * s)], 512)
+        act(D[0], D[0], ACT.Abs, ["D%d" % (2 * s)], ["D%d" % (2 * s)], 512)
+        sums(2 * s, s, lambda u: T.pg[:, 8 * k:8 * k + 8, u], ones, "onesA")
 
     def send_parts(k):
-        ps = T["ps%d" % k]
-        for ev in range(2):
-            cp(ps[:, :, 16 * ev:16 * ev + 16], T.pg[:, 128 * k + 64 * ev:128 * k + 64 * ev + 64], ["pg"], ["ps%d%d" % (k, ev)])
-        fused([(peer(d), small[d - 1], "part%d" % k, ps[:, (rank + d) % N, :], T.pl[:, 96 * k + 32 * (d - 1):96 * k + 32 * d])
-               for d in range(1, N)], ["ps%d0" % k, "ps%d1" % k])
+        ts(T.X[:, k, 0:8, 16:24], T.pg[:, 8 * k:8 * k + 8, 8:16], 1 / KY, ALU.mult, ["pg"], ["Xy%d" % k], 64)
+        cp(T.X[:, k, 0:8, 0:16], T.pg[:, 8 * k:8 * k + 8, :], ["pg"], ["Xg%d" % k], 128)
+        fused([(peer(d), small[d - 1], "part%d" % k, T.X[:, k, 2 * d - 2:2 * d, :], T.X[:, k, 6 + 2 * d:8 + 2 * d, :])
+               for d in range(1, N)], ["Xy%d" % k, "Xg%d" % k], ["@part%d" % k, "@g"], CROSS)
 
     def add_parts(k):
-        ps, a = T["ps%d" % k], 96 * k
-        tt(T.g2[:, a:a + 32], ps[:, rank, :], T.pl[:, a:a + 32], ALU.add, ["ps%d0" % k, "ps%d1" % k], ["g2a%d" % k],
-           after=[("part%d" % k, three)])
-        tt(T.g2[:, a + 32:a + 64], T.pl[:, a + 32:a + 64], T.pl[:, a + 64:a + 96], ALU.add, [], ["g2b%d" % k])
-        tt(gm(k), T.g2[:, a:a + 16], T.g2[:, a + 32:a + 48], ALU.add, ["g2a%d" % k, "g2b%d" % k], ["gm%d" % k])
-        tt(T.g2[:, a + 64:a + 80], T.g2[:, a + 16:a + 32], T.g2[:, a + 48:a + 64], ALU.add, ["g2a%d" % k, "g2b%d" % k], ["g2c%d" % k])
+        a = slice(2 * k, 2 * k + 2)
+        tt(T.S2[:, 4 * k:4 * k + 4, :], T.X[:, k, 6:10, :], T.X[:, k, 10:14, :], ALU.add, ["Xy%d" % k, "Xg%d" % k, "@part%d" % k],
+           ["S2%d" % k], 192, after=[("part%d" % k, three)])
+        tt(T.S1[:, a, :], T.S2[:, 4 * k:4 * k + 2, :], T.S2[:, 4 * k + 2:4 * k + 4, :], ALU.add, ["S2%d" % k], ["S1%d" % k], 96)
+        tt(T.PR[:, a, :], T.S1[:, a, 8:24], T.CO[:, a, :], ALU.mult, ["S1%d" % k, "co", "cm"], ["PR%d" % k], 64)
+        tt(T.gm[:, 0, 16 * k:16 * k + 16], T.PR[:, a, 0:8], T.PR[:, a, 8:16], ALU.add, ["PR%d" % k], ["gm0%d" % k], 32)
 
     def lo_setup():
-        cp(T.lohi[:, :], T.loB[:, :], ["loB", "loBown"], ["lohi"])
-        cp(T.offB[:, 0:128], T.loB[:, :], ["loB", "loBown"], ["offB0"])
-        tt(T.lolo[:, :], T.loB[:, :], T.lohi[:, :], ALU.subtract, ["loB", "loBown", "lohi"], ["lolo"])
-        columns(T.nb16, ["nb16", "nbc"], 0, 128)
-        cp(T.offB[:, 128:256], T.px[:, 128:256], ["px"], ["offB1"])
+        tt(T.LB[:, 128:256], T.LB[:, 0:128], T.n4[:, :], ALU.add, LOB + N4, ["loE"], 256)
+        cp(T.offB[:, :], T.LB[:, :], LOB + ["loE"], ["offB"], 256)
+        ts(T.lo2[:, :], T.LB[:, 0:128], MID, ALU.add, LOB, ["lo2"], 128)
+        cp(T.lohi[:, :], T.lo2[:, :], ["lo2"], ["lohi"], 128, "a")
+        tt(T.lolo[:, :], T.lo2[:, :], T.lohi[:, :], ALU.subtract, ["lo2", "lohi"], ["lolo"], 256)
 
-    def endB(k, i):
-        name = ("g0B", "geB")[i]
-        cp(T[name][:, 1024 * k:1024 * k + 1024], T.tabB[:, 0:W].indirect(T.offB[:, 128 * i + 64 * k:128 * i + 64 * k + 64]),
-           ["tabB", "tabBown", "offB%d" % i], [name + "%d" % k], PICK_B[2 * k + i])
-
-    def riseB(k):
+    def endsB(k):
+        for i, name in enumerate(("g0B", "geB")):
+            cp(T[name][:, 1024 * k:1024 * k + 1024], T.tabB[:, 0:W].indirect(T.offB[:, 128 * i + 64 * k:128 * i + 64 * k + 64]),
+               TABB + ["offB"], [name + "%d" % k], 1024 * PICK, PICK_B[2 * k + i])
         for s in range(2):
-            b, c0 = "pd%d" % s, 1024 * k + 512 * s
-            diff(b, s, (T.geB, 1024 * k), ["geB%d" % k], (T.g0B, 1024 * k), ["g0B%d" % k])
-            cp(T.riseB[:, c0:c0 + 512], T[b][:, :], [b], ["rB%d%d" % (k, s)], RISE_B[2 * k + s])
+            b, c0 = "pw%d" % (2 * k + s), 1024 * k + 512 * s
+            combine(b, s, [("Ibf", T.geB, 1024 * k, ["geB%d" % k]), ("Ineg", T.g0B, 1024 * k, ["g0B%d" % k])])
+            cp(T.riseB[:, c0:c0 + 512], T[b][:, :], [b], ["rB%d%d" % (k, s)], 512, RISE_B[2 * k + s])
 
     def finish(k):
-        f0 = 128 * k + r0
+        f0, a, gw_, gm_ = 128 * k + r0, slice(32 * k, 32 * k + 32), T.pg[:, 16 + k, :], T.gm[:, now[0], 16 * k:16 * k + 16]
+        rg = ["pg", "gm%d%d" % (now[0], k)]
+        ahead[0] = AHEAD
+        tt(T.FC[:, 0, 32 * k:32 * k + 32:2], gw_, gm_, ALU.is_gt, rg, ["up%d" % k], 16)
+        scan(T.fl[:, f0:f0 + 32], T.FC[:, 1, a], T.FC[:, 0, a], ["up%d" % k, "step", "mU", "FCz"], ["fl%d" % k], 32)
+        tt(T.fl[:, f0:f0 + 32:2], gw_, gm_, ALU.max, rg, ["fl%d" % k], 16)
+        ahead[0] = 0
         sent[0] += len(far)
         one = RemoteDMATransfer(dst_ids=[dstid(peer(d)) for d in range(1, N)], dma_engine_mask=bits(far), remote_sem=T.sem["fin%d" % k],
                                 srcs=[T.fl[:, f0:f0 + 32]], dsts=[T.fl[:, f0:f0 + 32]] * (N - 1))
-        op("g", lambda e: e.remote_dma_fused([one], local_sem=T.sem.sent), ["flm%d" % k, "flg%d" % k], (), remote=True)
+        op("g", lambda e: e.remote_dma_fused([one], local_sem=T.sem.sent), ["fl%d" % k], ["@fin%d" % k, "@g"], remote=True, busy=600, done=CROSS)
 
     def store(k):
         b = "pw%d" % (2 * k)
         for o in range(2):
-            mm(T[b][0:64, 128 * o:128 * o + 128], T.fl[:, 128 * k + o:128 * k + 128:2], T.If[:, :], True, True,
-               ["flm%d" % k, "flg%d" % k, "If"], [b], after=[("fin%d" % k, len(far) * (N - 1))])
-        cp(T.fs[0:64, 256 * k:256 * k + 256], T[b][0:64, 0:256], [b], ["fs%d" % k])
-        return [dma("sa"[o], (T.ym, T.yg)[o][:, 64 * k:64 * k + 64], T.fs[0:64, 256 * k + 128 * o:256 * k + 128 * o + 128], r=["fs%d" % k])
+            mm(T[b][0:64, 128 * o:128 * o + 128], T.fl[:, 128 * k + 1 - o:128 * k + 128:2], T.If[:, :], True, True,
+               ["fl%d" % k, "If", "@fin%d" % k], [b], 512, after=[("fin%d" % k, len(far) * (N - 1))])
+        cp(T.fs[0:64, 256 * k:256 * k + 256], T[b][0:64, 0:256], [b], ["fs%d" % k], 256)
+        return [dma("sa"[o], (T.ym, T.yg)[o][:, 64 * k:64 * k + 64], T.fs[0:64, 256 * k + 128 * o:256 * k + 128 * o + 128], ["fs%d" % k])
                 for o in range(2)]
 
-    def early(k, ch):
-        (dS, opA, opB)[EARLY.index(ch) // 2](k, EARLY.index(ch) % 2)
-
-    first = []
-    todo = {"c": more_constants, "l": lo_setup, "i": start_state, "F": lambda: run(first[1]),
-            "f": lambda: (first.extend(choose(0, T.g2[:, 64:80], ["g2c0"], False)), run(first[0])),
-            "z": lambda: [early(0, ch) for ch in ORDER[0] if ch in EARLY]}
     for k in range(2):
-        todo["p%d" % k] = lambda k=k: send_parts(k)
-        todo["q%d" % k] = lambda k=k: add_parts(k)
-        todo["r%d" % k] = lambda k=k: riseB(k)
         for s in range(2):
-            todo["e%d%d" % (k, s)] = lambda k=k, s=s: endB(k, s)
-            todo["s%d%d" % (k, s)] = lambda k=k, s=s: spreadA(k, s)
-            todo["n%d%d" % (k, s)] = lambda k=k, s=s: spread_nB(k, s)
-            todo["a%d%d" % (k, s)] = lambda k=k, s=s: evalA(k, s)
-            todo["u%d%d" % (k, s)] = lambda k=k, s=s: sumA(k, s)
+            spreadA(k, s)
         for i in range(4):
-            todo["g%d%d" % (k, i)] = lambda k=k, i=i: pickA(k, i)
-    for name in OPENING.split():
-        todo[name]()
+            pickA(k, i)
+        for s in range(2):
+            evalA(k, s)
+        send_parts(k)
+    more_constants()
+    start_state()
+    lo_setup()
+    for k in range(2):
+        add_parts(k)
+        for s in range(2):
+            spread_nB(k, s)
+        endsB(k)
+        choose(k, T.S1[:, 2 * k:2 * k + 2, 0:8], ["S1%d" % k], 32)
 
-    steps = 2 * (ROUNDS - 1)
-    for t in range(1, steps + 1):
-        y, x = t % 2, 1 - t % 2
-        gw_, rg = (T.g2[:, 160:176], ["g2c1"]) if t == 1 else (T.pg[:, 256 + 16 * y:272 + 16 * y], ["pg"])
-        chain, rest = choose(y, gw_, rg, t == steps)
-        if t == steps - 1:
-            rest = rest[:8]
-        big = {"b": lambda: opB(x, 0), "B": lambda: opB(x, 1), "a": lambda: opA(x, 0), "A": lambda: opA(x, 1),
-               "d": lambda: opD(x, 0), "D": lambda: opD(x, 1), "v": lambda: absD(2 * x), "V": lambda: absD(2 * x + 1),
-               "s": lambda: sumB(x, 0), "S": lambda: sumB(x, 1), "e": lambda: dS(x, 0), "E": lambda: dS(x, 1)}
-        for ch in ORDER[y]:
-            if ch in EARLY:
-                if t < steps:
-                    early(y, ch)
-            elif ch == ".":
-                run(chain[:1])
-                chain = chain[1:]
-            elif ch == ",":
-                run(rest[:1])
-                rest = rest[1:]
-            else:
-                big[ch]()
-    y = 1 - steps % 2
-    run(choose(y, T.pg[:, 256 + 16 * y:272 + 16 * y], ["pg"], True)[0])
-    stored = store(1 - y) + store(y)
-    op("g", None, after=stored + [("sent", sent[0])])
+    best(T.S1[:, :, 0:8], ["S10", "S11"], 64)
+    new_bracket(False)
+    for t in range(2, ROUNDS):
+        for k in range(2):
+            gain(k)
+            choose(k, T.pg[:, 16 + k, :], ["pg"], 16)
+        best(T.pg[:, 16:18, :], ["pg"], 32)
+        new_bracket(t == ROUNDS - 1)
+    for k in range(2):
+        gain(k)
+        finish(k)
+    stored = store(0) + store(1)
+    ops = arrange(ops)
+    ops.append({"q": "g", "fn": None, "r": [], "w": [], "dma": None, "remote": False,
+                "after": [(k, v, {}, "x") for k, v in stored + [("sent", sent[0])]]})
     emit(g, T, ops)

@@ -14,38 +14,50 @@ F32, BF, F16, I32, U16 = "float32", "bfloat16", "float16", "int32", "uint16"
 
 SCRATCH = {name: ("sbuf", [128] + shape, kind) for names, shape, kind in (
     ("tabA tabB", [W], BF), ("stage land", [6 * PIECE], BF), ("lost lold", [96], I32),
-    ("loA n4 J", [128], I32), ("V XI tmpi", [384], I32), ("LB", [256], I32), ("V16", [512], F16), ("Jt", [384], I32),
-    ("offA", [512], U16), ("offB", [256], U16), ("offw", [128], U16), ("nb16 w16 K0 K1 K2", [128], F16),
-    ("lohi lolo Ibf Ineg", [128], BF), ("If Inf lo2", [128], F32), ("fl", [256], F32),
+    ("loA n4 J", [128], I32), ("V XI tmpi", [384], I32), ("LB", [256], I32), ("V16", [512], F16), ("Jt", [272], I32),
+    ("offA", [512], U16), ("offB", [256], U16), ("offw", [128], U16), ("w16 K0 K1 K2", [128], F16),
+    ("Ibf Ineg Ihalf Inh", [128], BF), ("If lo2", [128], F32), ("fl fs", [512], F32),
     ("Pi", [8], I32), ("Pf onesB", [8], F32), ("M16 onesA", [16], F32), ("BD", [256], BF), ("Sel", [4096], BF),
-    ("nA wA nB Db", [2048], F32), ("riseB g0B geB gw", [2048], BF), ("gA", [8192], BF), ("Ab", [1024], F32),
+    ("nA wA Db Ab", [2048], F32), ("nB", [16, 128], I32), ("riseB g0B geB gw", [2048], BF), ("gA", [8192], BF),
     ("X", [2, 14, 24], I32), ("S2", [8, 24], F32), ("S1", [4, 24], F32), ("CO PR", [4, 16], F32),
-    ("Q0 Q1", [7, 128], F32), ("D0", [2, 128], F32), ("RW", [3, 128], F32), ("CH", [2, 96], F32), ("FC", [2, 64], F32),
-    ("t3", [3, 32], F32), ("gm", [2, 32], F32), ("tm", [32], F32), ("Z", [200], F16), ("fs", [512], F32)) for name in names.split()}
+    ("Q0 Q1", [7, 32], F16), ("D0", [256], F32), ("RW", [384], F32), ("CH", [2, 96], F32), ("FC", [2, 64], F32),
+    ("gm", [2, 32], F32), ("tm", [32], F32), ("Z", [200], F16)) for name in names.split()}
+SCRATCH["n4d"] = ("dram", [128, 128], I32)
 PSUM = ("pd0", "pd1", "pw0", "pw1", "pw2", "pw3", "pg", "px")
 SCRATCH.update({name: ("psum", [128, 512], F32) for name in PSUM})
-SCRATCH["pg"] = ("psum", [128, 32, 16], F32)
-SEMAPHORES = (["cv", "ca", "cp", "cg", "sent", "hin", "lo_in", "part0", "part1", "fin0", "fin1"]
-              + ["in%d" % i for i in range(6)] + ["d%d" % i for i in range(40)])
+SEMAPHORES = (["cv", "ca", "cp", "cg", "sent", "on", "lo_in", "part0", "part1", "fin0", "fin1"]
+              + ["in%d" % i for i in range(6)] + ["d%d" % i for i in range(56)])
 CSEM = {"v": "cv", "a": "ca", "p": "cp", "g": "cg"}
 
-SEL_ON = "vvavvavavvavvava"
-EVAC_A = "aaaaaaaa"
-EVAC_B = "aaaa"
+EARLY = 2
+RELAYOUT = (0, 2, 1, 4, 3, 5)
+
+SEL_ON = "aaavaavaaavaaava"
+EVAC_A = "aavaaaaa"
 PICK_A = "avavavav"
-PICK_B = "vaaa"
-RISE_B = "aaaa"
-RELAYOUT = (0, 2, 4, 1, 3, 5)
-ON_PE = ()
-SPLIT_SCAN = True
+PICK_B = "vaav"
+RISE_B = "aava"
+
+ROUND = {
+    "v": "A0 A1 D0 D1 B3 <next A2 <both up0 D2 w0 A3 row0 D3 off0 >B0 >B1 up1 best w1 low row1 lmr off1 pq >B2",
+    "a": "abs0 abs1 abs2 abs3 pick0 pick1 pick2 pick3 side gaps left",
+    "p": "x0 x1 <gaps <rep3 x2 x3 sum0 sum1 lo0 w0 rep0 rep1 sum2 sum3 lo1 w1 rep2",
+}
+PHASE = {(q, x.lstrip("<>")): i / len(ROUND[q].split()) + {"<": 1, ">": -1}.get(x[0], 0)
+         for q in ROUND for i, x in enumerate(ROUND[q].split())}
+STRICT = 2
+LAST = "A0 A1 D0 B3 D1 A2 A3 D2 D3 up0 w0 up1 w1".split()
+OPENING = ("list sel eye n00 n01 g00 g01 g02 g03 r00 z00 x00 r01 z01 x01 send0 more state pq gaps side left next both "
+           "n10 n11 g10 g11 g12 g13 r10 z10 x10 r11 z11 x11 send1 lo add0 add1 up0 w0 lo0 off0 row0 e00 e01 pick0 pick1 "
+           "rise00 rise01 rep0 rep1 up1 best w1 lo1 off1 row1 e10 e11 pick2 pick3 rise10 rise11 rep2 rep3 low lmr").split()
+AGAIN = ("pq", "gaps", "side", "left", "next", "both")
 
 CYC, PE_CYC, FIX, WAKE, PICK = 0.83, 0.42, {"v": 50, "a": 65, "g": 130}, 90, 1.5
-AHEAD = 100
 LOAD = 2000
 LOAD_BIG = 5000
 CROSS = 3000
-CROSS_LO = 13000
-CROSS_BIG = 16000
+CROSS_LO = 9000
+CROSS_BIG = 14000
 
 
 def bits(engines):
@@ -59,33 +71,44 @@ def helpers_of(core, topo):
     return [c for c in topo.cores_of(core) if topo.die(c) != topo.die(core)]
 
 
-def arrange(ops):
-    writer, readers, deps = {}, {}, []
+def needs(ops, skip=""):
+    writer, readers, turn, deps = {}, {}, {}, []
     for i, op in enumerate(ops):
-        d = set()
-        for r in op["r"]:
-            if r in writer:
-                d.add(writer[r])
-            if r in PSUM:
-                d.update(j for j in readers.get(r, []) if ops[j]["q"] != op["q"])
-        for r in op["w"]:
-            if r in writer:
-                d.add(writer[r])
+        rs, ws = [r for r in op["r"] if r[0] not in skip], [r for r in op["w"] if r[0] not in skip]
+        d = {writer[r] for r in rs + ws if r in writer}
+        for r in ws:
             d.update(readers.get(r, []))
+        for b in {r.split(":")[0] for r in rs + ws} & set(PSUM):
+            q, mine, before = turn.get(b, (op["q"], [], []))
+            if q != op["q"]:
+                mine, before = [], mine
+            d.update(before + mine[-1:] * (op["q"] == "p"))
+            turn[b] = op["q"], mine + [i], before
         d.discard(i)
         deps.append(d)
-        for r in op["r"]:
+        for r in rs:
             readers.setdefault(r, []).append(i)
-        for r in op["w"]:
+        for r in ws:
             writer[r] = i
             readers[r] = []
+    return deps
+
+
+def arrange(ops):
+    deps = needs(ops)
+    follow = {}
+    for q in ROUND:
+        line = sorted((op["rank"], i) for i, op in enumerate(ops) if op["q"] == q and op["kind"] and op["rank"] >= STRICT)
+        follow.update({b[1]: a[1] for a, b in zip(line, line[1:]) if a[1] not in deps[b[1]]})
+    for i, j in follow.items():
+        deps[i].add(j)
     users = [[] for op in ops]
     for i, d in enumerate(deps):
         for j in d:
             users[j].append(i)
 
     def gap(j, i):
-        if ops[j]["q"] == ops[i]["q"] and (ops[i]["q"] == "p" or "#" + ops[i]["q"] in ops[i]["w"]):
+        if follow.get(i) == j or ops[j]["q"] == ops[i]["q"] and ops[i]["q"] in "psg":
             return ops[j]["busy"]
         return ops[j]["done"] + WAKE
 
@@ -99,13 +122,12 @@ def arrange(ops):
     order = []
     while len(order) < len(ops):
         t, q = min((max(free[q], min(ready[i] for i in pool[q])), q) for q in pool if pool[q])
-        i = min(i for i in pool[q] if ready[i] <= t + ops[i]["ahead"])
+        i = min((ops[i]["rank"], i) for i in pool[q] if ready[i] <= t)[1]
         pool[q].remove(i)
-        start = max(t, ready[i])
-        free[q] = start + ops[i]["busy"]
+        free[q] = t + ops[i]["busy"]
         order.append(i)
         for u in users[i]:
-            ready[u] = max(ready[u], start + gap(i, u))
+            ready[u] = max(ready[u], t + gap(i, u))
             left[u] -= 1
             if not left[u]:
                 pool[ops[u]["q"]].append(u)
@@ -116,20 +138,10 @@ def emit(g, T, ops):
     queue = {"v": g.vector, "a": g.scalar, "p": g.tensor, "g": g, "s": g.sync}
     know = {q: {} for q in queue}
     seq = {q: 0 for q in queue}
-    writer, readers, needed, plan = {}, {}, set(), []
-    for op in ops:
+    needed, plan = set(), []
+    for op, before in zip(ops, needs(ops, "@#")):
         q = op["q"]
-        op = dict(op, r=[r for r in op["r"] if r[0] not in "@#"], w=[r for r in op["w"] if r[0] not in "@#"])
-        deps = list(op["after"])
-        for r in op["r"]:
-            if r in writer:
-                deps.append(writer[r])
-            if r in PSUM:
-                deps += [t for t in readers.get(r, []) if t[3] != q]
-        for r in op["w"]:
-            if r in writer:
-                deps.append(writer[r])
-            deps += readers.get(r, [])
+        deps = list(op["after"]) + [plan[j][2] for j in sorted(before) if plan[j][2]]
         best = {}
         for t in deps:
             if t[3] == "p" and q == "p":
@@ -151,12 +163,6 @@ def emit(g, T, ops):
         else:
             seq[q] += 1
             tok = (q, seq[q], dict(know[q]), q)
-        if tok:
-            for r in op["r"]:
-                readers.setdefault(r, []).append(tok)
-            for r in op["w"]:
-                writer[r] = tok
-                readers[r] = []
         plan.append((op, waits, tok))
     count = {}
     for q in CSEM:
@@ -191,7 +197,7 @@ def hand_on(g, core, T, topo):
             out = topo.engines(core, dst)
             s = 2 * (d - 1) + 1
             rid, pid = topo.addr(dst, core)
-            g.wait_ge(T.sem.hin, len(near))
+            g.wait_ge(T.sem.on, len(near))
             g.remote_dma(T.land[:, s * PIECE:(s + 1) * PIECE], T.stage[:, s * PIECE:(s + 1) * PIECE],
                          T.sem["in%d" % s], T.sem.sent, pid, rid, bits(out))
             g.wait_ge(T.sem.sent, len(out))
@@ -203,13 +209,24 @@ def rank_program(g, core, T, topo):
         hand_on(g, core, T, topo)
         return
 
-    ops, ndma, sent, bank, cur, now, ahead = [], [0], [0], [0], [0], [0], [0]
+    ops, ndma, sent, bank, cur, now, at = [], [0], [0], [0], [0], [0], [0, None]
 
     def op(q, fn, r, w, cycles=0, after=(), dma=None, remote=False, busy=None, done=None):
         if busy is None:
             busy = cycles * PE_CYC if q == "p" else FIX[q] + cycles * CYC
-        ops.append({"q": q, "fn": fn, "r": list(r), "w": list(w) + ["#" + q] * (q in "sg"), "dma": dma, "remote": remote, "busy": busy,
-                    "done": done or busy, "ahead": ahead[0], "after": [(k, v, {}, "x") for k, v in after]})
+        ops.append({"q": q, "fn": fn, "r": list(r), "w": list(w) + ["#" + q] * (q in "sg"), "dma": dma, "remote": remote,
+                    "busy": busy, "done": done or busy, "after": [(k, v, {}, "x") for k, v in after],
+                    "kind": at[1], "turn": at[0], "rank": place(q)})
+
+    def step(name):
+        at[1] = name
+
+    def place(q):
+        if at[0] < STRICT and at[1] in OPENING and not (at[0] and at[1] in AGAIN):
+            return (STRICT - 0.1) * OPENING.index(at[1]) / len(OPENING)
+        if at[0] == ROUNDS and q == "v" and at[1] in LAST:
+            return ROUNDS + LAST.index(at[1]) / len(LAST)
+        return at[0] + PHASE.get((q, at[1]), 0)
 
     def dma(q, out, in_, r=(), w=(), after=(), done=LOAD):
         sem = "d%d" % ndma[0]
@@ -234,6 +251,9 @@ def rank_program(g, core, T, topo):
 
     def fill(out, x, w, c):
         op("v", lambda e: e.memset(out, x), [], w, c)
+
+    def count(out, pattern, per_row, w, c):
+        op("g", lambda e: e.iota(out, pattern, 0, per_row), [], w, 2 * c)
 
     def scan(out, d0, d1, r, w, c):
         op("v", lambda e: e.tensor_tensor_scan(out, d0, d1, 0.0, ALU.mult, ALU.add), r, w, c)
@@ -273,31 +293,35 @@ def rank_program(g, core, T, topo):
     TABB = ["tabB%d" % i for i in range(7)]
     LOB = ["loB%d" % i for i in range(N)]
     N4 = ["n4%d" % i for i in range(N)]
+    NB = ["nB%d" % i for i in range(16)]
 
     dma("a", T.V[:, 0:128], T.span[:, :], w=["V0"])
     dma("a", T.loA[:, :], T.lo[:, :], w=["loA"])
     for d in range(1, N):
         q0 = 32 * ((rank + d) % N)
         dma("s", T.lost[:, 32 * (d - 1):32 * d], T.lo[q0:q0 + 32, :], w=["lost%d" % d])
-    dma("s", T.tabA[:, :], T.walk[:, :], w=["tabA"], done=LOAD_BIG)
     for s in range(6):
         q0, a = 32 * ((rank + 1 + s // 2) % N), s % 2
+        if s == EARLY:
+            dma("s", T.tabA[:, :], T.walk[:, :], w=["tabA"], done=LOAD_BIG)
         dma("s", T.stage[:, s * PIECE:(s + 1) * PIECE], T.walk[q0:q0 + 32, a * HALF:(a + 1) * HALF], w=["stage%d" % s])
     dma("s", T.LB[r0:r0 + 32, 0:128], T.lo[r0:r0 + 32, :], w=["loB0"])
     for q in range(N):
         dma("s", T.n4[32 * q:32 * q + 32, :], T.span[r0:r0 + 32, :], w=["n4%d" % q])
+        dma("s", T.n4d[32 * q:32 * q + 32, :], T.span[r0:r0 + 32, :], w=["n4d%d" % q])
 
-    op("g", lambda e: e.iota(T.J[:, :], [[1, 128]], 0, 0), [], ["J"], 256)
-    op("g", lambda e: e.iota(T.Pi[:, 0:1], [[1, 1]], 0, 1), [], ["Pi0"], 2)
-    ts(T.Jt[:, 0:128], T.J[:, :], 4, ALU.arith_shift_right, ["J"], ["Jt0"], 128)
-    ts(T.Jt[:, 128:256], T.J[:, :], 4, ALU.arith_shift_right, ["J"], ["Jt1"], 128, 1, ALU.bitwise_and)
-    ts(T.Jt[:, 256:272], T.J[:, 0:16], 7, ALU.bitwise_and, ["J"], ["Jt2"], 16)
+    step("list")
+    count(T.Pi[:, 0:1], [[1, 1]], 1, ["Pi0"], 1)
+    count(T.Jt[:, 0:128], [[1, 8], [0, 16]], 0, ["Jt0"], 128)
+    count(T.Jt[:, 128:256], [[0, 4], [1, 2], [0, 16]], 0, ["Jt1"], 128)
+    count(T.J[:, :], [[1, 128]], 0, ["J"], 128)
+    count(T.Jt[:, 256:272], [[0, 2], [1, 8]], 0, ["Jt2"], 16)
     ts(T.Pi[:, 1:2], T.Pi[:, 0:1], 15, ALU.bitwise_and, ["Pi0"], ["Pi1"], 1)
     ts(T.Pi[:, 2:3], T.Pi[:, 0:1], 4, ALU.arith_shift_right, ["Pi0"], ["Pi2"], 1)
     ts(T.Pi[:, 3:4], T.Pi[:, 0:1], 4, ALU.arith_shift_right, ["Pi0"], ["Pi3"], 1, 1, ALU.bitwise_and)
     cp(T.Pf[:, 0:4], T.Pi[:, 0:4], ["Pi0", "Pi1", "Pi2", "Pi3"], ["Pf"], 4)
-    ts(T.M16[:, :], T.J[:, 0:16], T.Pf[:, 1:2], ALU.is_equal, ["J", "Pf"], ["M16"], 16)
     ts(T.BD[:, 0:256], T.Jt[:, 0:256], T.Pf[:, 2:3], ALU.is_equal, ["Jt0", "Jt1", "Pf"], ["BD"], 256)
+    ts(T.M16[:, :], T.J[:, 0:16], T.Pf[:, 1:2], ALU.is_equal, ["J", "Pf"], ["M16"], 16)
     fill(T.BD[32:64, 128:256], 1.0, ["BD"], 64)
 
     ts(T.V[:, 128:256], T.V[:, 0:128], 1, ALU.arith_shift_right, ["V0"], ["V1"], 128)
@@ -305,58 +329,65 @@ def rank_program(g, core, T, topo):
     ts(T.tmpi[:, 128:256], T.V[:, 0:128], 2, ALU.arith_shift_right, ["V0"], ["tm1"], 128)
     tt(T.tmpi[:, 256:384], T.tmpi[:, 0:128], T.V[:, 128:256], ALU.mult, ["tm0", "V1"], ["tm2"], 256)
     tt(T.tmpi[:, 128:256], T.V[:, 128:256], T.tmpi[:, 128:256], ALU.subtract, ["V1", "tm1"], ["tm1"], 256)
-    ts(T.V16[:, 0:128], T.V[:, 0:128], -MID, ALU.add, ["V0"], ["V160"], 128)
-    tt(T.V[:, 256:384], T.tmpi[:, 128:256], T.tmpi[:, 256:384], ALU.add, ["tm1", "tm2"], ["V2"], 256)
     cp(T.offA[:, 0:128], T.loA[:, :], ["loA"], ["offA0"], 128)
-    ts(T.V16[:, 128:384], T.V[:, 128:384], -MID, ALU.add, ["V1", "V2"], ["V161", "V162"], 256)
+    tt(T.V[:, 256:384], T.tmpi[:, 128:256], T.tmpi[:, 256:384], ALU.add, ["tm1", "tm2"], ["V2"], 256)
     for i in range(3):
         tt(T.XI[:, 128 * i:128 * i + 128], T.loA[:, :], T.V[:, 128 * i:128 * i + 128], ALU.add, ["loA", "V%d" % i], ["XI%d" % i], 256)
+        if i == 0:
+            ts(T.V16[:, 0:384], T.V[:, :], -MID, ALU.add, ["V0", "V1", "V2"], ["V160", "V161", "V162"], 384)
     cp(T.offA[:, 128:512], T.XI[:, :], ["XI0", "XI1", "XI2"], ["offA1", "offA2", "offA3"], 384)
 
+    step("sel")
     for r in range(16):
         if SEL_ON[r] == "v":
             ts(T.Sel[:, 256 * r:256 * r + 256], T.BD[:, :], T.M16[:, r:r + 1], ALU.mult, ["BD", "M16"], ["Sel%d" % r], 128)
         else:
             act(T.Sel[:, 256 * r:256 * r + 256], T.BD[:, :], ACT.Identity, ["BD", "M16"], ["Sel%d" % r], 256, scale=T.M16[:, r:r + 1])
+    step("eye")
     ts(T.If[:, :], T.J[:, :], T.Pf[:, 0:1], ALU.is_equal, ["J", "Pf"], ["If"], 128)
-    for name, x in (("Ibf", 1.0), ("Ineg", -1.0)) + ((("Inf", -1.0),) if ON_PE else ()):
+    for name, x in (("Ibf", 1.0), ("Ineg", -1.0)):
         act(T[name][:, :], T.If[:, :], ACT.Identity, ["If"], [name], 128, scale=x)
     for name, x in (("K0", 2 * KY), ("K1", -KY - 1), ("K2", 1 - KY)):
         ts(T[name][:, :], T.Ibf[:, :], x, ALU.mult, ["Ibf"], [name], 64)
     ts(T.onesA[:, :], T.Jt[:, 256:272], T.Pf[:, 2:3], ALU.is_equal, ["Jt2", "Pf"], ["onesA"], 16)
 
     def more_constants():
+        step("more")
         ts(T.onesB[:, :], T.J[:, 0:8], T.Pf[:, 3:4], ALU.is_equal, ["J", "Pf"], ["onesB"], 8)
-        fill(T.nb16[32:64, :], MID, ["nbc"], 64)
         fill(T.w16[32:64, :], MID, ["wc"], 64)
         fill(T.Z[:, :], 0.0, ["Z0", "Z1"], 100)
         fill(T.CH[:, 1, 0:96:3], 0.0, ["CHz"], 32)
         fill(T.FC[:, 1, 0:64:2], 0.0, ["FCz"], 32)
-        fill(T.RW[:, 0, 3:128:4], WHOLE, ["RWc"], 32)
+        for k in range(2):
+            fill(T.fl[:, 256 * k + 2 * r0 + 3:256 * k + 2 * r0 + 64:4], 0.0, ["flz%d" % k], 16)
+        fill(T.RW[:, 3:128:4], WHOLE, ["RWc"], 32)
+        fill(T.px[:, 259:512:4], WHOLE, ["px:M"], 64)
+        for name, x in (("Ihalf", 0.5), ("Inh", -0.5)):
+            act(T[name][:, :], T.If[:, :], ACT.Identity, ["If"], [name], 128, scale=x)
         for i, x in ((0, 0.0), (2, UNDER), (3, 1.0)):
-            fill(T.D0[:, :, i:128:4], x, ["D0c%d" % i], 64)
-        for i in range(2):
-            fill(T["Q%d" % i][:, 2:5:2, 3:128:4], WHOLE, ["Q%dc" % i], 64)
-        fill(T.Q0[:, 0, 2:128:4], -MID, ["Q0l"], 32)
+            fill(T.D0[:, i:256:4], x, ["D0c%d" % i], 64)
+        fill(T.Q0[:, 0, :], -MID, ["Q0l"], 32)
         cp(T.V16[:, 384:512], T.tmpi[:, 0:128], ["tm0"], ["V163"], 128)
-        ts(T.nb16[0:32, :], T.n4[0:32, :], -MID, ALU.add, ["n40"], ["nb16"], 128)
 
+    step(None)
     fused([(peer(d), small[d - 1], "lo_in", T.lost[:, 32 * (d - 1):32 * d], T.lold[:, 32 * (d - 1):32 * d])
            for d in range(1, N)], ["lost1", "lost2", "lost3"], ["@lo"], CROSS_LO)
     for d in range(1, N):
         s = 2 * (d - 1)
         a0, a1 = slice(s * PIECE, (s + 1) * PIECE), slice((s + 1) * PIECE, (s + 2) * PIECE)
         fused([(peer(d), far, "in%d" % s, T.stage[:, a0], T.land[:, a0]),
-               (hs[d - 1], near, "hin", T.stage[:, a1], T.stage[:, a1])], ["stage%d" % s, "stage%d" % (s + 1)],
+               (hs[d - 1], near, "on", T.stage[:, a1], T.stage[:, a1])], ["stage%d" % s, "stage%d" % (s + 1)],
               ["@in%d" % s, "@in%d" % (s + 1)], CROSS_BIG)
     for d in range(1, N):
         q0 = 32 * ((rank - d) % N)
         dma("s", T.LB[q0:q0 + 32, 0:128], T.lold[:, 32 * (d - 1):32 * d], ["@lo"], ["loB%d" % d], [("lo_in", three)])
     dma("s", T.tabB[r0:r0 + 32, :], T.walk[r0:r0 + 32, :], ["@lo"], ["tabB6"])
-    for i, s in enumerate(RELAYOUT):
+    for s in RELAYOUT:
         q0, a = 32 * ((rank - 1 - s // 2) % N), s % 2
         dma("s", T.tabB[q0:q0 + 32, a * HALF:(a + 1) * HALF], T.land[:, s * PIECE:(s + 1) * PIECE],
             ["@in%d" % s], ["tabB%d" % s], [("in%d" % s, len(far))])
+    for i in range(16):
+        dma("s", T.nB[i:128:16, :, :], T.n4d[:, :], ["n4d%d" % q for q in range(N)], [NB[i]], done=2 * LOAD)
 
     def spread(s, lhs, rhs, rr, b):
         for r in range(8 * s, 8 * s + 8):
@@ -369,18 +400,14 @@ def rank_program(g, core, T, topo):
         return T.Sel[0:48, 256 * r + 128:256 * r + 256]
 
     def spreadA(k, s):
+        step("n%d%d" % (k, s))
         for j, (name, i) in enumerate((("nA", 0), ("wA", 2))):
-            b, c0 = next_bank(), 1024 * k + 512 * s
+            b, c0, key = next_bank(), 1024 * k + 512 * s, name + "%d%d" % (k, s)
             spread(s, selA, T.V16[:, 128 * i + 64 * k:128 * i + 64 * k + 64], ["V16%d" % i], b)
             if EVAC_A[2 * (2 * k + s) + j] == "a":
-                act(T[name][:, c0:c0 + 512], T[b][:, :], ACT.Identity, [b], [name + "%d%d" % (k, s)], 512, bias=MID)
+                act(T[name][:, c0:c0 + 512], T[b][:, :], ACT.Identity, [b], [key], 512, bias=MID)
             else:
-                ts(T[name][:, c0:c0 + 512], T[b][:, :], MID, ALU.add, [b], [name + "%d%d" % (k, s)], 512)
-
-    def spread_nB(k, s):
-        b, c0 = "pd%d" % s, 1024 * k + 512 * s
-        spread(s, selB, T.nb16[0:48, 64 * k:64 * k + 64], ["nb16", "nbc"], b)
-        cp(T.nB[:, c0:c0 + 512], T[b][:, :], [b], ["nB%d%d" % (k, s)], 512, EVAC_B[2 * k + s])
+                ts(T[name][:, c0:c0 + 512], T[b][:, :], MID, ALU.add, [b], [key], 512)
 
     def combine(b, s, terms):
         for r in range(8 * s, 8 * s + 8):
@@ -388,102 +415,137 @@ def rank_program(g, core, T, topo):
             for i, (weight, x, c0, rx) in enumerate(terms):
                 mm(o, T[weight][:, :], x[:, c0 + r:c0 + 1024:16], i == 0, i == len(terms) - 1, rx + [weight], [b])
 
-    def sums(slot, s, out, ones, rones):
+    def size(slot, b, a, names):
+        D = T.Db[:, 512 * slot:512 * slot + 512]
+        step(names[0])
+        tt(D, T[b][:, :], T.Ab[:, 512 * a:512 * a + 512], ALU.subtract, ["A%d" % a, b], ["D%d" % slot], 512)
+        step(names[1])
+        act(D, D, ACT.Abs, ["D%d" % slot], ["D%d" % slot], 512)
+
+    def sums(slot, s, out, ones, rones, part):
         for u in range(4 * s, 4 * s + 4):
             c0 = 512 * slot + 128 * (u - 4 * s)
-            mm(out(u), T.Db[:, c0:c0 + 128], ones, True, True, ["D%d" % slot, rones], ["pg"], 256)
+            mm(out(u), T.Db[:, c0:c0 + 128], ones, True, True, ["D%d" % slot, rones], [part], 256)
 
     W_, LOW = T.Z[:, 4:192:6], T.Z[:, 2:192:6]
+    ROW = {"l": 0, "p": 2, "q": 4}
+
+    def linear(out, terms, part):
+        Q, qn = T["Q%d" % cur[0]], "Q%d" % cur[0]
+        for i, (weight, rows) in enumerate(terms):
+            a, n = ROW[rows[0]], len(rows)
+            mm(out, T[weight][:, :], Q[:, a:a + 2 * n - 1:2, :], i == 0, i == len(terms) - 1,
+               [weight] + [qn + c for c in rows], [part], 32 * n)
 
     def after_probe():
         Q, qn = T["Q%d" % cur[0]], "Q%d" % cur[0]
-        m = Q[:, 3, 2:128:4]
-        tt(Q[:, 2, 2:128:4], m, W_, ALU.min, [qn + "m", "Z0", "Z1"], [qn + "p"], 64)
-        tt(Q[:, 4, 2:128:4], m, W_, ALU.max, [qn + "m", "Z0", "Z1"], [qn + "q"], 64)
-        tt(T.CH[:, 0, 1:96:3], W_, m, ALU.is_le, [qn + "m", "Z0", "Z1"], ["left"], 64)
-        act(T.CH[:, 1, 1:96:3], T.CH[:, 0, 1:96:3], ACT.Identity, ["left"], ["sgn"], 32, scale=-2.0, bias=1.0)
-        tt(Q[:, 2:7:2, 1:128:4], Q[:, 0:5:2, 2:128:4], Q[:, 2:7:2, 2:128:4], ALU.subtract, [qn + c for c in "lpqr"], [qn + "g"], 192)
-        tt(T.D0[:, :, 1:128:4], Q[:, 4:7:2, 2:128:4], Q[:, 0:3:2, 2:128:4], ALU.subtract, [qn + c for c in "lpqr"], ["span"], 128)
-        tt(Q[:, 2:5:2, 0:128:4], Q[:, 4:7:2, 1:128:4], Q[:, 2:5:2, 1:128:4], ALU.is_lt, [qn + "g"], [qn + "s"], 128)
-        need = [qn + c for c in "pqgsc"] + ["span", "D0c0", "D0c2", "D0c3"]
-        if SPLIT_SCAN:
-            for i in range(2):
-                scan(T.RW[:, 1 + i, :], T.D0[:, i, :], Q[:, 2 + 2 * i, :], need, ["RW%d" % i], 128)
-        else:
-            scan(T.RW[:, 1:3, :], T.D0[:, :, :], Q[:, 2:5:2, :], need, ["RW0", "RW1"], 256)
-        tt(T.CH[:, :, 2:96:3], T.RW[:, 1:3, 3:128:4], T.RW[:, 0:2, 3:128:4], ALU.subtract, ["RW0", "RW1", "RWc"], ["W2"], 128)
+        m = Q[:, 3, :]
+        step("pq")
+        tt(Q[:, 2, :], m, W_, ALU.min, [qn + "m", "Z0", "Z1"], [qn + "p"], 64)
+        tt(Q[:, 4, :], m, W_, ALU.max, [qn + "m", "Z0", "Z1"], [qn + "q"], 64)
+        step("gaps")
+        mm(T.px[:, 64:96], T.Ibf[:, :], W_, True, False, ["Ibf", "Z0", "Z1"], ["px:s"])
+        mm(T.px[:, 64:96], T.Ineg[:, :], m, False, True, ["Ineg", qn + "m"], ["px:s"])
+        linear(T.px[:, 257:512:4], [("Ihalf", "lp"), ("Ihalf", "qr"), ("Ineg", "pq")], "px:d")
+        linear(T.px[:, 192:256], [("Ihalf", "qr"), ("Inh", "lp")], "px:h")
+        linear(T.px[:, 258:512:4], [("Ibf", "pq")], "px:d")
+        linear(T.px[:, 96:192], [("Ibf", "lpq"), ("Ineg", "pqr")], "px:g")
+        act(T.px[:, 256:512:4], T.px[:, 257:512:4], ACT.Sign, ["px:d"], ["px:c"], 64, bias=-0.25)
+        act(T.D0[:, 1:256:4], T.px[:, 192:256], ACT.Identity, ["px:h"], ["span"], 64)
+        step("side")
+        act(T.CH[:, 1, 1:96:3], T.px[:, 64:96], ACT.Sign, ["px:s"], ["sgn"], 32, bias=-0.5)
+        step("left")
+        act(T.CH[:, 0, 1:96:3], T.CH[:, 1, 1:96:3], ACT.Identity, ["sgn"], ["left"], 32, scale=-0.5, bias=0.5)
+        step("next")
+        scan(T.RW[:, 128:384], T.D0[:, :], T.px[:, 256:512], ["px:d", "px:c", "px:M", "span", "D0c0", "D0c2", "D0c3"], ["RW"], 256)
+        step("both")
+        tt(T.CH[:, :, 2:96:3], T.RW[:, 131:384:4], T.RW[:, 3:256:4], ALU.subtract, ["RW", "RWc"], ["W2"], 128)
 
     def new_bracket(last):
         Q, qn = T["Q%d" % cur[0]], "Q%d" % cur[0]
         cur[0] ^= 1
         P, pn = T["Q%d" % cur[0]], "Q%d" % cur[0]
+        step("low")
         for i in ((1,) if last else (0, 1, 2)):
-            tt(T.t3[:, i, :], LOW, Q[:, 2 + 2 * i, 1:128:4], ALU.mult, ["Z0", "Z1", qn + "g"], ["t%d" % i], 64)
+            a = T.px[:, 96 + 32 * i:128 + 32 * i]
+            tt(a, a, LOW, ALU.mult, ["Z0", "Z1", "px:g"], ["px:t%d" % i], 32)
+        step("lmr")
         if last:
-            tt(T.tm[:, :], Q[:, 2, 2:128:4], T.t3[:, 1, :], ALU.subtract, ["t1", qn + "p"], ["tm"], 64)
+            tt(T.tm[:, :], Q[:, 2, :], T.px[:, 128:160], ALU.subtract, ["px:t1", qn + "p"], ["tm"], 32)
+            step("pq")
             tt(T.FC[:, 1, 1:64:2], W_, T.tm[:, :], ALU.subtract, ["tm", "Z0", "Z1"], ["step"], 64)
+            step("side")
             act(T.FC[:, 0, 1:64:2], T.tm[:, :], ACT.Identity, ["tm"], ["mU"], 32, bias=MID)
             return
-        tt(P[:, 0:7:3, 2:128:4], Q[:, 0:5:2, 2:128:4], T.t3[:, :, :], ALU.subtract,
-           ["t0", "t1", "t2", qn + "l", qn + "p", qn + "q"], [pn + "l", pn + "m", pn + "r"], 192)
+        tt(P[:, 0:7:3, :], Q[:, 0:5:2, :], T.px[:, 96:192], ALU.subtract,
+           ["px:t0", "px:t1", "px:t2", qn + "l", qn + "p", qn + "q"], [pn + "l", pn + "m", pn + "r"], 96)
         after_probe()
 
-    def choose(k, gw_, rg, c):
-        a = slice(48 * k, 48 * k + 48)
-        ahead[0] = AHEAD
+    def choose(k, gw_, rg, c, *both):
+        a, c0, z = slice(48 * k, 48 * k + 48), 64 * k, 96 * k
+        step("up%d" % k)
         tt(T.CH[:, 0, 48 * k:48 * k + 48:3], gw_, T.gm[:, now[0], 16 * k:16 * k + 16], ALU.is_gt, rg + ["gm%d%d" % (now[0], k)], ["up%d" % k], c)
-        scan(T.Z[:, 96 * k:96 * k + 96:2], T.CH[:, 1, a], T.CH[:, 0, a], ["up%d" % k, "left", "sgn", "W2", "CHz"], ["Z%d" % k], 48)
-        c0, z = 64 * k, 96 * k
-        mm(T.px[:, 0:64], T.Ibf[:, :], T.lohi[:, c0:c0 + 64], True, False, ["Ibf", "lohi"], ["px"])
-        mm(T.px[:, 0:64], T.Ibf[:, :], T.lolo[:, c0:c0 + 64], False, False, ["Ibf", "lolo"], ["px"])
+        if k == 1:
+            best(*both)
+        step("w%d" % k)
+        scan(T.Z[:, z:z + 96:2], T.CH[:, 1, a], T.CH[:, 0, a], ["up%d" % k, "left", "sgn", "W2", "CHz"], ["Z%d" % k], 48)
+        step("lo%d" % k)
+        mm(T.pg[:, 320:384], T.If[:, :], T.lo2[:, c0:c0 + 64], True, False, ["If", "lo2"], ["pg:w"], 256)
+        step("w%d" % k)
         for q in range(N):
-            mm(T.px[32 * q:32 * q + 32, 0:64], T.Z[:, z + 4:z + 100:3], T.Ibf[:, 0:64], False, False, ["Z%d" % k, "Ibf"], ["px"])
-            mm(T.px[32 * q:32 * q + 32, 0:64], T.Z[:, z + 1:z + 97:3], T.Ibf[:, 64:128], False, True, ["Z%d" % k, "Ibf"], ["px"])
-        cp(T.offw[:, c0:c0 + 64], T.px[:, 0:64], ["px"], ["offw%d" % k], 64)
-        tt(T.w16[0:32, c0:c0 + 64], T.px[0:32, 0:64], T.lo2[0:32, c0:c0 + 64], ALU.subtract, ["px", "lo2"], ["w16%d" % k], 64)
+            o = T.pg[32 * q:32 * q + 32, 320:384]
+            mm(o, T.Z[:, z + 4:z + 100:3], T.Ibf[:, 0:64], False, False, ["Z%d" % k, "Ibf"], ["pg:w"])
+            mm(o, T.Z[:, z + 1:z + 97:3], T.Ibf[:, 64:128], False, True, ["Z%d" % k, "Ibf"], ["pg:w"])
+        step("off%d" % k)
+        cp(T.offw[:, c0:c0 + 64], T.pg[:, 320:384], ["pg:w"], ["offw%d" % k], 64)
+        step("row%d" % k)
+        tt(T.w16[0:32, c0:c0 + 64], T.pg[0:32, 320:384], T.lo2[0:32, c0:c0 + 64], ALU.subtract, ["pg:w", "lo2"], ["w16%d" % k], 64)
         for part in range(2):
             c1 = c0 + 32 * part
+            step("pick%d" % (2 * k + part))
             cp(T.gw[:, 16 * c1:16 * c1 + 512], T.tabB[:, 0:W].indirect(T.offw[:, c1:c1 + 32]),
                TABB + ["offw%d" % k], ["gw%d%d" % (k, part)], 512 * PICK, "a")
         for s in range(2):
+            step("rep%d" % (2 * k + s))
             spread(s, selB, T.w16[0:48, c0:c0 + 64], ["w16%d" % k, "wc"], "pw%d" % (2 * k + s))
-        ahead[0] = 0
 
     def best(gw_, rg, c):
         old, new = now[0], 1 - now[0]
+        step("best")
         tt(T.gm[:, new, :], gw_, T.gm[:, old, :], ALU.max, rg + ["gm%d0" % old, "gm%d1" % old], ["gm%d0" % new, "gm%d1" % new], c)
         now[0] = new
 
     def gain(k):
         for s in range(2):
             b, pd, slot, c0 = "pw%d" % (2 * k + s), "pd%d" % s, 2 * k + s, 1024 * k + 512 * s
-            A, D = T.Ab[:, 512 * s:512 * s + 512], T.Db[:, 512 * slot:512 * slot + 512]
+            step("B%d" % slot)
             tt(T[b][:, :], T[b][:, :], T.riseB[:, c0:c0 + 512], ALU.mult, [b, "rB%d%d" % (k, s)], [b], 512)
+            step("x%d" % slot)
             combine(pd, s, [("Ibf", T.gw, 1024 * k, ["gw%d0" % k, "gw%d1" % k]), ("Ineg", T.g0B, 1024 * k, ["g0B%d" % k])])
-            tt(A, T[pd][:, :], T.nB[:, c0:c0 + 512], ALU.mult, [pd, "nB%d%d" % (k, s)], ["A%d" % s], 512)
-            if slot in ON_PE:
-                mm(T[b][:, :], T.Inf[:, :], A, False, True, ["Inf", "A%d" % s], [b], 2048)
-                act(D, T[b][:, :], ACT.Abs, [b], ["D%d" % slot], 512)
-            else:
-                tt(D, A, T[b][:, :], ALU.subtract, ["A%d" % s, b], ["D%d" % slot], 512)
-                act(D, D, ACT.Abs, ["D%d" % slot], ["D%d" % slot], 512)
-            sums(slot, s, lambda u: T.pg[:, 16 + k, u:16:8], T.onesB[:, 0:2], "onesB")
+            step("A%d" % slot)
+            tt(T.Ab[:, 512 * slot:512 * slot + 512], T[pd][:, :], T.nB[:, 8 * s:8 * s + 8, 64 * k:64 * k + 64], ALU.mult,
+               [pd] + NB, ["A%d" % slot], 512)
+            size(slot, b, slot, ("D%d" % slot, "abs%d" % slot))
+            step("sum%d" % slot)
+            sums(slot, s, lambda u: T.pg[:, 256 + 16 * k + u:272 + 16 * k:8], T.onesB[:, 0:2], "onesB", "pg:%d" % k)
 
     def start_state():
+        step("state")
         for j, i in enumerate((1, 0, 2, 3)):
             for k in range(2):
                 for rr in range(2):
                     c0 = 128 + 32 * j + 16 * k
                     mm(T.px[64 * rr:64 * rr + 64, c0:c0 + 16], T.V16[:, 128 * i + 64 * k:128 * i + 64 * k + 64],
                        T.Ibf[:, r0 + rr:r0 + 32:2], True, True, ["V16%d" % i, "Ibf"], ["px"])
-        cp(T.Q0[:, 3:7:3, 2:128:4], T.px[:, 128:192], ["px"], ["Q0m", "Q0r"], 64)
-        cp(W_, T.px[:, 192:224], ["px"], ["Z0", "Z1"], 32)
         act(T.CO[:, :, 0:8], T.px[:, 224:256], ACT.Identity, ["px"], ["co"], 32, scale=0.5)
         act(T.tm[:, :], T.px[:, 224:256], ACT.Identity, ["px"], ["tm"], 32, scale=(1 - KY) / 2, bias=MID)
+        cp(T.Q0[:, 3:7:3, :], T.px[:, 128:192], ["px"], ["Q0m", "Q0r"], 64)
+        cp(W_, T.px[:, 192:224], ["px"], ["Z0", "Z1"], 32)
         tt(T.CO[:, :, 8:16], T.px[:, 128:160], T.tm[:, :], ALU.add, ["px", "tm"], ["cm"], 32)
         after_probe()
 
     def pickA(k, i):
+        step("g%d%d" % (k, i))
         cp(T.gA[:, 2048 * i + 1024 * k:2048 * i + 1024 * k + 1024],
            T.tabA[:, 0:W].indirect(T.offA[:, 128 * i + 64 * k:128 * i + 64 * k + 64]),
            ["tabA", "offA%d" % i], ["gA%d%d" % (i, k)], 1024 * PICK, PICK_A[4 * k + i])
@@ -492,70 +554,77 @@ def rank_program(g, core, T, topo):
         def term(weight, i):
             return weight, T.gA, 2048 * i + 1024 * k, ["gA%d%d" % (i, k)]
         bz, br, bx, c0 = next_bank(), next_bank(), next_bank(), 1024 * k + 512 * s
-        A, ones = T.Ab[:, 512 * s:512 * s + 512], T.onesA[:, (2 * rank + 2) % 8:(2 * rank + 2) % 8 + 8]
-        D = [T.Db[:, 512 * (2 * s + ev):512 * (2 * s + ev) + 512] for ev in range(2)]
+        ones, a = T.onesA[:, (2 * rank + 2) % 8:(2 * rank + 2) % 8 + 8], 2 * k + s
+        step("r%d%d" % (k, s))
         combine(br, s, [term("Ibf", 1), term("Ineg", 0)])
-        tt(A, T[br][:, :], T.wA[:, c0:c0 + 512], ALU.mult, [br, "wA%d%d" % (k, s)], ["A%d" % s], 512)
+        tt(T.Ab[:, 512 * a:512 * a + 512], T[br][:, :], T.wA[:, c0:c0 + 512], ALU.mult, [br, "wA%d%d" % (k, s)], ["A%d" % a], 512)
+        step("z%d%d" % (k, s))
         combine(bz, s, [term("K0", 2), term("K1", 0), term("K2", 1)])
-        act(D[1], T[bz][:, :], ACT.Abs, [bz], ["D%d" % (2 * s + 1)], 512)
-        sums(2 * s + 1, s, lambda u: T.pg[:, 8 * k:8 * k + 8, 8 + u], ones, "onesA")
+        act(T.Db[:, 1024 * s + 512:1024 * s + 1024], T[bz][:, :], ACT.Abs, [bz], ["D%d" % (2 * s + 1)], 512)
+        sums(2 * s + 1, s, lambda u: T.pg[:, 128 * k + 64 + u:128 * k + 128:8], ones, "onesA", "pg:t")
+        step("x%d%d" % (k, s))
         combine(bx, s, [term("Ibf", 3), term("Ineg", 0)])
         tt(T[bx][:, :], T[bx][:, :], T.nA[:, c0:c0 + 512], ALU.mult, [bx, "nA%d%d" % (k, s)], [bx], 512)
-        tt(D[0], T[bx][:, :], A, ALU.subtract, [bx, "A%d" % s], ["D%d" % (2 * s)], 512)
-        act(D[0], D[0], ACT.Abs, ["D%d" % (2 * s)], ["D%d" % (2 * s)], 512)
-        sums(2 * s, s, lambda u: T.pg[:, 8 * k:8 * k + 8, u], ones, "onesA")
+        size(2 * s, bx, a, ["x%d%d" % (k, s)] * 2)
+        sums(2 * s, s, lambda u: T.pg[:, 128 * k + u:128 * k + 64:8], ones, "onesA", "pg:g")
 
     def send_parts(k):
-        ts(T.X[:, k, 0:8, 16:24], T.pg[:, 8 * k:8 * k + 8, 8:16], 1 / KY, ALU.mult, ["pg"], ["Xy%d" % k], 64)
-        cp(T.X[:, k, 0:8, 0:16], T.pg[:, 8 * k:8 * k + 8, :], ["pg"], ["Xg%d" % k], 128)
+        step("send%d" % k)
+        ts(T.X[:, k, 0:8, 16:24], T.pg[:, 128 * k + 64:128 * k + 128], 1 / KY, ALU.mult, ["pg:t"], ["Xy%d" % k], 64)
+        cp(T.X[:, k, 0:8, 8:16], T.pg[:, 128 * k + 64:128 * k + 128], ["pg:t"], ["Xt%d" % k], 64)
+        cp(T.X[:, k, 0:8, 0:8], T.pg[:, 128 * k:128 * k + 64], ["pg:g"], ["Xg%d" % k], 64)
         fused([(peer(d), small[d - 1], "part%d" % k, T.X[:, k, 2 * d - 2:2 * d, :], T.X[:, k, 6 + 2 * d:8 + 2 * d, :])
-               for d in range(1, N)], ["Xy%d" % k, "Xg%d" % k], ["@part%d" % k, "@g"], CROSS)
+               for d in range(1, N)], ["Xy%d" % k, "Xt%d" % k, "Xg%d" % k], ["@part%d" % k], CROSS)
 
     def add_parts(k):
+        step("add%d" % k)
         a = slice(2 * k, 2 * k + 2)
-        tt(T.S2[:, 4 * k:4 * k + 4, :], T.X[:, k, 6:10, :], T.X[:, k, 10:14, :], ALU.add, ["Xy%d" % k, "Xg%d" % k, "@part%d" % k],
-           ["S2%d" % k], 192, after=[("part%d" % k, three)])
+        tt(T.S2[:, 4 * k:4 * k + 4, :], T.X[:, k, 6:10, :], T.X[:, k, 10:14, :], ALU.add,
+           ["Xy%d" % k, "Xt%d" % k, "Xg%d" % k, "@part%d" % k], ["S2%d" % k], 192, after=[("part%d" % k, three)])
         tt(T.S1[:, a, :], T.S2[:, 4 * k:4 * k + 2, :], T.S2[:, 4 * k + 2:4 * k + 4, :], ALU.add, ["S2%d" % k], ["S1%d" % k], 96)
         tt(T.PR[:, a, :], T.S1[:, a, 8:24], T.CO[:, a, :], ALU.mult, ["S1%d" % k, "co", "cm"], ["PR%d" % k], 64)
         tt(T.gm[:, 0, 16 * k:16 * k + 16], T.PR[:, a, 0:8], T.PR[:, a, 8:16], ALU.add, ["PR%d" % k], ["gm0%d" % k], 32)
 
     def lo_setup():
+        step("lo")
         tt(T.LB[:, 128:256], T.LB[:, 0:128], T.n4[:, :], ALU.add, LOB + N4, ["loE"], 256)
-        cp(T.offB[:, :], T.LB[:, :], LOB + ["loE"], ["offB"], 256)
         ts(T.lo2[:, :], T.LB[:, 0:128], MID, ALU.add, LOB, ["lo2"], 128)
-        cp(T.lohi[:, :], T.lo2[:, :], ["lo2"], ["lohi"], 128, "a")
-        tt(T.lolo[:, :], T.lo2[:, :], T.lohi[:, :], ALU.subtract, ["lo2", "lohi"], ["lolo"], 256)
+        cp(T.offB[:, :], T.LB[:, :], LOB + ["loE"], ["offB"], 256)
 
     def endsB(k):
         for i, name in enumerate(("g0B", "geB")):
+            step("e%d%d" % (k, i))
             cp(T[name][:, 1024 * k:1024 * k + 1024], T.tabB[:, 0:W].indirect(T.offB[:, 128 * i + 64 * k:128 * i + 64 * k + 64]),
-               TABB + ["offB"], [name + "%d" % k], 1024 * PICK, PICK_B[2 * k + i])
+               TABB + ["offB", "Xg1"], [name + "%d" % k], 1024 * PICK, PICK_B[2 * k + i])
         for s in range(2):
             b, c0 = "pw%d" % (2 * k + s), 1024 * k + 512 * s
+            step("rise%d%d" % (k, s))
             combine(b, s, [("Ibf", T.geB, 1024 * k, ["geB%d" % k]), ("Ineg", T.g0B, 1024 * k, ["g0B%d" % k])])
             cp(T.riseB[:, c0:c0 + 512], T[b][:, :], [b], ["rB%d%d" % (k, s)], 512, RISE_B[2 * k + s])
 
     def finish(k):
-        f0, a, gw_, gm_ = 128 * k + r0, slice(32 * k, 32 * k + 32), T.pg[:, 16 + k, :], T.gm[:, now[0], 16 * k:16 * k + 16]
-        rg = ["pg", "gm%d%d" % (now[0], k)]
-        ahead[0] = AHEAD
+        f0, a = 256 * k + 2 * r0, slice(32 * k, 32 * k + 32)
+        gw_, gm_, rg = T.pg[:, 256 + 16 * k:272 + 16 * k], T.gm[:, now[0], 16 * k:16 * k + 16], ["pg:%d" % k, "gm%d%d" % (now[0], k)]
+        step("up%d" % k)
         tt(T.FC[:, 0, 32 * k:32 * k + 32:2], gw_, gm_, ALU.is_gt, rg, ["up%d" % k], 16)
-        scan(T.fl[:, f0:f0 + 32], T.FC[:, 1, a], T.FC[:, 0, a], ["up%d" % k, "step", "mU", "FCz"], ["fl%d" % k], 32)
-        tt(T.fl[:, f0:f0 + 32:2], gw_, gm_, ALU.max, rg, ["fl%d" % k], 16)
-        ahead[0] = 0
+        tt(T.fl[:, f0 + 1:f0 + 64:4], gw_, gm_, ALU.max, rg, ["fg%d" % k], 16)
+        step("w%d" % k)
+        scan(T.fl[:, f0:f0 + 64:2], T.FC[:, 1, a], T.FC[:, 0, a], ["up%d" % k, "step", "mU", "FCz"], ["fl%d" % k], 32)
         sent[0] += len(far)
         one = RemoteDMATransfer(dst_ids=[dstid(peer(d)) for d in range(1, N)], dma_engine_mask=bits(far), remote_sem=T.sem["fin%d" % k],
-                                srcs=[T.fl[:, f0:f0 + 32]], dsts=[T.fl[:, f0:f0 + 32]] * (N - 1))
-        op("g", lambda e: e.remote_dma_fused([one], local_sem=T.sem.sent), ["fl%d" % k], ["@fin%d" % k, "@g"], remote=True, busy=600, done=CROSS)
+                                srcs=[T.fl[:, f0:f0 + 64]], dsts=[T.fl[:, f0:f0 + 64]] * (N - 1))
+        op("g", lambda e: e.remote_dma_fused([one], local_sem=T.sem.sent), ["fl%d" % k, "fg%d" % k, "flz%d" % k], ["@fin%d" % k],
+           remote=True, busy=600, done=CROSS)
 
     def store(k):
-        b = "pw%d" % (2 * k)
+        done = []
         for o in range(2):
-            mm(T[b][0:64, 128 * o:128 * o + 128], T.fl[:, 128 * k + 1 - o:128 * k + 128:2], T.If[:, :], True, True,
-               ["fl%d" % k, "If", "@fin%d" % k], [b], 512, after=[("fin%d" % k, len(far) * (N - 1))])
-        cp(T.fs[0:64, 256 * k:256 * k + 256], T[b][0:64, 0:256], [b], ["fs%d" % k], 256)
-        return [dma("sa"[o], (T.ym, T.yg)[o][:, 64 * k:64 * k + 64], T.fs[0:64, 256 * k + 128 * o:256 * k + 128 * o + 128], ["fs%d" % k])
-                for o in range(2)]
+            b, out = "pw%d" % (2 * k + o), T.fs[0:64, 256 * k + 128 * o:256 * k + 128 * o + 128]
+            mm(T[b][0:64, 0:128], T.fl[:, 256 * k + 2 - o:256 * k + 256:4], T.If[:, :], True, True,
+               ["fl%d" % k, "fg%d" % k, "If", "@fin%d" % k], [b], 512, after=[("fin%d" % k, len(far) * (N - 1))])
+            cp(out, T[b][0:64, 0:128], [b], ["fs%d%d" % (k, o)], 128, "va"[o])
+            done.append(dma("sa"[o], (T.ym, T.yg)[o][:, 64 * k:64 * k + 64], out, ["fs%d%d" % (k, o)]))
+        return done
 
     for k in range(2):
         for s in range(2):
@@ -565,27 +634,30 @@ def rank_program(g, core, T, topo):
         for s in range(2):
             evalA(k, s)
         send_parts(k)
-    more_constants()
-    start_state()
+        if k == 0:
+            more_constants()
+            start_state()
     lo_setup()
     for k in range(2):
         add_parts(k)
-        for s in range(2):
-            spread_nB(k, s)
+    for k in range(2):
         endsB(k)
-        choose(k, T.S1[:, 2 * k:2 * k + 2, 0:8], ["S1%d" % k], 32)
 
-    best(T.S1[:, :, 0:8], ["S10", "S11"], 64)
+    at[0] = 1
+    for k in range(2):
+        choose(k, T.S1[:, 2 * k:2 * k + 2, 0:8], ["S1%d" % k], 32, T.S1[:, :, 0:8], ["S10", "S11"], 64)
     new_bracket(False)
     for t in range(2, ROUNDS):
+        at[0] = t
         for k in range(2):
             gain(k)
-            choose(k, T.pg[:, 16 + k, :], ["pg"], 16)
-        best(T.pg[:, 16:18, :], ["pg"], 32)
+            choose(k, T.pg[:, 256 + 16 * k:272 + 16 * k], ["pg:%d" % k], 16, T.pg[:, 256:288], ["pg:0", "pg:1"], 32)
         new_bracket(t == ROUNDS - 1)
+    at[0] = ROUNDS
     for k in range(2):
         gain(k)
         finish(k)
+    at[:] = ROUNDS + 2, None
     stored = store(0) + store(1)
     ops = arrange(ops)
     ops.append({"q": "g", "fn": None, "r": [], "w": [], "dma": None, "remote": False,

from concourse.bass import DstId, RemoteDMATransfer
from concourse.mybir import AluOpType, ActivationFunctionType

ALU = AluOpType
ACT = ActivationFunctionType
N, W, ROUNDS = 4, 6144, 7
HALF = W // 2
PIECE = HALF // 4
MID = 2048.0
KY = 2046.0
WHOLE = 12582912.0
UNDER = 0.4998
F32, BF, F16, I32, U16 = "float32", "bfloat16", "float16", "int32", "uint16"

SCRATCH = {name: ("sbuf", [128] + shape, kind) for names, shape, kind in (
    ("tabA tabB", [W], BF), ("stage land", [6 * PIECE], BF), ("lost lold", [96], I32),
    ("loA n4 J", [128], I32), ("V XI tmpi", [384], I32), ("LB", [256], I32), ("V16", [512], F16), ("Jt", [272], I32),
    ("offA", [512], U16), ("offB", [256], U16), ("offw", [128], U16), ("w16 K0 K1 K2", [128], F16),
    ("Ibf Ineg Ihalf Inh", [128], BF), ("If lo2", [128], F32), ("fl fs", [512], F32),
    ("Pi", [8], I32), ("Pf onesB", [8], F32), ("M16 onesA", [16], F32), ("BD", [256], BF), ("Sel", [4096], BF),
    ("nA wA Db Ab", [2048], F32), ("nB", [16, 128], I32), ("riseB g0B geB gw", [2048], BF), ("gA", [8192], BF),
    ("X", [2, 14, 24], I32), ("S2", [8, 24], F32), ("S1", [4, 24], F32), ("CO PR", [4, 16], F32),
    ("Q0 Q1", [7, 32], F16), ("D0", [256], F32), ("RW", [384], F32), ("CH", [2, 96], F32), ("FC", [2, 64], F32),
    ("gm", [2, 32], F32), ("tm", [32], F32), ("Z", [200], F16)) for name in names.split()}
SCRATCH["n4d"] = ("dram", [128, 128], I32)
PSUM = ("pd0", "pd1", "pw0", "pw1", "pw2", "pw3", "pg", "px")
SCRATCH.update({name: ("psum", [128, 512], F32) for name in PSUM})
SEMAPHORES = (["cv", "ca", "cp", "cg", "sent", "on", "lo_in", "part0", "part1", "fin0", "fin1"]
              + ["in%d" % i for i in range(6)] + ["d%d" % i for i in range(56)])
CSEM = {"v": "cv", "a": "ca", "p": "cp", "g": "cg"}

EARLY = 2
RELAYOUT = (0, 2, 1, 4, 3, 5)

SEL_ON = "aaavaavaaavaaava"
EVAC_A = "aavaaaaa"
PICK_A = "avavavav"
PICK_B = "vaav"
RISE_B = "aava"

ROUND = {
    "v": "A0 A1 D0 D1 B3 <next A2 <both up0 D2 w0 A3 row0 D3 off0 >B0 >B1 up1 best w1 low row1 lmr off1 pq >B2",
    "a": "abs0 abs1 abs2 abs3 pick0 pick1 pick2 pick3 side gaps left",
    "p": "x0 x1 <gaps <rep3 x2 x3 sum0 sum1 lo0 w0 rep0 rep1 sum2 sum3 lo1 w1 rep2",
}
PHASE = {(q, x.lstrip("<>")): i / len(ROUND[q].split()) + {"<": 1, ">": -1}.get(x[0], 0)
         for q in ROUND for i, x in enumerate(ROUND[q].split())}
STRICT = 2
LAST = "A0 A1 D0 B3 D1 A2 A3 D2 D3 up0 w0 up1 w1".split()
OPENING = ("list sel eye n00 n01 g00 g01 g02 g03 r00 z00 x00 r01 z01 x01 send0 more state pq gaps side left next both "
           "n10 n11 g10 g11 g12 g13 r10 z10 x10 r11 z11 x11 send1 lo add0 add1 up0 w0 lo0 off0 row0 e00 e01 pick0 pick1 "
           "rise00 rise01 rep0 rep1 up1 best w1 lo1 off1 row1 e10 e11 pick2 pick3 rise10 rise11 rep2 rep3 low lmr").split()
AGAIN = ("pq", "gaps", "side", "left", "next", "both")

CYC, PE_CYC, FIX, WAKE, PICK = 0.83, 0.42, {"v": 50, "a": 65, "g": 130}, 90, 1.5
LOAD = 2000
LOAD_BIG = 5000
CROSS = 3000
CROSS_LO = 9000
CROSS_BIG = 14000


def bits(engines):
    m = 0
    for e in engines:
        m |= 1 << e
    return m


def helpers_of(core, topo):
    return [c for c in topo.cores_of(core) if topo.die(c) != topo.die(core)]


def needs(ops, skip=""):
    writer, readers, turn, deps = {}, {}, {}, []
    for i, op in enumerate(ops):
        rs, ws = [r for r in op["r"] if r[0] not in skip], [r for r in op["w"] if r[0] not in skip]
        d = {writer[r] for r in rs + ws if r in writer}
        for r in ws:
            d.update(readers.get(r, []))
        for b in {r.split(":")[0] for r in rs + ws} & set(PSUM):
            q, mine, before = turn.get(b, (op["q"], [], []))
            if q != op["q"]:
                mine, before = [], mine
            d.update(before + mine[-1:] * (op["q"] == "p"))
            turn[b] = op["q"], mine + [i], before
        d.discard(i)
        deps.append(d)
        for r in rs:
            readers.setdefault(r, []).append(i)
        for r in ws:
            writer[r] = i
            readers[r] = []
    return deps


def arrange(ops):
    deps = needs(ops)
    follow = {}
    for q in ROUND:
        line = sorted((op["rank"], i) for i, op in enumerate(ops) if op["q"] == q and op["kind"] and op["rank"] >= STRICT)
        follow.update({b[1]: a[1] for a, b in zip(line, line[1:]) if a[1] not in deps[b[1]]})
    for i, j in follow.items():
        deps[i].add(j)
    users = [[] for op in ops]
    for i, d in enumerate(deps):
        for j in d:
            users[j].append(i)

    def gap(j, i):
        if follow.get(i) == j or ops[j]["q"] == ops[i]["q"] and ops[i]["q"] in "psg":
            return ops[j]["busy"]
        return ops[j]["done"] + WAKE

    left = [len(d) for d in deps]
    ready = [0.0] * len(ops)
    pool = {q: [] for q in "vapgs"}
    free = {q: 0.0 for q in pool}
    for i, op in enumerate(ops):
        if not left[i]:
            pool[op["q"]].append(i)
    order = []
    while len(order) < len(ops):
        t, q = min((max(free[q], min(ready[i] for i in pool[q])), q) for q in pool if pool[q])
        i = min((ops[i]["rank"], i) for i in pool[q] if ready[i] <= t)[1]
        pool[q].remove(i)
        free[q] = t + ops[i]["busy"]
        order.append(i)
        for u in users[i]:
            ready[u] = max(ready[u], t + gap(i, u))
            left[u] -= 1
            if not left[u]:
                pool[ops[u]["q"]].append(u)
    return [ops[i] for i in order]


def emit(g, T, ops):
    queue = {"v": g.vector, "a": g.scalar, "p": g.tensor, "g": g, "s": g.sync}
    know = {q: {} for q in queue}
    seq = {q: 0 for q in queue}
    needed, plan = set(), []
    for op, before in zip(ops, needs(ops, "@#")):
        q = op["q"]
        deps = list(op["after"]) + [plan[j][2] for j in sorted(before) if plan[j][2]]
        best = {}
        for t in deps:
            if t[3] == "p" and q == "p":
                continue
            if t[1] > know[q].get(t[0], 0) and t[1] > best.get(t[0], (0, 0))[1]:
                best[t[0]] = t
        waits = []
        for t in sorted(best.values(), key=lambda t: -len(t[2])):
            if t[1] > know[q].get(t[0], 0):
                waits.append((t[0], t[1]))
                for k, v in list(t[2].items()) + [(t[0], t[1])]:
                    know[q][k] = max(know[q].get(k, 0), v)
                if t[0] in CSEM:
                    needed.add((t[0], t[1]))
        if op["dma"]:
            tok = (op["dma"], 16, dict(know[q]), "dma")
        elif op["fn"] is None or op["remote"]:
            tok = None
        else:
            seq[q] += 1
            tok = (q, seq[q], dict(know[q]), q)
        plan.append((op, waits, tok))
    count = {}
    for q in CSEM:
        c = 0
        for s in range(1, seq[q] + 1):
            if (q, s) in needed:
                c += 1
                count[(q, s)] = c
    for op, waits, tok in plan:
        e = queue[op["q"]]
        for k, v in waits:
            if k in CSEM:
                e.wait_ge(T.sem[CSEM[k]], count[(k, v)])
            else:
                e.wait_ge(T.sem[k], v)
        if op["fn"] is None:
            continue
        ins = op["fn"](e)
        if op["dma"]:
            ins.then_inc(T.sem[op["dma"]], 16)
        elif tok and (tok[0], tok[1]) in needed:
            ins.then_inc(T.sem[CSEM[tok[0]]], 1)


def hand_on(g, core, T, topo):
    for src in T.cores:
        hs = helpers_of(src, topo)[:N - 1]
        if core in hs:
            d = hs.index(core) + 1
            dst = T.cores[(T.rank_of(src) + d) % N]
            near = [e for e in topo.engines(src, core) if e not in topo.engines(src, dst)]
            out = topo.engines(core, dst)
            s = 2 * (d - 1) + 1
            rid, pid = topo.addr(dst, core)
            g.wait_ge(T.sem.on, len(near))
            g.remote_dma(T.land[:, s * PIECE:(s + 1) * PIECE], T.stage[:, s * PIECE:(s + 1) * PIECE],
                         T.sem["in%d" % s], T.sem.sent, pid, rid, bits(out))
            g.wait_ge(T.sem.sent, len(out))


def rank_program(g, core, T, topo):
    rank = T.rank_of(core)
    if rank is None:
        hand_on(g, core, T, topo)
        return

    ops, ndma, sent, bank, cur, now, at = [], [0], [0], [0], [0], [0], [0, None]

    def op(q, fn, r, w, cycles=0, after=(), dma=None, remote=False, busy=None, done=None):
        if busy is None:
            busy = cycles * PE_CYC if q == "p" else FIX[q] + cycles * CYC
        ops.append({"q": q, "fn": fn, "r": list(r), "w": list(w) + ["#" + q] * (q in "sg"), "dma": dma, "remote": remote,
                    "busy": busy, "done": done or busy, "after": [(k, v, {}, "x") for k, v in after],
                    "kind": at[1], "turn": at[0], "rank": place(q)})

    def step(name):
        at[1] = name

    def place(q):
        if at[0] < STRICT and at[1] in OPENING and not (at[0] and at[1] in AGAIN):
            return (STRICT - 0.1) * OPENING.index(at[1]) / len(OPENING)
        if at[0] == ROUNDS and q == "v" and at[1] in LAST:
            return ROUNDS + LAST.index(at[1]) / len(LAST)
        return at[0] + PHASE.get((q, at[1]), 0)

    def dma(q, out, in_, r=(), w=(), after=(), done=LOAD):
        sem = "d%d" % ndma[0]
        ndma[0] += 1
        op(q, lambda e: e.dma_start(out, in_), r, w, after=after, dma=sem, busy=60, done=done)
        return sem, 16

    def tt(out, a, b, alu, r, w, c, after=()):
        op("v", lambda e: e.tensor_tensor(out, a, b, alu), r, w, c, after)

    def ts(out, a, s1, o1, r, w, c, s2=None, o2=None):
        if o2 is None:
            op("v", lambda e: e.tensor_scalar(out, a, s1, None, o1), r, w, c)
        else:
            op("v", lambda e: e.tensor_scalar(out, a, s1, s2, o1, o2), r, w, c)

    def cp(out, a, r, w, c, q="v"):
        if q == "v":
            op("v", lambda e: e.tensor_copy(out, a), r, w, c)
        else:
            act(out, a, ACT.Copy, r, w, c)

    def fill(out, x, w, c):
        op("v", lambda e: e.memset(out, x), [], w, c)

    def count(out, pattern, per_row, w, c):
        op("g", lambda e: e.iota(out, pattern, 0, per_row), [], w, 2 * c)

    def scan(out, d0, d1, r, w, c):
        op("v", lambda e: e.tensor_tensor_scan(out, d0, d1, 0.0, ALU.mult, ALU.add), r, w, c)

    def act(out, a, func, r, w, c, **kw):
        op("a", lambda e: e.activation(out, a, func, **kw), r, w, c)

    def mm(out, lhsT, rhs, start, stop, r, w, c=64, after=()):
        op("p", lambda e: e.matmul(out, lhsT, rhs, start, stop), r, w, c, after)

    def peer(d):
        return T.cores[(rank + d) % N]

    def dstid(c):
        rid, pid = topo.addr(c, core)
        return DstId(rid=rid, pnc=pid)

    def fused(transfers, r, w, done):
        sent[0] += sum(len(t[1]) for t in transfers)
        lst = [RemoteDMATransfer(dst_ids=[dstid(c)], dma_engine_mask=bits(en), remote_sem=T.sem[sem], src=src, dst=dst)
               for c, en, sem, src, dst in transfers]
        op("g", lambda e: e.remote_dma_fused(lst, local_sem=T.sem.sent), r, w, remote=True, busy=600, done=done)

    def next_bank():
        bank[0] += 1
        return PSUM[bank[0] % 6]

    far = topo.engines(core, peer(1))
    share = 1
    while 2 * share * (N - 1) <= len(far):
        share *= 2
    small = [far[i * share:(i + 1) * share] for i in range(N - 1)]
    three = share * (N - 1)
    hs = helpers_of(core, topo)
    near = [e for e in topo.engines(core, hs[0]) if e not in far]
    r0 = 32 * rank
    TABB = ["tabB%d" % i for i in range(7)]
    LOB = ["loB%d" % i for i in range(N)]
    N4 = ["n4%d" % i for i in range(N)]
    NB = ["nB%d" % i for i in range(16)]

    dma("a", T.V[:, 0:128], T.span[:, :], w=["V0"])
    dma("a", T.loA[:, :], T.lo[:, :], w=["loA"])
    for d in range(1, N):
        q0 = 32 * ((rank + d) % N)
        dma("s", T.lost[:, 32 * (d - 1):32 * d], T.lo[q0:q0 + 32, :], w=["lost%d" % d])
    for s in range(6):
        q0, a = 32 * ((rank + 1 + s // 2) % N), s % 2
        if s == EARLY:
            dma("s", T.tabA[:, :], T.walk[:, :], w=["tabA"], done=LOAD_BIG)
        dma("s", T.stage[:, s * PIECE:(s + 1) * PIECE], T.walk[q0:q0 + 32, a * HALF:(a + 1) * HALF], w=["stage%d" % s])
    dma("s", T.LB[r0:r0 + 32, 0:128], T.lo[r0:r0 + 32, :], w=["loB0"])
    for q in range(N):
        dma("s", T.n4[32 * q:32 * q + 32, :], T.span[r0:r0 + 32, :], w=["n4%d" % q])
        dma("s", T.n4d[32 * q:32 * q + 32, :], T.span[r0:r0 + 32, :], w=["n4d%d" % q])

    step("list")
    count(T.Pi[:, 0:1], [[1, 1]], 1, ["Pi0"], 1)
    count(T.Jt[:, 0:128], [[1, 8], [0, 16]], 0, ["Jt0"], 128)
    count(T.Jt[:, 128:256], [[0, 4], [1, 2], [0, 16]], 0, ["Jt1"], 128)
    count(T.J[:, :], [[1, 128]], 0, ["J"], 128)
    count(T.Jt[:, 256:272], [[0, 2], [1, 8]], 0, ["Jt2"], 16)
    ts(T.Pi[:, 1:2], T.Pi[:, 0:1], 15, ALU.bitwise_and, ["Pi0"], ["Pi1"], 1)
    ts(T.Pi[:, 2:3], T.Pi[:, 0:1], 4, ALU.arith_shift_right, ["Pi0"], ["Pi2"], 1)
    ts(T.Pi[:, 3:4], T.Pi[:, 0:1], 4, ALU.arith_shift_right, ["Pi0"], ["Pi3"], 1, 1, ALU.bitwise_and)
    cp(T.Pf[:, 0:4], T.Pi[:, 0:4], ["Pi0", "Pi1", "Pi2", "Pi3"], ["Pf"], 4)
    ts(T.BD[:, 0:256], T.Jt[:, 0:256], T.Pf[:, 2:3], ALU.is_equal, ["Jt0", "Jt1", "Pf"], ["BD"], 256)
    ts(T.M16[:, :], T.J[:, 0:16], T.Pf[:, 1:2], ALU.is_equal, ["J", "Pf"], ["M16"], 16)
    fill(T.BD[32:64, 128:256], 1.0, ["BD"], 64)

    ts(T.V[:, 128:256], T.V[:, 0:128], 1, ALU.arith_shift_right, ["V0"], ["V1"], 128)
    ts(T.tmpi[:, 0:128], T.V[:, 0:128], 1, ALU.bitwise_and, ["V0"], ["tm0"], 128)
    ts(T.tmpi[:, 128:256], T.V[:, 0:128], 2, ALU.arith_shift_right, ["V0"], ["tm1"], 128)
    tt(T.tmpi[:, 256:384], T.tmpi[:, 0:128], T.V[:, 128:256], ALU.mult, ["tm0", "V1"], ["tm2"], 256)
    tt(T.tmpi[:, 128:256], T.V[:, 128:256], T.tmpi[:, 128:256], ALU.subtract, ["V1", "tm1"], ["tm1"], 256)
    cp(T.offA[:, 0:128], T.loA[:, :], ["loA"], ["offA0"], 128)
    tt(T.V[:, 256:384], T.tmpi[:, 128:256], T.tmpi[:, 256:384], ALU.add, ["tm1", "tm2"], ["V2"], 256)
    for i in range(3):
        tt(T.XI[:, 128 * i:128 * i + 128], T.loA[:, :], T.V[:, 128 * i:128 * i + 128], ALU.add, ["loA", "V%d" % i], ["XI%d" % i], 256)
        if i == 0:
            ts(T.V16[:, 0:384], T.V[:, :], -MID, ALU.add, ["V0", "V1", "V2"], ["V160", "V161", "V162"], 384)
    cp(T.offA[:, 128:512], T.XI[:, :], ["XI0", "XI1", "XI2"], ["offA1", "offA2", "offA3"], 384)

    step("sel")
    for r in range(16):
        if SEL_ON[r] == "v":
            ts(T.Sel[:, 256 * r:256 * r + 256], T.BD[:, :], T.M16[:, r:r + 1], ALU.mult, ["BD", "M16"], ["Sel%d" % r], 128)
        else:
            act(T.Sel[:, 256 * r:256 * r + 256], T.BD[:, :], ACT.Identity, ["BD", "M16"], ["Sel%d" % r], 256, scale=T.M16[:, r:r + 1])
    step("eye")
    ts(T.If[:, :], T.J[:, :], T.Pf[:, 0:1], ALU.is_equal, ["J", "Pf"], ["If"], 128)
    for name, x in (("Ibf", 1.0), ("Ineg", -1.0)):
        act(T[name][:, :], T.If[:, :], ACT.Identity, ["If"], [name], 128, scale=x)
    for name, x in (("K0", 2 * KY), ("K1", -KY - 1), ("K2", 1 - KY)):
        ts(T[name][:, :], T.Ibf[:, :], x, ALU.mult, ["Ibf"], [name], 64)
    ts(T.onesA[:, :], T.Jt[:, 256:272], T.Pf[:, 2:3], ALU.is_equal, ["Jt2", "Pf"], ["onesA"], 16)

    def more_constants():
        step("more")
        ts(T.onesB[:, :], T.J[:, 0:8], T.Pf[:, 3:4], ALU.is_equal, ["J", "Pf"], ["onesB"], 8)
        fill(T.w16[32:64, :], MID, ["wc"], 64)
        fill(T.Z[:, :], 0.0, ["Z0", "Z1"], 100)
        fill(T.CH[:, 1, 0:96:3], 0.0, ["CHz"], 32)
        fill(T.FC[:, 1, 0:64:2], 0.0, ["FCz"], 32)
        for k in range(2):
            fill(T.fl[:, 256 * k + 2 * r0 + 3:256 * k + 2 * r0 + 64:4], 0.0, ["flz%d" % k], 16)
        fill(T.RW[:, 3:128:4], WHOLE, ["RWc"], 32)
        fill(T.px[:, 259:512:4], WHOLE, ["px:M"], 64)
        for name, x in (("Ihalf", 0.5), ("Inh", -0.5)):
            act(T[name][:, :], T.If[:, :], ACT.Identity, ["If"], [name], 128, scale=x)
        for i, x in ((0, 0.0), (2, UNDER), (3, 1.0)):
            fill(T.D0[:, i:256:4], x, ["D0c%d" % i], 64)
        fill(T.Q0[:, 0, :], -MID, ["Q0l"], 32)
        cp(T.V16[:, 384:512], T.tmpi[:, 0:128], ["tm0"], ["V163"], 128)

    step(None)
    fused([(peer(d), small[d - 1], "lo_in", T.lost[:, 32 * (d - 1):32 * d], T.lold[:, 32 * (d - 1):32 * d])
           for d in range(1, N)], ["lost1", "lost2", "lost3"], ["@lo"], CROSS_LO)
    for d in range(1, N):
        s = 2 * (d - 1)
        a0, a1 = slice(s * PIECE, (s + 1) * PIECE), slice((s + 1) * PIECE, (s + 2) * PIECE)
        fused([(peer(d), far, "in%d" % s, T.stage[:, a0], T.land[:, a0]),
               (hs[d - 1], near, "on", T.stage[:, a1], T.stage[:, a1])], ["stage%d" % s, "stage%d" % (s + 1)],
              ["@in%d" % s, "@in%d" % (s + 1)], CROSS_BIG)
    for d in range(1, N):
        q0 = 32 * ((rank - d) % N)
        dma("s", T.LB[q0:q0 + 32, 0:128], T.lold[:, 32 * (d - 1):32 * d], ["@lo"], ["loB%d" % d], [("lo_in", three)])
    dma("s", T.tabB[r0:r0 + 32, :], T.walk[r0:r0 + 32, :], ["@lo"], ["tabB6"])
    for s in RELAYOUT:
        q0, a = 32 * ((rank - 1 - s // 2) % N), s % 2
        dma("s", T.tabB[q0:q0 + 32, a * HALF:(a + 1) * HALF], T.land[:, s * PIECE:(s + 1) * PIECE],
            ["@in%d" % s], ["tabB%d" % s], [("in%d" % s, len(far))])
    for i in range(16):
        dma("s", T.nB[i:128:16, :, :], T.n4d[:, :], ["n4d%d" % q for q in range(N)], [NB[i]], done=2 * LOAD)

    def spread(s, lhs, rhs, rr, b):
        for r in range(8 * s, 8 * s + 8):
            mm(T[b][:, 64 * (r - 8 * s):64 * (r - 8 * s) + 64], lhs(r), rhs, True, True, rr + ["Sel%d" % r], [b])

    def selA(r):
        return T.Sel[:, 256 * r:256 * r + 128]

    def selB(r):
        return T.Sel[0:48, 256 * r + 128:256 * r + 256]

    def spreadA(k, s):
        step("n%d%d" % (k, s))
        for j, (name, i) in enumerate((("nA", 0), ("wA", 2))):
            b, c0, key = next_bank(), 1024 * k + 512 * s, name + "%d%d" % (k, s)
            spread(s, selA, T.V16[:, 128 * i + 64 * k:128 * i + 64 * k + 64], ["V16%d" % i], b)
            if EVAC_A[2 * (2 * k + s) + j] == "a":
                act(T[name][:, c0:c0 + 512], T[b][:, :], ACT.Identity, [b], [key], 512, bias=MID)
            else:
                ts(T[name][:, c0:c0 + 512], T[b][:, :], MID, ALU.add, [b], [key], 512)

    def combine(b, s, terms):
        for r in range(8 * s, 8 * s + 8):
            o = T[b][:, 64 * (r - 8 * s):64 * (r - 8 * s) + 64]
            for i, (weight, x, c0, rx) in enumerate(terms):
                mm(o, T[weight][:, :], x[:, c0 + r:c0 + 1024:16], i == 0, i == len(terms) - 1, rx + [weight], [b])

    def size(slot, b, a, names):
        D = T.Db[:, 512 * slot:512 * slot + 512]
        step(names[0])
        tt(D, T[b][:, :], T.Ab[:, 512 * a:512 * a + 512], ALU.subtract, ["A%d" % a, b], ["D%d" % slot], 512)
        step(names[1])
        act(D, D, ACT.Abs, ["D%d" % slot], ["D%d" % slot], 512)

    def sums(slot, s, out, ones, rones, part):
        for u in range(4 * s, 4 * s + 4):
            c0 = 512 * slot + 128 * (u - 4 * s)
            mm(out(u), T.Db[:, c0:c0 + 128], ones, True, True, ["D%d" % slot, rones], [part], 256)

    W_, LOW = T.Z[:, 4:192:6], T.Z[:, 2:192:6]
    ROW = {"l": 0, "p": 2, "q": 4}

    def linear(out, terms, part):
        Q, qn = T["Q%d" % cur[0]], "Q%d" % cur[0]
        for i, (weight, rows) in enumerate(terms):
            a, n = ROW[rows[0]], len(rows)
            mm(out, T[weight][:, :], Q[:, a:a + 2 * n - 1:2, :], i == 0, i == len(terms) - 1,
               [weight] + [qn + c for c in rows], [part], 32 * n)

    def after_probe():
        Q, qn = T["Q%d" % cur[0]], "Q%d" % cur[0]
        m = Q[:, 3, :]
        step("pq")
        tt(Q[:, 2, :], m, W_, ALU.min, [qn + "m", "Z0", "Z1"], [qn + "p"], 64)
        tt(Q[:, 4, :], m, W_, ALU.max, [qn + "m", "Z0", "Z1"], [qn + "q"], 64)
        step("gaps")
        mm(T.px[:, 64:96], T.Ibf[:, :], W_, True, False, ["Ibf", "Z0", "Z1"], ["px:s"])
        mm(T.px[:, 64:96], T.Ineg[:, :], m, False, True, ["Ineg", qn + "m"], ["px:s"])
        linear(T.px[:, 257:512:4], [("Ihalf", "lp"), ("Ihalf", "qr"), ("Ineg", "pq")], "px:d")
        linear(T.px[:, 192:256], [("Ihalf", "qr"), ("Inh", "lp")], "px:h")
        linear(T.px[:, 258:512:4], [("Ibf", "pq")], "px:d")
        linear(T.px[:, 96:192], [("Ibf", "lpq"), ("Ineg", "pqr")], "px:g")
        act(T.px[:, 256:512:4], T.px[:, 257:512:4], ACT.Sign, ["px:d"], ["px:c"], 64, bias=-0.25)
        act(T.D0[:, 1:256:4], T.px[:, 192:256], ACT.Identity, ["px:h"], ["span"], 64)
        step("side")
        act(T.CH[:, 1, 1:96:3], T.px[:, 64:96], ACT.Sign, ["px:s"], ["sgn"], 32, bias=-0.5)
        step("left")
        act(T.CH[:, 0, 1:96:3], T.CH[:, 1, 1:96:3], ACT.Identity, ["sgn"], ["left"], 32, scale=-0.5, bias=0.5)
        step("next")
        scan(T.RW[:, 128:384], T.D0[:, :], T.px[:, 256:512], ["px:d", "px:c", "px:M", "span", "D0c0", "D0c2", "D0c3"], ["RW"], 256)
        step("both")
        tt(T.CH[:, :, 2:96:3], T.RW[:, 131:384:4], T.RW[:, 3:256:4], ALU.subtract, ["RW", "RWc"], ["W2"], 128)

    def new_bracket(last):
        Q, qn = T["Q%d" % cur[0]], "Q%d" % cur[0]
        cur[0] ^= 1
        P, pn = T["Q%d" % cur[0]], "Q%d" % cur[0]
        step("low")
        for i in ((1,) if last else (0, 1, 2)):
            a = T.px[:, 96 + 32 * i:128 + 32 * i]
            tt(a, a, LOW, ALU.mult, ["Z0", "Z1", "px:g"], ["px:t%d" % i], 32)
        step("lmr")
        if last:
            tt(T.tm[:, :], Q[:, 2, :], T.px[:, 128:160], ALU.subtract, ["px:t1", qn + "p"], ["tm"], 32)
            step("pq")
            tt(T.FC[:, 1, 1:64:2], W_, T.tm[:, :], ALU.subtract, ["tm", "Z0", "Z1"], ["step"], 64)
            step("side")
            act(T.FC[:, 0, 1:64:2], T.tm[:, :], ACT.Identity, ["tm"], ["mU"], 32, bias=MID)
            return
        tt(P[:, 0:7:3, :], Q[:, 0:5:2, :], T.px[:, 96:192], ALU.subtract,
           ["px:t0", "px:t1", "px:t2", qn + "l", qn + "p", qn + "q"], [pn + "l", pn + "m", pn + "r"], 96)
        after_probe()

    def choose(k, gw_, rg, c, *both):
        a, c0, z = slice(48 * k, 48 * k + 48), 64 * k, 96 * k
        step("up%d" % k)
        tt(T.CH[:, 0, 48 * k:48 * k + 48:3], gw_, T.gm[:, now[0], 16 * k:16 * k + 16], ALU.is_gt, rg + ["gm%d%d" % (now[0], k)], ["up%d" % k], c)
        if k == 1:
            best(*both)
        step("w%d" % k)
        scan(T.Z[:, z:z + 96:2], T.CH[:, 1, a], T.CH[:, 0, a], ["up%d" % k, "left", "sgn", "W2", "CHz"], ["Z%d" % k], 48)
        step("lo%d" % k)
        mm(T.pg[:, 320:384], T.If[:, :], T.lo2[:, c0:c0 + 64], True, False, ["If", "lo2"], ["pg:w"], 256)
        step("w%d" % k)
        for q in range(N):
            o = T.pg[32 * q:32 * q + 32, 320:384]
            mm(o, T.Z[:, z + 4:z + 100:3], T.Ibf[:, 0:64], False, False, ["Z%d" % k, "Ibf"], ["pg:w"])
            mm(o, T.Z[:, z + 1:z + 97:3], T.Ibf[:, 64:128], False, True, ["Z%d" % k, "Ibf"], ["pg:w"])
        step("off%d" % k)
        cp(T.offw[:, c0:c0 + 64], T.pg[:, 320:384], ["pg:w"], ["offw%d" % k], 64)
        step("row%d" % k)
        tt(T.w16[0:32, c0:c0 + 64], T.pg[0:32, 320:384], T.lo2[0:32, c0:c0 + 64], ALU.subtract, ["pg:w", "lo2"], ["w16%d" % k], 64)
        for part in range(2):
            c1 = c0 + 32 * part
            step("pick%d" % (2 * k + part))
            cp(T.gw[:, 16 * c1:16 * c1 + 512], T.tabB[:, 0:W].indirect(T.offw[:, c1:c1 + 32]),
               TABB + ["offw%d" % k], ["gw%d%d" % (k, part)], 512 * PICK, "a")
        for s in range(2):
            step("rep%d" % (2 * k + s))
            spread(s, selB, T.w16[0:48, c0:c0 + 64], ["w16%d" % k, "wc"], "pw%d" % (2 * k + s))

    def best(gw_, rg, c):
        old, new = now[0], 1 - now[0]
        step("best")
        tt(T.gm[:, new, :], gw_, T.gm[:, old, :], ALU.max, rg + ["gm%d0" % old, "gm%d1" % old], ["gm%d0" % new, "gm%d1" % new], c)
        now[0] = new

    def gain(k):
        for s in range(2):
            b, pd, slot, c0 = "pw%d" % (2 * k + s), "pd%d" % s, 2 * k + s, 1024 * k + 512 * s
            step("B%d" % slot)
            tt(T[b][:, :], T[b][:, :], T.riseB[:, c0:c0 + 512], ALU.mult, [b, "rB%d%d" % (k, s)], [b], 512)
            step("x%d" % slot)
            combine(pd, s, [("Ibf", T.gw, 1024 * k, ["gw%d0" % k, "gw%d1" % k]), ("Ineg", T.g0B, 1024 * k, ["g0B%d" % k])])
            step("A%d" % slot)
            tt(T.Ab[:, 512 * slot:512 * slot + 512], T[pd][:, :], T.nB[:, 8 * s:8 * s + 8, 64 * k:64 * k + 64], ALU.mult,
               [pd] + NB, ["A%d" % slot], 512)
            size(slot, b, slot, ("D%d" % slot, "abs%d" % slot))
            step("sum%d" % slot)
            sums(slot, s, lambda u: T.pg[:, 256 + 16 * k + u:272 + 16 * k:8], T.onesB[:, 0:2], "onesB", "pg:%d" % k)

    def start_state():
        step("state")
        for j, i in enumerate((1, 0, 2, 3)):
            for k in range(2):
                for rr in range(2):
                    c0 = 128 + 32 * j + 16 * k
                    mm(T.px[64 * rr:64 * rr + 64, c0:c0 + 16], T.V16[:, 128 * i + 64 * k:128 * i + 64 * k + 64],
                       T.Ibf[:, r0 + rr:r0 + 32:2], True, True, ["V16%d" % i, "Ibf"], ["px"])
        act(T.CO[:, :, 0:8], T.px[:, 224:256], ACT.Identity, ["px"], ["co"], 32, scale=0.5)
        act(T.tm[:, :], T.px[:, 224:256], ACT.Identity, ["px"], ["tm"], 32, scale=(1 - KY) / 2, bias=MID)
        cp(T.Q0[:, 3:7:3, :], T.px[:, 128:192], ["px"], ["Q0m", "Q0r"], 64)
        cp(W_, T.px[:, 192:224], ["px"], ["Z0", "Z1"], 32)
        tt(T.CO[:, :, 8:16], T.px[:, 128:160], T.tm[:, :], ALU.add, ["px", "tm"], ["cm"], 32)
        after_probe()

    def pickA(k, i):
        step("g%d%d" % (k, i))
        cp(T.gA[:, 2048 * i + 1024 * k:2048 * i + 1024 * k + 1024],
           T.tabA[:, 0:W].indirect(T.offA[:, 128 * i + 64 * k:128 * i + 64 * k + 64]),
           ["tabA", "offA%d" % i], ["gA%d%d" % (i, k)], 1024 * PICK, PICK_A[4 * k + i])

    def evalA(k, s):
        def term(weight, i):
            return weight, T.gA, 2048 * i + 1024 * k, ["gA%d%d" % (i, k)]
        bz, br, bx, c0 = next_bank(), next_bank(), next_bank(), 1024 * k + 512 * s
        ones, a = T.onesA[:, (2 * rank + 2) % 8:(2 * rank + 2) % 8 + 8], 2 * k + s
        step("r%d%d" % (k, s))
        combine(br, s, [term("Ibf", 1), term("Ineg", 0)])
        tt(T.Ab[:, 512 * a:512 * a + 512], T[br][:, :], T.wA[:, c0:c0 + 512], ALU.mult, [br, "wA%d%d" % (k, s)], ["A%d" % a], 512)
        step("z%d%d" % (k, s))
        combine(bz, s, [term("K0", 2), term("K1", 0), term("K2", 1)])
        act(T.Db[:, 1024 * s + 512:1024 * s + 1024], T[bz][:, :], ACT.Abs, [bz], ["D%d" % (2 * s + 1)], 512)
        sums(2 * s + 1, s, lambda u: T.pg[:, 128 * k + 64 + u:128 * k + 128:8], ones, "onesA", "pg:t")
        step("x%d%d" % (k, s))
        combine(bx, s, [term("Ibf", 3), term("Ineg", 0)])
        tt(T[bx][:, :], T[bx][:, :], T.nA[:, c0:c0 + 512], ALU.mult, [bx, "nA%d%d" % (k, s)], [bx], 512)
        size(2 * s, bx, a, ["x%d%d" % (k, s)] * 2)
        sums(2 * s, s, lambda u: T.pg[:, 128 * k + u:128 * k + 64:8], ones, "onesA", "pg:g")

    def send_parts(k):
        step("send%d" % k)
        ts(T.X[:, k, 0:8, 16:24], T.pg[:, 128 * k + 64:128 * k + 128], 1 / KY, ALU.mult, ["pg:t"], ["Xy%d" % k], 64)
        cp(T.X[:, k, 0:8, 8:16], T.pg[:, 128 * k + 64:128 * k + 128], ["pg:t"], ["Xt%d" % k], 64)
        cp(T.X[:, k, 0:8, 0:8], T.pg[:, 128 * k:128 * k + 64], ["pg:g"], ["Xg%d" % k], 64)
        fused([(peer(d), small[d - 1], "part%d" % k, T.X[:, k, 2 * d - 2:2 * d, :], T.X[:, k, 6 + 2 * d:8 + 2 * d, :])
               for d in range(1, N)], ["Xy%d" % k, "Xt%d" % k, "Xg%d" % k], ["@part%d" % k], CROSS)

    def add_parts(k):
        step("add%d" % k)
        a = slice(2 * k, 2 * k + 2)
        tt(T.S2[:, 4 * k:4 * k + 4, :], T.X[:, k, 6:10, :], T.X[:, k, 10:14, :], ALU.add,
           ["Xy%d" % k, "Xt%d" % k, "Xg%d" % k, "@part%d" % k], ["S2%d" % k], 192, after=[("part%d" % k, three)])
        tt(T.S1[:, a, :], T.S2[:, 4 * k:4 * k + 2, :], T.S2[:, 4 * k + 2:4 * k + 4, :], ALU.add, ["S2%d" % k], ["S1%d" % k], 96)
        tt(T.PR[:, a, :], T.S1[:, a, 8:24], T.CO[:, a, :], ALU.mult, ["S1%d" % k, "co", "cm"], ["PR%d" % k], 64)
        tt(T.gm[:, 0, 16 * k:16 * k + 16], T.PR[:, a, 0:8], T.PR[:, a, 8:16], ALU.add, ["PR%d" % k], ["gm0%d" % k], 32)

    def lo_setup():
        step("lo")
        tt(T.LB[:, 128:256], T.LB[:, 0:128], T.n4[:, :], ALU.add, LOB + N4, ["loE"], 256)
        ts(T.lo2[:, :], T.LB[:, 0:128], MID, ALU.add, LOB, ["lo2"], 128)
        cp(T.offB[:, :], T.LB[:, :], LOB + ["loE"], ["offB"], 256)

    def endsB(k):
        for i, name in enumerate(("g0B", "geB")):
            step("e%d%d" % (k, i))
            cp(T[name][:, 1024 * k:1024 * k + 1024], T.tabB[:, 0:W].indirect(T.offB[:, 128 * i + 64 * k:128 * i + 64 * k + 64]),
               TABB + ["offB", "Xg1"], [name + "%d" % k], 1024 * PICK, PICK_B[2 * k + i])
        for s in range(2):
            b, c0 = "pw%d" % (2 * k + s), 1024 * k + 512 * s
            step("rise%d%d" % (k, s))
            combine(b, s, [("Ibf", T.geB, 1024 * k, ["geB%d" % k]), ("Ineg", T.g0B, 1024 * k, ["g0B%d" % k])])
            cp(T.riseB[:, c0:c0 + 512], T[b][:, :], [b], ["rB%d%d" % (k, s)], 512, RISE_B[2 * k + s])

    def finish(k):
        f0, a = 256 * k + 2 * r0, slice(32 * k, 32 * k + 32)
        gw_, gm_, rg = T.pg[:, 256 + 16 * k:272 + 16 * k], T.gm[:, now[0], 16 * k:16 * k + 16], ["pg:%d" % k, "gm%d%d" % (now[0], k)]
        step("up%d" % k)
        tt(T.FC[:, 0, 32 * k:32 * k + 32:2], gw_, gm_, ALU.is_gt, rg, ["up%d" % k], 16)
        tt(T.fl[:, f0 + 1:f0 + 64:4], gw_, gm_, ALU.max, rg, ["fg%d" % k], 16)
        step("w%d" % k)
        scan(T.fl[:, f0:f0 + 64:2], T.FC[:, 1, a], T.FC[:, 0, a], ["up%d" % k, "step", "mU", "FCz"], ["fl%d" % k], 32)
        sent[0] += len(far)
        one = RemoteDMATransfer(dst_ids=[dstid(peer(d)) for d in range(1, N)], dma_engine_mask=bits(far), remote_sem=T.sem["fin%d" % k],
                                srcs=[T.fl[:, f0:f0 + 64]], dsts=[T.fl[:, f0:f0 + 64]] * (N - 1))
        op("g", lambda e: e.remote_dma_fused([one], local_sem=T.sem.sent), ["fl%d" % k, "fg%d" % k, "flz%d" % k], ["@fin%d" % k],
           remote=True, busy=600, done=CROSS)

    def store(k):
        done = []
        for o in range(2):
            b, out = "pw%d" % (2 * k + o), T.fs[0:64, 256 * k + 128 * o:256 * k + 128 * o + 128]
            mm(T[b][0:64, 0:128], T.fl[:, 256 * k + 2 - o:256 * k + 256:4], T.If[:, :], True, True,
               ["fl%d" % k, "fg%d" % k, "If", "@fin%d" % k], [b], 512, after=[("fin%d" % k, len(far) * (N - 1))])
            cp(out, T[b][0:64, 0:128], [b], ["fs%d%d" % (k, o)], 128, "va"[o])
            done.append(dma("sa"[o], (T.ym, T.yg)[o][:, 64 * k:64 * k + 64], out, ["fs%d%d" % (k, o)]))
        return done

    for k in range(2):
        for s in range(2):
            spreadA(k, s)
        for i in range(4):
            pickA(k, i)
        for s in range(2):
            evalA(k, s)
        send_parts(k)
        if k == 0:
            more_constants()
            start_state()
    lo_setup()
    for k in range(2):
        add_parts(k)
    for k in range(2):
        endsB(k)

    at[0] = 1
    for k in range(2):
        choose(k, T.S1[:, 2 * k:2 * k + 2, 0:8], ["S1%d" % k], 32, T.S1[:, :, 0:8], ["S10", "S11"], 64)
    new_bracket(False)
    for t in range(2, ROUNDS):
        at[0] = t
        for k in range(2):
            gain(k)
            choose(k, T.pg[:, 256 + 16 * k:272 + 16 * k], ["pg:%d" % k], 16, T.pg[:, 256:288], ["pg:0", "pg:1"], 32)
        new_bracket(t == ROUNDS - 1)
    at[0] = ROUNDS
    for k in range(2):
        gain(k)
        finish(k)
    at[:] = ROUNDS + 2, None
    stored = store(0) + store(1)
    ops = arrange(ops)
    ops.append({"q": "g", "fn": None, "r": [], "w": [], "dma": None, "remote": False,
                "after": [(k, v, {}, "x") for k, v in stored + [("sent", sent[0])]]})
    emit(g, T, ops)
